import numpy as np
import ml_dtypes


def mxq(x, axis, fmt="e4m3"):
    dtype, down = {"e4m3": (ml_dtypes.float8_e4m3fn, 7), "e5m2": (ml_dtypes.float8_e5m2, 14)}[fmt]
    v = np.moveaxis(np.asarray(x, np.float32).astype(ml_dtypes.bfloat16).astype(np.float64), axis, -1)
    blocks = v.reshape(v.shape[:-1] + (-1, 32))
    amax = np.abs(blocks).max(-1, keepdims=True)
    byte = np.maximum(np.where(amax > 0, np.frexp(amax)[1] - 1 + 127, 0) - down, 1)
    scale = np.exp2(byte - 127.0)
    codes = (blocks / scale).astype(np.float32).astype(dtype).astype(np.float64)
    return np.moveaxis((codes * scale).reshape(v.shape), -1, axis)


WIDE = False


def mx_kscale(k):
    if not WIDE:
        return np.ones(k)
    levels = np.array([24, -24, 12, -12, 0])
    if k % 512:
        return np.exp2(np.random.permutation(np.resize(levels, k // 32))).repeat(32)
    a = np.empty((k // 512, 16))
    for p in range(k // 512):
        a[p, :8] = np.random.permutation(np.resize(levels, 8))
        for g in range(8):
            far = levels[np.abs(levels - a[p, g]) >= 10]
            a[p, g + 8] = far[np.random.randint(len(far))]
    return np.exp2(a.ravel()).repeat(32)


def f64(x):
    return np.asarray(x).astype(np.float64)


def striped(idx):
    return np.tile(idx.reshape(-1, 16).T, (8, 1)).astype(np.uint16)


def unstriped(offs):
    return offs[:16].T.reshape(-1).astype(np.int64)


E2M1 = np.array([0.0, 0.5, 1.0, 1.5, 2.0, 3.0, 4.0, 6.0, -0.0, -0.5, -1.0, -1.5, -2.0, -3.0, -4.0, -6.0])


def pack_weight(w, fmt):
    k, n = w.shape
    w = f64(np.asarray(w, np.float32).astype(ml_dtypes.bfloat16)).reshape(k // 32, 32, n)
    amax = np.abs(w).max(1)
    if fmt == "e4m3":
        byte = np.frexp(amax)[1] - 1 + 127 - 7
    else:
        mant, ex = np.frexp(amax / 6.0)
        byte = np.where(mant > 0.5, ex, ex - 1) + 127
    byte = np.clip(np.where(amax > 0, byte, 1), 1, 254)
    scaled = (w * np.exp2(127.0 - byte)[:, None, :]).reshape(k, n).astype(np.float32)
    by_word = np.ascontiguousarray(scaled.reshape(k // 512, 128, 4, n).transpose(0, 1, 3, 2))
    if fmt == "e4m3":
        words = by_word.astype(ml_dtypes.float8_e4m3fn).view(np.uint8)
    else:
        c = by_word.astype(ml_dtypes.float4_e2m1fn).view(np.uint8) & 0xF
        words = (c[..., 0::2] | (c[..., 1::2] << 4)).reshape(k // 512, 128, 2 * n)
    return np.ascontiguousarray(words), np.ascontiguousarray(byte.astype(np.uint8).reshape(k // 512, 16, n))


def unpack_weight(words, scales, fmt):
    g, _, n = scales.shape
    words = np.ascontiguousarray(words).reshape(g, 128, n, -1)
    if fmt == "e4m3":
        vals = words.view(ml_dtypes.float8_e4m3fn).astype(np.float64)
    else:
        nib = np.empty((g, 128, n, 4), np.uint8)
        nib[..., 0::2] = words & 0xF
        nib[..., 1::2] = words >> 4
        vals = E2M1[nib]
    vals = vals * np.repeat(np.exp2(scales.astype(np.float64) - 127.0), 8, axis=1)[..., None]
    return vals.transpose(0, 1, 3, 2).reshape(g * 512, n)


def pack_table4(v):
    words, scales = pack_weight(v, "e2m1")
    g, t = words.shape[0] // 2, v.shape[1]
    return np.ascontiguousarray(words.reshape(g, 2, 128, t, 2).transpose(0, 2, 3, 1, 4).reshape(g, 128, t, 4)), scales


def unpack_table4(words, scales):
    g, _, t, _ = words.shape
    return unpack_weight(words.reshape(g, 128, t, 2, 2).transpose(0, 3, 1, 2, 4).reshape(2 * g, 128, 2 * t), scales, "e2m1")


def planes(y):
    n, m = y.shape
    v = y.astype(np.float32).astype(ml_dtypes.bfloat16).astype(np.float64).reshape(n // 32, 32, m)
    top = np.abs(v).max(1)
    byte = np.clip(np.where(top > 0, np.frexp(top)[1] - 1 + 127 - 7, 1), 1, 254)
    codes = (v * np.exp2(127.0 - byte)[:, None, :]).reshape(n, m).astype(np.float32).astype(ml_dtypes.float8_e4m3fn).view(np.uint8)
    words = codes.reshape(n // 512, 128, 4, m).transpose(0, 1, 3, 2)
    return np.ascontiguousarray(words), np.ascontiguousarray(byte.astype(np.uint8).reshape(n // 512, 16, m))


def sigm(f):
    return 1.0 / (1.0 + np.exp(-np.maximum(f, -700.0)))


K, M, N, T, J = 1024, 1024, 1024, 2048, 1024


def setup_inputs():
    n = np.random.standard_normal
    s = mx_kscale(K)[:, None]
    s2 = mx_kscale(M)[:, None]
    h = np.tanh(n((N, T)))
    p_tab = pack_table4(h * s2)
    p_wz = pack_weight(n((K, N)) / np.sqrt(K) / s, "e4m3")
    p_uz = pack_weight(n((M, N)) / np.sqrt(M) / s2, "e4m3")
    p_wn = pack_weight(n((K, N)) / np.sqrt(K) / s, "e4m3")
    p_un = pack_weight(n((M, N)) / np.sqrt(M) / s2, "e4m3")
    return {
        "x": (n((K, J)) * s).astype(np.float32),
        "tab_words": p_tab[0],
        "tab_scales": p_tab[1],
        "wz_words": p_wz[0],
        "wz_scales": p_wz[1],
        "uz_words": p_uz[0],
        "uz_scales": p_uz[1],
        "wn_words": p_wn[0],
        "wn_scales": p_wn[1],
        "un_words": p_un[0],
        "un_scales": p_un[1],
        "bz": (0.3 * n(N)).astype(np.float32),
        "bn": (0.3 * n(N)).astype(np.float32),
        "hT": (h).astype(np.float32),
        "wgo": np.tile(np.random.uniform(0.5, 2.0, J), (128, 1)).astype(np.float32),
        "offs": striped(np.random.permutation(T)[:J]),
    }


def reference(x, tab_words, tab_scales, wz_words, wz_scales, uz_words, uz_scales, wn_words, wn_scales, un_words, un_scales, bz, bn, hT, wgo, offs):
    idx = unstriped(offs)
    x_ = mxq(f64(x), 0, "e4m3")
    tab_ = unpack_table4(tab_words, tab_scales)[:, idx]
    wz_ = unpack_weight(wz_words, wz_scales, "e4m3")
    uz_ = unpack_weight(uz_words, uz_scales, "e4m3")
    wn_ = unpack_weight(wn_words, wn_scales, "e4m3")
    un_ = unpack_weight(un_words, un_scales, "e4m3")
    sz = wz_.T @ x_ + uz_.T @ tab_
    z = sigm(sz + f64(bz)[:, None])
    xn = wn_.T @ x_
    hn = un_.T @ tab_
    cd = np.tanh(xn + f64(bn)[:, None] + z * hn)
    out = np.zeros((N, T))
    out[:, idx] = f64(wgo)[0] * (f64(hT)[:, idx] + z * (cd - f64(hT)[:, idx]))
    return (out,) + planes(out)

@@ -1,0 +1,306 @@
+from contextlib import ExitStack
+
+import concourse.mybir as mybir
+
+K, M, N, T, J = 1024, 1024, 1024, 2048, 1024
+FLOPS = 2 * (2 * K + 2 * M) * N * J
+
+F32 = mybir.dt.float32
+BF16 = mybir.dt.bfloat16
+I32 = mybir.dt.int32
+U32 = mybir.dt.uint32
+U16 = mybir.dt.uint16
+U8 = mybir.dt.uint8
+FP8X4 = mybir.dt.float8_e4m3fn_x4
+FP4X4 = mybir.dt.float4_e2m1fn_x4
+ALU = mybir.AluOpType
+ACT = mybir.ActivationFunctionType
+
+P = 128
+PACK = 4
+KP = P * PACK
+H = 512
+NPAGE = 3
+
+
+def tile_list_tgn_mguP_kernel(
+    tc, x, tab_words, tab_scales, wz_words, wz_scales, uz_words, uz_scales, wn_words, wn_scales,
+    un_words, un_scales, bz, bn, hT, wgo, offs, out_0, out_1, out_2,
+):
+    nc = tc.nc
+    with ExitStack() as ctx:
+        keep = ctx.enter_context(tc.tile_pool(name="keep", bufs=1))
+        ring = ctx.enter_context(tc.tile_pool(name="ring", bufs=2))
+        psum = ctx.enter_context(tc.psum_pool(name="psum", bufs=2))
+
+        offsets = keep.tile([P, J // 16], U16, name="offsets")
+        nc.sync.dma_start(offsets[:], offs)
+
+        def listed(j0, j1):
+            return offsets[:, j0 // 16 : j1 // 16]
+
+        tab_sc = keep.tile([P, 2, T], U8, name="tab_sc", align_bytes=64)
+        xw_sc_raw = keep.tile([P, N], U8, name="xw_sc_raw", align_bytes=64)
+        hw_sc_raw = keep.tile([P, 4, N], U8, name="hw_sc_raw", align_bytes=64)
+        nc.vector.memset(tab_sc[:].rearrange("p a t -> p (a t)").bitcast(I32), 0)
+        nc.vector.memset(hw_sc_raw[:].rearrange("p a t -> p (a t)").bitcast(I32), 0)
+        nc.vector.memset(xw_sc_raw[:].bitcast(I32), 0)
+
+        warm = keep.tile([P, 1], F32, name="warm")
+        bz_sb = keep.tile([P, 2, PACK], F32, name="bz_sb")
+        bn_sb = keep.tile([P, 2, PACK], F32, name="bn_sb")
+
+        def load_x(a, jh):
+            raw = ring.tile([P, PACK, H], F32, name="xraw", tag="big", bufs=5, align_bytes=64)
+            nc.sync.dma_start(raw[:], x[KP * a : KP * (a + 1), H * jh : H * (jh + 1)].rearrange("(p i) c -> p i c", i=PACK))
+            return raw
+
+        x_codes = [keep.tile([P, 2, H], U32, name="x_codes%d" % jh, align_bytes=64) for jh in range(2)]
+        x_sc = [keep.tile([P, 2, H], U8, name="x_sc%d" % jh, align_bytes=64) for jh in range(2)]
+
+        def round_x(raw):
+            xb = ring.tile([P, H, PACK], BF16, name="xb", tag="woven", bufs=5, align_bytes=64)
+            nc.scalar.copy(xb[:].rearrange("p (c i) t -> p c t i", i=4), raw[:].rearrange("p t (c i) -> p c t i", i=4))
+            return xb
+
+        def quant_x(xb, a, jh):
+            nc.vector.quantize_mx(out=x_codes[jh][:, a, :].bitcast(FP8X4), scales=x_sc[jh][:, a, :],
+                                  in_=xb[:].rearrange("p c t -> p (c t)"))
+
+        def load_w(words, g):
+            raw = ring.tile([P, 2, H], I32, name="wraw", tag="wraw", bufs=4, align_bytes=64)
+            nc.sync.dma_start(raw[:], words.rearrange("a p n i -> p a (n i)")[:, :, 4 * H * g : 4 * H * (g + 1)].bitcast(I32))
+            return raw
+
+        def deal_w(raw, name):
+            dealt = keep.tile([P, 2, H], I32, name=name, align_bytes=64)
+            nc.vector.tensor_copy(dealt[:].rearrange("p a (t c i) -> p a c t i", t=4, i=4),
+                                  raw[:].rearrange("p a (c i t) -> p a c t i", t=4, i=4))
+            return dealt
+
+        def deal_scales(g):
+            xw = keep.tile([P, H], U8, name="xw_sc%d" % g, align_bytes=64)
+            hw = keep.tile([P, 4, H], U8, name="hw_sc%d" % g, align_bytes=64)
+            nc.vector.tensor_copy(hw[:].rearrange("p a (t c i) -> p a c t i", t=4, i=16),
+                                  hw_sc_raw[:, :, H * g : H * (g + 1)].rearrange("p a (c i t) -> p a c t i", t=4, i=16))
+            nc.vector.tensor_copy(xw[:].rearrange("p (t c i) -> p c t i", t=4, i=16),
+                                  xw_sc_raw[:, H * g : H * (g + 1)].rearrange("p (c i t) -> p c t i", t=4, i=16))
+            return xw, hw
+
+        def load_h(k):
+            g, t = divmod(k, 4)
+            rows = ring.tile([P, T], F32, name="hrows", tag="big", bufs=5, align_bytes=64)
+            nc.sync.dma_start(rows[:], hT.rearrange("(g p t) c -> g t p c", p=P, t=PACK)[g, t])
+            return rows
+
+        def gather_table(jh):
+            picked = ring.tile([P, H], U32, name="picked", tag="picked", bufs=2, align_bytes=64)
+            codes = keep.tile([P, 2, 2 * H], U8, name="v_codes%d" % jh, align_bytes=64)
+            scales = keep.tile([P, 2, H], U8, name="v_sc%d" % jh, align_bytes=64)
+            lst = listed(H * jh, H * (jh + 1))
+            nc.vector.tensor_copy(picked[:], tabw[:].bitcast(U32).indirect(lst))
+            nc.vector.tensor_copy(scales[:, 0, :], tab_sc[:, 0, :].indirect(lst))
+            nc.vector.tensor_copy(codes[:].bitcast(U16).rearrange("p d (c i) -> p c d i", i=8),
+                                  picked[:].bitcast(U16).rearrange("p (c i d) -> p c d i", i=8, d=2))
+            nc.vector.tensor_copy(scales[:, 1, :], tab_sc[:, 1, :].indirect(lst))
+            return codes, scales
+
+        def load_tab_sc(q):
+            nc.sync.dma_start(
+                tab_sc[32 * q : 32 * q + 4, :, :].bitcast(I32),
+                tab_scales[:, 4 * q : 4 * q + 4, :].rearrange("a r t -> r a t").bitcast(I32),
+            )
+
+        def load_hw_sc(w, q):
+            nc.sync.dma_start(
+                hw_sc_raw[32 * q : 32 * q + 4, 2 * w : 2 * w + 2, :].bitcast(I32),
+                (uz_scales, un_scales)[w][:, 4 * q : 4 * q + 4, :].rearrange("a r t -> r a t").bitcast(I32),
+            )
+
+        def load_xw_sc(w, q):
+            nc.sync.dma_start(
+                xw_sc_raw[32 * q + 8 * w : 32 * q + 8 * w + 8, :].bitcast(I32),
+                (wz_scales, wn_scales)[w][:, 4 * q : 4 * q + 4, :].bitcast(I32),
+            )
+
+        nc.sync.dma_start(bz_sb[:], bz.rearrange("(g p t) -> p g t", p=P, t=PACK))
+        nc.sync.dma_start(bn_sb[:], bn.rearrange("(g p t) -> p g t", p=P, t=PACK))
+        tabw = ring.tile([P, T], I32, name="tabw", tag="big", bufs=5, align_bytes=64)
+        tab_rows = tab_words[0].rearrange("p t b -> p (t b)").bitcast(I32)
+        for c in range(4):
+            nc.sync.dma_start(tabw[:, H * c : H * (c + 1)], tab_rows[:, H * c : H * (c + 1)])
+        x_raw = {}
+        x_raw[0, 0] = load_x(0, 0)
+        for q in range(4):
+            load_tab_sc(q)
+        x_raw[1, 0] = load_x(1, 0)
+        all_words = (("uz", uz_words), ("wz", wz_words), ("un", un_words), ("wn", wn_words))
+        w_raw = {}
+        for n, (nm, words) in enumerate(all_words):
+            for q in range(4):
+                if n < 2:
+                    load_hw_sc(n, q)
+                else:
+                    load_xw_sc(n - 2, q)
+            w_raw[nm, 0] = load_w(words, 0)
+        h_rows = {0: load_h(0)}
+        wgo_sb = keep.tile([P, J], F32, name="wgo_sb")
+        nc.sync.dma_start(wgo_sb[:], wgo)
+
+        nc.vector.memset(warm[:], 0.0)
+        nc.scalar.activation(warm[:], warm[:], ACT.Sigmoid)
+
+        pages = [keep.tile([P, T], F32, name="page%d" % i, align_bytes=64) for i in range(NPAGE)]
+        for page in pages:
+            nc.gpsimd.memset(page[:], 0.0)
+        y_sc = keep.tile([P, T], U8, name="y_sc", align_bytes=64)
+
+        table = {0: gather_table(0)}
+        for a in range(2):
+            quant_x(round_x(x_raw[a, 0]), a, 0)
+        w_sc = {0: deal_scales(0)}
+        w_dealt = {(nm, 0): deal_w(w_raw[nm, 0], nm + "0") for nm, words in all_words}
+
+        h_rows[1] = load_h(1)
+        x_raw[0, 1] = load_x(0, 1)
+        x_raw[1, 1] = load_x(1, 1)
+
+        def products(k, jh):
+            g, t = divmod(k, 4)
+            cols = slice(P * t, P * (t + 1))
+            xw_sc, hw_sc = w_sc[g]
+            v_codes, v_sc = table[jh]
+
+            def with_x(bank, nm, w, first, last):
+                for a in range(2):
+                    nc.tensor.matmul_mx(out=bank[:], lhsT=w_dealt[nm, g][:, a, cols].bitcast(FP8X4),
+                                        lhsT_scale=xw_sc[8 * w + 4 * a : P, cols],
+                                        rhs=x_codes[jh][:, a, :].bitcast(FP8X4), rhs_scale=x_sc[jh][:, a, :],
+                                        start=first and a == 0, stop=last and a == 1)
+
+            def with_v(bank, nm, w, first, last):
+                for a in range(2):
+                    nc.tensor.matmul_mx(out=bank[:], lhsT=w_dealt[nm, g][:, a, cols].bitcast(FP8X4),
+                                        lhsT_scale=hw_sc[:, 2 * w + a, cols],
+                                        rhs=v_codes[:, a, :].bitcast(FP4X4), rhs_scale=v_sc[:, a, :],
+                                        start=first and a == 0, stop=last and a == 1)
+
+            sz = psum.tile([P, H], F32, name="sz", tag="sz", bufs=2)
+            hn = psum.tile([P, H], F32, name="hn", tag="hn", bufs=3)
+            xn = psum.tile([P, H], F32, name="xn", tag="xn", bufs=3)
+            with_v(sz, "uz", 0, True, False)
+            with_x(sz, "wz", 0, False, True)
+            with_v(hn, "un", 1, True, True)
+            with_x(xn, "wn", 1, True, True)
+            return sz, hn, xn
+
+        items = [(0, (0,)), (1, (0,)), (0, (1,)), (1, (1,))] + [(k, (0, 1)) for k in range(2, 8)]
+
+        def gates(item):
+            k, halves = item
+            g, t = divmod(k, 4)
+            z = ring.tile([P, J], F32, name="z", tag="z", bufs=4)
+            banks = []
+            for s, jh in enumerate(halves):
+                sz, hn, xn = products(k, jh)
+                nc.scalar.activation(z[:, H * s : H * (s + 1)], sz[:], ACT.Sigmoid, bias=bz_sb[:, g, t : t + 1])
+                banks.append((hn, xn))
+            return z, banks
+
+        def sums(z, banks):
+            work = ring.tile([P, J], F32, name="work", tag="work", bufs=3)
+            for s, (hn, xn) in enumerate(banks):
+                cols = slice(H * s, H * (s + 1))
+                nc.vector.tensor_tensor(work[:, cols], hn[:], z[:, cols], ALU.mult)
+            for s, (hn, xn) in enumerate(banks):
+                cols = slice(H * s, H * (s + 1))
+                nc.vector.tensor_tensor(work[:, cols], xn[:], work[:, cols], ALU.add)
+            return work
+
+        def candidate(item, work):
+            k, halves = item
+            g, t = divmod(k, 4)
+            w = H * len(halves)
+            cd = ring.tile([P, J], F32, name="cd", tag="cd", bufs=2)
+            nc.scalar.activation(cd[:, 0:w], work[:, 0:w], ACT.Tanh, bias=bn_sb[:, g, t : t + 1])
+            return cd
+
+        woven = {}
+        done = {k: 0 for k in range(8)}
+
+        old = {}
+
+        def gather_h(k):
+            old[k] = ring.tile([P, J], F32, name="old", tag="old", bufs=3)
+            nc.vector.tensor_copy(old[k][:], h_rows[k][:].indirect(listed(0, J)))
+
+        def middle(item, z, cd, d):
+            k, halves = item
+            j0, j1 = H * halves[0], H * (halves[-1] + 1)
+            w = j1 - j0
+            nc.gpsimd.tensor_tensor(d[:, 0:w], cd[:, 0:w], old[k][:, j0:j1], ALU.subtract)
+            nc.gpsimd.tensor_tensor(d[:, 0:w], d[:, 0:w], z[:, 0:w], ALU.mult)
+            nc.gpsimd.tensor_tensor(d[:, 0:w], d[:, 0:w], old[k][:, j0:j1], ALU.add)
+            nc.gpsimd.tensor_tensor(d[:, 0:w], d[:, 0:w], wgo_sb[:, j0:j1], ALU.mult)
+            return d
+
+        def put(item, d):
+            k, halves = item
+            j0, j1 = H * halves[0], H * (halves[-1] + 1)
+            nc.vector.tensor_copy(pages[k % NPAGE][:].indirect(listed(j0, j1)), d[:, 0 : j1 - j0])
+            done[k] = done[k] + len(halves)
+            return k if done[k] == 2 else None
+
+        def finish(k):
+            g, t = divmod(k, 4)
+            page = pages[k % NPAGE]
+            nc.sync.dma_start(out_0.rearrange("(g p t) c -> g t p c", p=P, t=PACK)[g, t], page[:])
+            for c in range(T // H):
+                if t == 0:
+                    woven[c] = ring.tile([P, H, PACK], BF16, name="yb", tag="woven", bufs=5, align_bytes=64)
+                nc.scalar.copy(woven[c][:, :, t], page[:, H * c : H * (c + 1)])
+            if t == PACK - 1:
+                for c in range(T // H):
+                    cols = slice(H * c, H * (c + 1))
+                    codes = ring.tile([P, H], U32, name="y_codes", tag="y_codes", bufs=4, align_bytes=64)
+                    nc.vector.quantize_mx(out=codes[:].bitcast(FP8X4), scales=y_sc[4 * g : P, cols],
+                                          in_=woven[c][:].rearrange("p c t -> p (c t)"))
+                    nc.sync.dma_start(out_1[g].rearrange("p t b -> p (t b)")[:, 4 * H * c : 4 * H * (c + 1)].bitcast(I32),
+                                      codes[:].bitcast(I32))
+                for q in range(4):
+                    nc.sync.dma_start(out_2[g, 4 * q : 4 * q + 4, :].bitcast(I32),
+                                      y_sc[32 * q + 4 * g : 32 * q + 4 * g + 4, :].bitcast(I32))
+
+        ready = {}
+        gated = {0: gates(items[0])}
+        gather_h(0)
+        for i in range(len(items) + 3):
+            if i == 1:
+                table[1] = gather_table(1)
+                for a in range(2):
+                    quant_x(round_x(x_raw[a, 1]), a, 1)
+                h_rows[2] = load_h(2)
+                for nm, words in all_words:
+                    w_raw[nm, 1] = load_w(words, 1)
+            if i == 3:
+                w_sc[1] = deal_scales(1)
+            if 2 <= i <= 5:
+                nm = all_words[i - 2][0]
+                w_dealt[nm, 1] = deal_w(w_raw[nm, 1], nm + "1")
+            if 3 <= i <= 7:
+                h_rows[i] = load_h(i)
+            full = put(items[i - 3], ready[i - 3]) if i >= 3 else None
+            if i < len(items):
+                z, banks = gated[i]
+                work = sums(z, banks)
+                if i + 1 < len(items) and items[i + 1][0] not in old:
+                    gather_h(items[i + 1][0])
+            if full is not None and full % 4 == 3:
+                finish(full)
+            if i < len(items):
+                cd = candidate(items[i], work)
+                if i + 1 < len(items):
+                    gated[i + 1] = gates(items[i + 1])
+                ready[i] = middle(items[i], z, cd, work)
+            if full is not None and full % 4 != 3:
+                finish(full)

@@ -20,7 +20,9 @@ P = 128
 PACK = 4
 KP = P * PACK
 H = 512
-NPAGE = 3
+NPAGE = 2
+DEPTH = 2
+NCD = 3
 
 
 def tile_list_tgn_mguP_kernel(
@@ -36,13 +38,15 @@ def tile_list_tgn_mguP_kernel(
         offsets = keep.tile([P, J // 16], U16, name="offsets")
         nc.sync.dma_start(offsets[:], offs)
 
+        tiles = [(g, t) for g in range(2) for t in (0, 2, 1, 3)]
+
         def listed(j0, j1):
             return offsets[:, j0 // 16 : j1 // 16]
 
         tab_sc = keep.tile([P, 2, T], U8, name="tab_sc", align_bytes=64)
         xw_sc_raw = keep.tile([P, N], U8, name="xw_sc_raw", align_bytes=64)
         hw_sc_raw = keep.tile([P, 4, N], U8, name="hw_sc_raw", align_bytes=64)
-        nc.vector.memset(tab_sc[:].rearrange("p a t -> p (a t)").bitcast(I32), 0)
+        nc.gpsimd.memset(tab_sc[:].rearrange("p a t -> p (a t)").bitcast(I32), 0)
         nc.vector.memset(hw_sc_raw[:].rearrange("p a t -> p (a t)").bitcast(I32), 0)
         nc.vector.memset(xw_sc_raw[:].bitcast(I32), 0)
 
@@ -59,7 +63,7 @@ def tile_list_tgn_mguP_kernel(
         x_sc = [keep.tile([P, 2, H], U8, name="x_sc%d" % jh, align_bytes=64) for jh in range(2)]
 
         def round_x(raw):
-            xb = ring.tile([P, H, PACK], BF16, name="xb", tag="woven", bufs=5, align_bytes=64)
+            xb = ring.tile([P, H, PACK], BF16, name="xb", tag="woven", bufs=8, align_bytes=64)
             nc.scalar.copy(xb[:].rearrange("p (c i) t -> p c t i", i=4), raw[:].rearrange("p t (c i) -> p c t i", i=4))
             return xb
 
@@ -67,42 +71,39 @@ def tile_list_tgn_mguP_kernel(
             nc.vector.quantize_mx(out=x_codes[jh][:, a, :].bitcast(FP8X4), scales=x_sc[jh][:, a, :],
                                   in_=xb[:].rearrange("p c t -> p (c t)"))
 
-        def load_w(words, g):
-            raw = ring.tile([P, 2, H], I32, name="wraw", tag="wraw", bufs=4, align_bytes=64)
-            nc.sync.dma_start(raw[:], words.rearrange("a p n i -> p a (n i)")[:, :, 4 * H * g : 4 * H * (g + 1)].bitcast(I32))
-            return raw
+        def load_w(raw, words, g):
+            nc.sync.dma_start(raw, words.rearrange("a p n i -> p a (n i)")[:, :, 4 * H * g : 4 * H * (g + 1)].bitcast(I32))
 
-        def deal_w(raw, name):
-            dealt = keep.tile([P, 2, H], I32, name=name, align_bytes=64)
-            nc.vector.tensor_copy(dealt[:].rearrange("p a (t c i) -> p a c t i", t=4, i=4),
+        def deal_w(eng, raw, name):
+            dealt = keep.tile(list(raw.shape), I32, name=name, align_bytes=64)
+            eng.tensor_copy(dealt[:].rearrange("p a (t c i) -> p a c t i", t=4, i=4),
                                   raw[:].rearrange("p a (c i t) -> p a c t i", t=4, i=4))
             return dealt
 
-        def deal_scales(g):
+        def deal_scales(eng, g):
             xw = keep.tile([P, H], U8, name="xw_sc%d" % g, align_bytes=64)
             hw = keep.tile([P, 4, H], U8, name="hw_sc%d" % g, align_bytes=64)
-            nc.vector.tensor_copy(hw[:].rearrange("p a (t c i) -> p a c t i", t=4, i=16),
+            eng.tensor_copy(hw[:].rearrange("p a (t c i) -> p a c t i", t=4, i=16),
                                   hw_sc_raw[:, :, H * g : H * (g + 1)].rearrange("p a (c i t) -> p a c t i", t=4, i=16))
-            nc.vector.tensor_copy(xw[:].rearrange("p (t c i) -> p c t i", t=4, i=16),
+            eng.tensor_copy(xw[:].rearrange("p (t c i) -> p c t i", t=4, i=16),
                                   xw_sc_raw[:, H * g : H * (g + 1)].rearrange("p (c i t) -> p c t i", t=4, i=16))
             return xw, hw
 
         def load_h(k):
-            g, t = divmod(k, 4)
+            g, t = tiles[k]
             rows = ring.tile([P, T], F32, name="hrows", tag="big", bufs=5, align_bytes=64)
             nc.sync.dma_start(rows[:], hT.rearrange("(g p t) c -> g t p c", p=P, t=PACK)[g, t])
             return rows
 
-        def gather_table(jh):
-            picked = ring.tile([P, H], U32, name="picked", tag="picked", bufs=2, align_bytes=64)
-            codes = keep.tile([P, 2, 2 * H], U8, name="v_codes%d" % jh, align_bytes=64)
-            scales = keep.tile([P, 2, H], U8, name="v_sc%d" % jh, align_bytes=64)
-            lst = listed(H * jh, H * (jh + 1))
-            nc.vector.tensor_copy(picked[:], tabw[:].bitcast(U32).indirect(lst))
-            nc.vector.tensor_copy(scales[:, 0, :], tab_sc[:, 0, :].indirect(lst))
+        def gather_table():
+            picked = ring.tile([P, J], U32, name="picked", tag="work", bufs=DEPTH, align_bytes=64)
+            codes = keep.tile([P, 2, 2 * J], U8, name="v_codes", align_bytes=64)
+            scales = keep.tile([P, 2, J], U8, name="v_sc", align_bytes=64)
+            nc.vector.tensor_copy(picked[:], tabw[:].bitcast(U32).indirect(offsets[:]))
+            nc.vector.tensor_copy(scales[:, 0, :], tab_sc[:, 0, :].indirect(offsets[:]))
             nc.vector.tensor_copy(codes[:].bitcast(U16).rearrange("p d (c i) -> p c d i", i=8),
                                   picked[:].bitcast(U16).rearrange("p (c i d) -> p c d i", i=8, d=2))
-            nc.vector.tensor_copy(scales[:, 1, :], tab_sc[:, 1, :].indirect(lst))
+            nc.vector.tensor_copy(scales[:, 1, :], tab_sc[:, 1, :].indirect(offsets[:]))
             return codes, scales
 
         def load_tab_sc(q):
@@ -134,42 +135,50 @@ def tile_list_tgn_mguP_kernel(
         for q in range(4):
             load_tab_sc(q)
         x_raw[1, 0] = load_x(1, 0)
+        for q in range(4):
+            load_hw_sc(0, q)
+        x_raw[0, 1] = load_x(0, 1)
+        for q in range(4):
+            load_hw_sc(1, q)
+        x_raw[1, 1] = load_x(1, 1)
         all_words = (("uz", uz_words), ("wz", wz_words), ("un", un_words), ("wn", wn_words))
         w_raw = {}
         for n, (nm, words) in enumerate(all_words):
-            for q in range(4):
-                if n < 2:
-                    load_hw_sc(n, q)
-                else:
-                    load_xw_sc(n - 2, q)
-            w_raw[nm, 0] = load_w(words, 0)
+            if n < 2:
+                for q in range(4):
+                    load_xw_sc(n, q)
+            w_raw[nm] = ring.tile([P, 2, H], I32, name="wraw", tag="z", bufs=4, align_bytes=64)
+            load_w(w_raw[nm][:], words, 0)
+        late_raw = keep.tile([P, 8, H], I32, name="late_raw", align_bytes=64)
+        for n, (nm, words) in enumerate(all_words):
+            load_w(late_raw[:, 2 * n : 2 * n + 2, :], words, 1)
         h_rows = {0: load_h(0)}
-        wgo_sb = keep.tile([P, J], F32, name="wgo_sb")
+        wgo_sb = keep.tile([P, J], F32, name="wgo_sb", tag="wgo", align_bytes=64)
         nc.sync.dma_start(wgo_sb[:], wgo)
+        for k in range(1, 8):
+            h_rows[k] = load_h(k)
 
         nc.vector.memset(warm[:], 0.0)
         nc.scalar.activation(warm[:], warm[:], ACT.Sigmoid)
 
         pages = [keep.tile([P, T], F32, name="page%d" % i, align_bytes=64) for i in range(NPAGE)]
         for page in pages:
-            nc.gpsimd.memset(page[:], 0.0)
-        y_sc = keep.tile([P, T], U8, name="y_sc", align_bytes=64)
+            nc.vector.memset(page[:], 0.0)
 
-        table = {0: gather_table(0)}
-        for a in range(2):
-            quant_x(round_x(x_raw[a, 0]), a, 0)
-        w_sc = {0: deal_scales(0)}
-        w_dealt = {(nm, 0): deal_w(w_raw[nm, 0], nm + "0") for nm, words in all_words}
-
-        h_rows[1] = load_h(1)
-        x_raw[0, 1] = load_x(0, 1)
-        x_raw[1, 1] = load_x(1, 1)
+        bz_neg = keep.tile([P, 2, PACK], F32, name="bz_neg")
+        nc.scalar.activation(bz_neg[:], bz_sb[:], ACT.Copy, scale=-1.0)
+        v_codes, v_sc = gather_table()
+        for jh in range(2):
+            for a in range(2):
+                quant_x(round_x(x_raw[a, jh]), a, jh)
+        w_sc = {0: deal_scales(nc.vector, 0)}
+        w_dealt = {(nm, 0): deal_w(nc.vector, w_raw[nm], nm + "0") for nm, words in all_words}
+        w_sc[1] = deal_scales(nc.vector, 1)
 
         def products(k, jh):
-            g, t = divmod(k, 4)
+            g, t = tiles[k]
             cols = slice(P * t, P * (t + 1))
             xw_sc, hw_sc = w_sc[g]
-            v_codes, v_sc = table[jh]
 
             def with_x(bank, nm, w, first, last):
                 for a in range(2):
@@ -182,7 +191,8 @@ def tile_list_tgn_mguP_kernel(
                 for a in range(2):
                     nc.tensor.matmul_mx(out=bank[:], lhsT=w_dealt[nm, g][:, a, cols].bitcast(FP8X4),
                                         lhsT_scale=hw_sc[:, 2 * w + a, cols],
-                                        rhs=v_codes[:, a, :].bitcast(FP4X4), rhs_scale=v_sc[:, a, :],
+                                        rhs=v_codes[:, a, 2 * H * jh : 2 * H * (jh + 1)].bitcast(FP4X4),
+                                        rhs_scale=v_sc[:, a, H * jh : H * (jh + 1)],
                                         start=first and a == 0, stop=last and a == 1)
 
             sz = psum.tile([P, H], F32, name="sz", tag="sz", bufs=2)
@@ -194,113 +204,105 @@ def tile_list_tgn_mguP_kernel(
             with_x(xn, "wn", 1, True, True)
             return sz, hn, xn
 
-        items = [(0, (0,)), (1, (0,)), (0, (1,)), (1, (1,))] + [(k, (0, 1)) for k in range(2, 8)]
+        items = [(k, (0, 1)) for k in range(8)]
 
         def gates(item):
             k, halves = item
-            g, t = divmod(k, 4)
-            z = ring.tile([P, J], F32, name="z", tag="z", bufs=4)
+            g, t = tiles[k]
+            z = ring.tile([P, J], F32, name="z", tag="z", bufs=4, align_bytes=64)
             banks = []
             for s, jh in enumerate(halves):
                 sz, hn, xn = products(k, jh)
-                nc.scalar.activation(z[:, H * s : H * (s + 1)], sz[:], ACT.Sigmoid, bias=bz_sb[:, g, t : t + 1])
+                nc.scalar.activation(z[:, H * s : H * (s + 1)], sz[:], ACT.Sigmoid, bias=bz_neg[:, g, t : t + 1], scale=-1.0)
                 banks.append((hn, xn))
             return z, banks
 
-        def sums(z, banks):
-            work = ring.tile([P, J], F32, name="work", tag="work", bufs=3)
-            for s, (hn, xn) in enumerate(banks):
-                cols = slice(H * s, H * (s + 1))
-                nc.vector.tensor_tensor(work[:, cols], hn[:], z[:, cols], ALU.mult)
-            for s, (hn, xn) in enumerate(banks):
-                cols = slice(H * s, H * (s + 1))
-                nc.vector.tensor_tensor(work[:, cols], xn[:], work[:, cols], ALU.add)
-            return work
-
-        def candidate(item, work):
+        def candidate(item, keepw, banks):
             k, halves = item
-            g, t = divmod(k, 4)
+            g, t = tiles[k]
             w = H * len(halves)
-            cd = ring.tile([P, J], F32, name="cd", tag="cd", bufs=2)
-            nc.scalar.activation(cd[:, 0:w], work[:, 0:w], ACT.Tanh, bias=bn_sb[:, g, t : t + 1])
+            part = ring.tile([P, J], F32, name="part", tag="work", bufs=DEPTH, align_bytes=64)
+            cd = ring.tile([P, J], F32, name="cd", tag="cd", bufs=NCD)
+            for s, (hn, xn) in enumerate(banks):
+                cols = slice(H * s, H * (s + 1))
+                nc.vector.scalar_tensor_tensor(part[:, cols], keepw[:, cols], 1.0, hn[:], ALU.subtract, ALU.mult)
+            for s, (hn, xn) in enumerate(banks):
+                cols = slice(H * s, H * (s + 1))
+                nc.vector.tensor_tensor(cd[:, cols], xn[:], part[:, cols], ALU.subtract)
+            nc.scalar.activation(cd[:, 0:w], cd[:, 0:w], ACT.Tanh, bias=bn_sb[:, g, t : t + 1])
             return cd
 
         woven = {}
         done = {k: 0 for k in range(8)}
 
-        old = {}
-
-        def gather_h(k):
-            old[k] = ring.tile([P, J], F32, name="old", tag="old", bufs=3)
-            nc.vector.tensor_copy(old[k][:], h_rows[k][:].indirect(listed(0, J)))
-
-        def middle(item, z, cd, d):
+        def blend(item, keepw, cd, last):
             k, halves = item
             j0, j1 = H * halves[0], H * (halves[-1] + 1)
             w = j1 - j0
-            nc.gpsimd.tensor_tensor(d[:, 0:w], cd[:, 0:w], old[k][:, j0:j1], ALU.subtract)
-            nc.gpsimd.tensor_tensor(d[:, 0:w], d[:, 0:w], z[:, 0:w], ALU.mult)
-            nc.gpsimd.tensor_tensor(d[:, 0:w], d[:, 0:w], old[k][:, j0:j1], ALU.add)
-            nc.gpsimd.tensor_tensor(d[:, 0:w], d[:, 0:w], wgo_sb[:, j0:j1], ALU.mult)
+            d = ring.tile([P, J], F32, name="d", tag="work", bufs=DEPTH, align_bytes=64)
+            mid = ring.tile([P, J], F32, name="mid", tag="mid", bufs=1)
+            nc.vector.tensor_tensor(d[:, 0:w], h_rows[k][:].indirect(listed(j0, j1)), cd[:, 0:w], ALU.subtract)
+            nc.gpsimd.tensor_tensor(mid[:, 0:w], d[:, 0:w], keepw[:, 0:w], ALU.mult)
+            if last:
+                nc.gpsimd.tensor_tensor(d[:, 0:w], mid[:, 0:w], cd[:, 0:w], ALU.add)
+            else:
+                nc.gpsimd.tensor_tensor(mid[:, 0:w], mid[:, 0:w], cd[:, 0:w], ALU.add)
+                nc.gpsimd.tensor_tensor(d[:, 0:w], mid[:, 0:w], wgo_sb[:, j0:j1], ALU.mult)
             return d
 
-        def put(item, d):
+        def put(item, d, last):
             k, halves = item
             j0, j1 = H * halves[0], H * (halves[-1] + 1)
-            nc.vector.tensor_copy(pages[k % NPAGE][:].indirect(listed(j0, j1)), d[:, 0 : j1 - j0])
+            window = pages[k % NPAGE][:].indirect(listed(j0, j1))
+            if last:
+                nc.vector.tensor_tensor(window, d[:, 0 : j1 - j0], wgo_sb[:, j0:j1], ALU.mult)
+            else:
+                nc.vector.tensor_copy(window, d[:, 0 : j1 - j0])
             done[k] = done[k] + len(halves)
             return k if done[k] == 2 else None
 
         def finish(k):
-            g, t = divmod(k, 4)
+            g, t = tiles[k]
             page = pages[k % NPAGE]
             nc.sync.dma_start(out_0.rearrange("(g p t) c -> g t p c", p=P, t=PACK)[g, t], page[:])
             for c in range(T // H):
-                if t == 0:
-                    woven[c] = ring.tile([P, H, PACK], BF16, name="yb", tag="woven", bufs=5, align_bytes=64)
-                nc.scalar.copy(woven[c][:, :, t], page[:, H * c : H * (c + 1)])
-            if t == PACK - 1:
-                for c in range(T // H):
-                    cols = slice(H * c, H * (c + 1))
-                    codes = ring.tile([P, H], U32, name="y_codes", tag="y_codes", bufs=4, align_bytes=64)
-                    nc.vector.quantize_mx(out=codes[:].bitcast(FP8X4), scales=y_sc[4 * g : P, cols],
-                                          in_=woven[c][:].rearrange("p c t -> p (c t)"))
-                    nc.sync.dma_start(out_1[g].rearrange("p t b -> p (t b)")[:, 4 * H * c : 4 * H * (c + 1)].bitcast(I32),
-                                      codes[:].bitcast(I32))
-                for q in range(4):
-                    nc.sync.dma_start(out_2[g, 4 * q : 4 * q + 4, :].bitcast(I32),
-                                      y_sc[32 * q + 4 * g : 32 * q + 4 * g + 4, :].bitcast(I32))
+                if k % 4 == 0:
+                    woven[g, c] = ring.tile([P, H, PACK], BF16, name="yb", tag="woven", bufs=8, align_bytes=64)
+                if k == 7 and c == 3:
+                    nc.vector.tensor_copy(woven[g, c][:, :, t], page[:, H * c : H * (c + 1)])
+                else:
+                    nc.scalar.copy(woven[g, c][:, :, t], page[:, H * c : H * (c + 1)])
 
-        ready = {}
-        gated = {0: gates(items[0])}
-        gather_h(0)
-        for i in range(len(items) + 3):
-            if i == 1:
-                table[1] = gather_table(1)
-                for a in range(2):
-                    quant_x(round_x(x_raw[a, 1]), a, 1)
-                h_rows[2] = load_h(2)
-                for nm, words in all_words:
-                    w_raw[nm, 1] = load_w(words, 1)
-            if i == 3:
-                w_sc[1] = deal_scales(1)
-            if 2 <= i <= 5:
-                nm = all_words[i - 2][0]
-                w_dealt[nm, 1] = deal_w(w_raw[nm, 1], nm + "1")
-            if 3 <= i <= 7:
-                h_rows[i] = load_h(i)
-            full = put(items[i - 3], ready[i - 3]) if i >= 3 else None
-            if i < len(items):
-                z, banks = gated[i]
-                work = sums(z, banks)
-                if i + 1 < len(items) and items[i + 1][0] not in old:
-                    gather_h(items[i + 1][0])
-            if full is not None and full % 4 == 3:
+        def planes(g, y_sc, chunks):
+            codes = ring.tile([P, T], U32, name="y_codes", tag="big", bufs=5, align_bytes=64)
+            for c in chunks:
+                cols = slice(H * c, H * (c + 1))
+                nc.vector.quantize_mx(out=codes[:, cols].bitcast(FP8X4), scales=y_sc[:, cols],
+                                      in_=woven[g, c][:].rearrange("p c t -> p (c t)"))
+                nc.sync.dma_start(out_1[g].rearrange("p t b -> p (t b)")[:, 4 * H * c : 4 * H * (c + 1)].bitcast(I32),
+                                  codes[:, cols].bitcast(I32))
+            for q in range(4):
+                nc.sync.dma_start(out_2[g, 4 * q : 4 * q + 4, :].bitcast(I32), y_sc[32 * q : 32 * q + 4, :].bitcast(I32))
+
+        late = keep.tile([P, 8, H], I32, name="late_dealt", align_bytes=64)
+        for n, (nm, words) in enumerate(all_words):
+            w_dealt[nm, 1] = late[:, 2 * n : 2 * n + 2, :]
+        for n in range(4):
+            nc.gpsimd.tensor_copy(late[:, 2 * n : 2 * n + 2, :].rearrange("p a (t c i) -> p a c t i", t=4, i=4),
+                                  late_raw[:, 2 * n : 2 * n + 2, :].rearrange("p a (c i t) -> p a c t i", t=4, i=4))
+        count = len(items)
+        gated, cands, news = {0: gates(items[0])}, {}, {}
+        for i in range(count + 3):
+            full = put(items[i - 3], news[i - 3], i - 3 == count - 1) if i >= 3 else None
+            if i < count:
+                cands[i] = candidate(items[i], *gated[i])
+            if 1 <= i <= count:
+                news[i - 1] = blend(items[i - 1], gated[i - 1][0], cands[i - 1], i == count)
+            if i + 1 < count:
+                gated[i + 1] = gates(items[i + 1])
+            if full is not None:
                 finish(full)
-            if i < len(items):
-                cd = candidate(items[i], work)
-                if i + 1 < len(items):
-                    gated[i + 1] = gates(items[i + 1])
-                ready[i] = middle(items[i], z, cd, work)
-            if full is not None and full % 4 != 3:
-                finish(full)
+        y_sc0 = keep.tile([P, T], U8, name="y_sc0", tag="wgo", align_bytes=64)
+        y_sc1 = keep.tile([P, T], U8, name="y_sc1", align_bytes=64)
+        planes(0, y_sc0, (0, 1, 2, 3))
+        planes(1, y_sc1, (3, 0, 1, 2))

@@ -18,11 +18,20 @@ ACT = mybir.ActivationFunctionType
 
 P = 128
 PACK = 4
-KP = P * PACK
-H = 512
-NPAGE = 2
-DEPTH = 2
-NCD = 3
+PASS = P * PACK
+COLS = 512
+QUADS = 4
+QUAD = 32
+PASSES = K // PASS
+GROUPS = N // PASS
+HALVES = J // COLS
+CHUNKS = T // COLS
+LINE = 16
+PAGES = 2
+TILES = [(g, t) for g in range(GROUPS) for t in (0, 2, 1, 3)]
+LAST = len(TILES) - 1
+LAG = 3
+VECTOR_CHUNK = CHUNKS - 1
 
 
 def tile_list_tgn_mguP_kernel(
@@ -35,274 +44,263 @@ def tile_list_tgn_mguP_kernel(
         ring = ctx.enter_context(tc.tile_pool(name="ring", bufs=2))
         psum = ctx.enter_context(tc.psum_pool(name="psum", bufs=2))
 
+        def big(shape, dtype, name):
+            return ring.tile(shape, dtype, name=name, tag="big", bufs=5, align_bytes=64)
+
+        def woven_tile(name):
+            return ring.tile([P, COLS, PACK], BF16, name=name, tag="woven", bufs=8, align_bytes=64)
+
+        def work_tile(dtype, name):
+            return ring.tile([P, J], dtype, name=name, tag="work", bufs=2, align_bytes=64)
+
         offsets = keep.tile([P, J // 16], U16, name="offsets")
         nc.sync.dma_start(offsets[:], offs)
 
-        tiles = [(g, t) for g in range(2) for t in (0, 2, 1, 3)]
-
-        def listed(j0, j1):
-            return offsets[:, j0 // 16 : j1 // 16]
-
-        tab_sc = keep.tile([P, 2, T], U8, name="tab_sc", align_bytes=64)
-        xw_sc_raw = keep.tile([P, N], U8, name="xw_sc_raw", align_bytes=64)
-        hw_sc_raw = keep.tile([P, 4, N], U8, name="hw_sc_raw", align_bytes=64)
+        tab_sc = keep.tile([P, PASSES, T], U8, name="tab_sc", align_bytes=64)
+        w_sc_raw = keep.tile([P, N], U8, name="w_sc_raw", align_bytes=64)
+        u_sc_raw = [keep.tile([P, PASSES, N], U8, name="u_sc_raw%d" % n, align_bytes=64) for n in range(2)]
         nc.gpsimd.memset(tab_sc[:].rearrange("p a t -> p (a t)").bitcast(I32), 0)
-        nc.vector.memset(hw_sc_raw[:].rearrange("p a t -> p (a t)").bitcast(I32), 0)
-        nc.vector.memset(xw_sc_raw[:].bitcast(I32), 0)
+        for raw in u_sc_raw:
+            nc.vector.memset(raw[:].rearrange("p a t -> p (a t)").bitcast(I32), 0)
+        nc.vector.memset(w_sc_raw[:].bitcast(I32), 0)
 
-        warm = keep.tile([P, 1], F32, name="warm")
-        bz_sb = keep.tile([P, 2, PACK], F32, name="bz_sb")
-        bn_sb = keep.tile([P, 2, PACK], F32, name="bn_sb")
+        bz_sb = keep.tile([P, GROUPS, PACK], F32, name="bz_sb")
+        bn_sb = keep.tile([P, GROUPS, PACK], F32, name="bn_sb")
+        x_codes = [keep.tile([P, PASSES, COLS], U32, name="x_codes%d" % half, align_bytes=64) for half in range(HALVES)]
+        x_sc = [keep.tile([P, PASSES, COLS], U8, name="x_sc%d" % half, align_bytes=64) for half in range(HALVES)]
 
-        def load_x(a, jh):
-            raw = ring.tile([P, PACK, H], F32, name="xraw", tag="big", bufs=5, align_bytes=64)
-            nc.sync.dma_start(raw[:], x[KP * a : KP * (a + 1), H * jh : H * (jh + 1)].rearrange("(p i) c -> p i c", i=PACK))
+        def load_x(a, half):
+            raw = big([P, PACK, COLS], F32, "x_raw")
+            rows = x[PASS * a : PASS * (a + 1), COLS * half : COLS * (half + 1)]
+            nc.sync.dma_start(raw[:], rows.rearrange("(p i) c -> p i c", i=PACK))
             return raw
 
-        x_codes = [keep.tile([P, 2, H], U32, name="x_codes%d" % jh, align_bytes=64) for jh in range(2)]
-        x_sc = [keep.tile([P, 2, H], U8, name="x_sc%d" % jh, align_bytes=64) for jh in range(2)]
+        def load_planes(dst, scales):
+            for r in range(QUADS):
+                nc.sync.dma_start(dst[r:P:QUAD, :, :].bitcast(I32),
+                                  scales[:, r : QUADS * QUADS : QUADS, :].rearrange("a q t -> q a t").bitcast(I32))
 
-        def round_x(raw):
-            xb = ring.tile([P, H, PACK], BF16, name="xb", tag="woven", bufs=8, align_bytes=64)
-            nc.scalar.copy(xb[:].rearrange("p (c i) t -> p c t i", i=4), raw[:].rearrange("p t (c i) -> p c t i", i=4))
-            return xb
+        def load_packed_planes(n, scales):
+            rows = PASSES * QUADS
+            for q in range(QUADS):
+                first = QUAD * q + rows * n
+                nc.sync.dma_start(w_sc_raw[first : first + rows, :].bitcast(I32),
+                                  scales[:, QUADS * q : QUADS * (q + 1), :].bitcast(I32))
 
-        def quant_x(xb, a, jh):
-            nc.vector.quantize_mx(out=x_codes[jh][:, a, :].bitcast(FP8X4), scales=x_sc[jh][:, a, :],
-                                  in_=xb[:].rearrange("p c t -> p (c t)"))
+        def load_words(raw, words, g):
+            columns = words.rearrange("a p n i -> p a (n i)")[:, :, PACK * PASS * g : PACK * PASS * (g + 1)]
+            nc.sync.dma_start(raw[:], columns.bitcast(I32))
+            return raw
 
-        def load_w(raw, words, g):
-            nc.sync.dma_start(raw, words.rearrange("a p n i -> p a (n i)")[:, :, 4 * H * g : 4 * H * (g + 1)].bitcast(I32))
+        def load_first_words(name):
+            raw = keep.tile([P, PASSES, PASS], I32, name="first_raw", tag="raw_" + name, align_bytes=64)
+            return load_words(raw, words_of[name], 0)
 
-        def deal_w(eng, raw, name):
-            dealt = keep.tile(list(raw.shape), I32, name=name, align_bytes=64)
-            eng.tensor_copy(dealt[:].rearrange("p a (t c i) -> p a c t i", t=4, i=4),
-                                  raw[:].rearrange("p a (c i t) -> p a c t i", t=4, i=4))
-            return dealt
-
-        def deal_scales(eng, g):
-            xw = keep.tile([P, H], U8, name="xw_sc%d" % g, align_bytes=64)
-            hw = keep.tile([P, 4, H], U8, name="hw_sc%d" % g, align_bytes=64)
-            eng.tensor_copy(hw[:].rearrange("p a (t c i) -> p a c t i", t=4, i=16),
-                                  hw_sc_raw[:, :, H * g : H * (g + 1)].rearrange("p a (c i t) -> p a c t i", t=4, i=16))
-            eng.tensor_copy(xw[:].rearrange("p (t c i) -> p c t i", t=4, i=16),
-                                  xw_sc_raw[:, H * g : H * (g + 1)].rearrange("p (c i t) -> p c t i", t=4, i=16))
-            return xw, hw
-
-        def load_h(k):
-            g, t = tiles[k]
-            rows = ring.tile([P, T], F32, name="hrows", tag="big", bufs=5, align_bytes=64)
+        def load_state(k, rows):
+            g, t = TILES[k]
             nc.sync.dma_start(rows[:], hT.rearrange("(g p t) c -> g t p c", p=P, t=PACK)[g, t])
             return rows
 
-        def gather_table():
-            picked = ring.tile([P, J], U32, name="picked", tag="work", bufs=DEPTH, align_bytes=64)
-            codes = keep.tile([P, 2, 2 * J], U8, name="v_codes", align_bytes=64)
-            scales = keep.tile([P, 2, J], U8, name="v_sc", align_bytes=64)
-            nc.vector.tensor_copy(picked[:], tabw[:].bitcast(U32).indirect(offsets[:]))
-            nc.vector.tensor_copy(scales[:, 0, :], tab_sc[:, 0, :].indirect(offsets[:]))
-            nc.vector.tensor_copy(codes[:].bitcast(U16).rearrange("p d (c i) -> p c d i", i=8),
-                                  picked[:].bitcast(U16).rearrange("p (c i d) -> p c d i", i=8, d=2))
-            nc.vector.tensor_copy(scales[:, 1, :], tab_sc[:, 1, :].indirect(offsets[:]))
-            return codes, scales
+        def deal(dst, src, run):
+            lead = "p a" if len(src.shape) == 3 else "p"
+            nc.vector.tensor_copy(dst.rearrange("%s (t c i) -> %s c t i" % (lead, lead), t=PACK, i=run),
+                                  src.rearrange("%s (c i t) -> %s c t i" % (lead, lead), t=PACK, i=run))
 
-        def load_tab_sc(q):
-            nc.sync.dma_start(
-                tab_sc[32 * q : 32 * q + 4, :, :].bitcast(I32),
-                tab_scales[:, 4 * q : 4 * q + 4, :].rearrange("a r t -> r a t").bitcast(I32),
-            )
+        def deal_words(raw, name, tag):
+            dealt = keep.tile([P, PASSES, PASS], I32, name=name, tag=tag, align_bytes=64)
+            deal(dealt[:], raw[:], LINE // 4)
+            return dealt
 
-        def load_hw_sc(w, q):
-            nc.sync.dma_start(
-                hw_sc_raw[32 * q : 32 * q + 4, 2 * w : 2 * w + 2, :].bitcast(I32),
-                (uz_scales, un_scales)[w][:, 4 * q : 4 * q + 4, :].rearrange("a r t -> r a t").bitcast(I32),
-            )
-
-        def load_xw_sc(w, q):
-            nc.sync.dma_start(
-                xw_sc_raw[32 * q + 8 * w : 32 * q + 8 * w + 8, :].bitcast(I32),
-                (wz_scales, wn_scales)[w][:, 4 * q : 4 * q + 4, :].bitcast(I32),
-            )
-
+        words_of = {"uz": uz_words, "wz": wz_words, "un": un_words, "wn": wn_words}
+        tab_w = big([P, T], I32, "tab_w")
+        tab_rows = tab_words[0].rearrange("p t b -> p (t b)").bitcast(I32)
+        for c in range(CHUNKS):
+            nc.sync.dma_start(tab_w[:, COLS * c : COLS * (c + 1)], tab_rows[:, COLS * c : COLS * (c + 1)])
+        wgo_sb = keep.tile([P, J], F32, name="wgo_sb", tag="wgo", align_bytes=64)
+        x_raw, first_raw = {}, {}
+        x_raw[0, 0] = load_x(0, 0)
         nc.sync.dma_start(bz_sb[:], bz.rearrange("(g p t) -> p g t", p=P, t=PACK))
         nc.sync.dma_start(bn_sb[:], bn.rearrange("(g p t) -> p g t", p=P, t=PACK))
-        tabw = ring.tile([P, T], I32, name="tabw", tag="big", bufs=5, align_bytes=64)
-        tab_rows = tab_words[0].rearrange("p t b -> p (t b)").bitcast(I32)
-        for c in range(4):
-            nc.sync.dma_start(tabw[:, H * c : H * (c + 1)], tab_rows[:, H * c : H * (c + 1)])
-        x_raw = {}
-        x_raw[0, 0] = load_x(0, 0)
-        for q in range(4):
-            load_tab_sc(q)
         x_raw[1, 0] = load_x(1, 0)
-        for q in range(4):
-            load_hw_sc(0, q)
+        load_planes(tab_sc, tab_scales)
         x_raw[0, 1] = load_x(0, 1)
-        for q in range(4):
-            load_hw_sc(1, q)
+        load_planes(u_sc_raw[0], uz_scales)
+        first_raw["uz"] = load_first_words("uz")
+        first_raw["un"] = load_first_words("un")
+        load_planes(u_sc_raw[1], un_scales)
         x_raw[1, 1] = load_x(1, 1)
-        all_words = (("uz", uz_words), ("wz", wz_words), ("un", un_words), ("wn", wn_words))
-        w_raw = {}
-        for n, (nm, words) in enumerate(all_words):
-            if n < 2:
-                for q in range(4):
-                    load_xw_sc(n, q)
-            w_raw[nm] = ring.tile([P, 2, H], I32, name="wraw", tag="z", bufs=4, align_bytes=64)
-            load_w(w_raw[nm][:], words, 0)
-        late_raw = keep.tile([P, 8, H], I32, name="late_raw", align_bytes=64)
-        for n, (nm, words) in enumerate(all_words):
-            load_w(late_raw[:, 2 * n : 2 * n + 2, :], words, 1)
-        h_rows = {0: load_h(0)}
-        wgo_sb = keep.tile([P, J], F32, name="wgo_sb", tag="wgo", align_bytes=64)
+        load_packed_planes(0, wz_scales)
+        first_raw["wz"] = load_first_words("wz")
+        load_packed_planes(1, wn_scales)
+        first_raw["wn"] = load_first_words("wn")
+        second_raw = {
+            name: load_words(ring.tile([P, PASSES, PASS], I32, name="second_raw", tag="second", bufs=4, align_bytes=64),
+                             words, 1)
+            for name, words in words_of.items()
+        }
+        state = {0: load_state(0, keep.tile([P, T], F32, name="state0", tag="state0", align_bytes=64))}
         nc.sync.dma_start(wgo_sb[:], wgo)
-        for k in range(1, 8):
-            h_rows[k] = load_h(k)
+        for k in range(1, len(TILES)):
+            state[k] = load_state(k, big([P, T], F32, "state"))
 
-        nc.vector.memset(warm[:], 0.0)
-        nc.scalar.activation(warm[:], warm[:], ACT.Sigmoid)
-
-        pages = [keep.tile([P, T], F32, name="page%d" % i, align_bytes=64) for i in range(NPAGE)]
+        pages = [keep.tile([P, T], F32, name="page%d" % n, align_bytes=64) for n in range(PAGES)]
         for page in pages:
             nc.vector.memset(page[:], 0.0)
 
-        bz_neg = keep.tile([P, 2, PACK], F32, name="bz_neg")
+        bz_neg = keep.tile([P, GROUPS, PACK], F32, name="bz_neg")
         nc.scalar.activation(bz_neg[:], bz_sb[:], ACT.Copy, scale=-1.0)
-        v_codes, v_sc = gather_table()
-        for jh in range(2):
-            for a in range(2):
-                quant_x(round_x(x_raw[a, jh]), a, jh)
-        w_sc = {0: deal_scales(nc.vector, 0)}
-        w_dealt = {(nm, 0): deal_w(nc.vector, w_raw[nm], nm + "0") for nm, words in all_words}
-        w_sc[1] = deal_scales(nc.vector, 1)
 
-        def products(k, jh):
-            g, t = tiles[k]
+        picked = work_tile(U32, "picked")
+        v_codes = keep.tile([P, PASSES, 2 * J], U8, name="v_codes", align_bytes=64)
+        v_sc = keep.tile([P, PASSES, J], U8, name="v_sc", align_bytes=64)
+        nc.vector.tensor_copy(picked[:], tab_w[:].bitcast(U32).indirect(offsets[:]))
+        nc.vector.tensor_copy(v_sc[:, 0, :], tab_sc[:, 0, :].indirect(offsets[:]))
+        nc.vector.tensor_copy(v_codes[:].bitcast(U16).rearrange("p a (c i) -> p c a i", i=LINE // 2),
+                              picked[:].bitcast(U16).rearrange("p (c i a) -> p c a i", i=LINE // 2, a=PASSES))
+        nc.vector.tensor_copy(v_sc[:, 1, :], tab_sc[:, 1, :].indirect(offsets[:]))
+
+        def quantise_x(half):
+            for a in range(PASSES):
+                rounded = woven_tile("x_rounded")
+                nc.scalar.copy(rounded[:].rearrange("p (c n) i -> p c i n", n=LINE // 4),
+                               x_raw[a, half][:].rearrange("p i (c n) -> p c i n", n=LINE // 4))
+                nc.vector.quantize_mx(out=x_codes[half][:, a, :].bitcast(FP8X4), scales=x_sc[half][:, a, :],
+                                      in_=rounded[:].rearrange("p c i -> p (c i)"))
+
+        planes_of = {0: {"uz": keep.tile([P, PASSES, PASS], U8, name="uz_sc0", align_bytes=64)[:],
+                         "un": keep.tile([P, PASSES, PASS], U8, name="un_sc0", align_bytes=64)[:],
+                         "w": keep.tile([P, PASS], U8, name="w_sc0", align_bytes=64)[:]}}
+        dealt = {}
+        for n, name in enumerate(("uz", "un")):
+            deal(planes_of[0][name], u_sc_raw[n][:, :, 0:PASS], LINE)
+            dealt[name, 0] = deal_words(first_raw[name], name + "0", name + "0")
+        for half in range(HALVES):
+            quantise_x(half)
+        deal(planes_of[0]["w"], w_sc_raw[:, 0:PASS], LINE)
+        for name in ("wz", "wn"):
+            dealt[name, 0] = deal_words(first_raw[name], name + "0", name + "0")
+
+        def products(k, half):
+            g, t = TILES[k]
             cols = slice(P * t, P * (t + 1))
-            xw_sc, hw_sc = w_sc[g]
 
-            def with_x(bank, nm, w, first, last):
-                for a in range(2):
-                    nc.tensor.matmul_mx(out=bank[:], lhsT=w_dealt[nm, g][:, a, cols].bitcast(FP8X4),
-                                        lhsT_scale=xw_sc[8 * w + 4 * a : P, cols],
-                                        rhs=x_codes[jh][:, a, :].bitcast(FP8X4), rhs_scale=x_sc[jh][:, a, :],
-                                        start=first and a == 0, stop=last and a == 1)
+            def with_x(bank, name, n, opens):
+                for a in range(PASSES):
+                    nc.tensor.matmul_mx(out=bank[:], lhsT=dealt[name, g][:, a, cols].bitcast(FP8X4),
+                                        lhsT_scale=planes_of[g]["w"][QUADS * (PASSES * n + a) : P, cols],
+                                        rhs=x_codes[half][:, a, :].bitcast(FP8X4), rhs_scale=x_sc[half][:, a, :],
+                                        start=opens and a == 0, stop=a == PASSES - 1)
 
-            def with_v(bank, nm, w, first, last):
-                for a in range(2):
-                    nc.tensor.matmul_mx(out=bank[:], lhsT=w_dealt[nm, g][:, a, cols].bitcast(FP8X4),
-                                        lhsT_scale=hw_sc[:, 2 * w + a, cols],
-                                        rhs=v_codes[:, a, 2 * H * jh : 2 * H * (jh + 1)].bitcast(FP4X4),
-                                        rhs_scale=v_sc[:, a, H * jh : H * (jh + 1)],
-                                        start=first and a == 0, stop=last and a == 1)
+            def with_v(bank, name, closes):
+                for a in range(PASSES):
+                    nc.tensor.matmul_mx(out=bank[:], lhsT=dealt[name, g][:, a, cols].bitcast(FP8X4),
+                                        lhsT_scale=planes_of[g][name][:, a, cols],
+                                        rhs=v_codes[:, a, 2 * COLS * half : 2 * COLS * (half + 1)].bitcast(FP4X4),
+                                        rhs_scale=v_sc[:, a, COLS * half : COLS * (half + 1)],
+                                        start=a == 0, stop=closes and a == PASSES - 1)
 
-            sz = psum.tile([P, H], F32, name="sz", tag="sz", bufs=2)
-            hn = psum.tile([P, H], F32, name="hn", tag="hn", bufs=3)
-            xn = psum.tile([P, H], F32, name="xn", tag="xn", bufs=3)
-            with_v(sz, "uz", 0, True, False)
-            with_x(sz, "wz", 0, False, True)
-            with_v(hn, "un", 1, True, True)
-            with_x(xn, "wn", 1, True, True)
+            sz = psum.tile([P, COLS], F32, name="sz", tag="sz", bufs=2)
+            hn = psum.tile([P, COLS], F32, name="hn", tag="hn", bufs=3)
+            xn = psum.tile([P, COLS], F32, name="xn", tag="xn", bufs=3)
+            with_v(sz, "uz", False)
+            with_x(sz, "wz", 0, False)
+            with_v(hn, "un", True)
+            with_x(xn, "wn", 1, True)
             return sz, hn, xn
 
-        items = [(k, (0, 1)) for k in range(8)]
-
-        def gates(item):
-            k, halves = item
-            g, t = tiles[k]
-            z = ring.tile([P, J], F32, name="z", tag="z", bufs=4, align_bytes=64)
+        def gate(k):
+            g, t = TILES[k]
+            stay = ring.tile([P, J], F32, name="stay", tag="stay", bufs=4, align_bytes=64)
             banks = []
-            for s, jh in enumerate(halves):
-                sz, hn, xn = products(k, jh)
-                nc.scalar.activation(z[:, H * s : H * (s + 1)], sz[:], ACT.Sigmoid, bias=bz_neg[:, g, t : t + 1], scale=-1.0)
+            for half in range(HALVES):
+                sz, hn, xn = products(k, half)
+                nc.scalar.activation(stay[:, COLS * half : COLS * (half + 1)], sz[:], ACT.Sigmoid,
+                                     bias=bz_neg[:, g, t : t + 1], scale=-1.0)
                 banks.append((hn, xn))
-            return z, banks
+            return stay, banks
 
-        def candidate(item, keepw, banks):
-            k, halves = item
-            g, t = tiles[k]
-            w = H * len(halves)
-            part = ring.tile([P, J], F32, name="part", tag="work", bufs=DEPTH, align_bytes=64)
-            cd = ring.tile([P, J], F32, name="cd", tag="cd", bufs=NCD)
-            for s, (hn, xn) in enumerate(banks):
-                cols = slice(H * s, H * (s + 1))
-                nc.vector.scalar_tensor_tensor(part[:, cols], keepw[:, cols], 1.0, hn[:], ALU.subtract, ALU.mult)
-            for s, (hn, xn) in enumerate(banks):
-                cols = slice(H * s, H * (s + 1))
-                nc.vector.tensor_tensor(cd[:, cols], xn[:], part[:, cols], ALU.subtract)
-            nc.scalar.activation(cd[:, 0:w], cd[:, 0:w], ACT.Tanh, bias=bn_sb[:, g, t : t + 1])
-            return cd
+        def candidate(k, stay, banks):
+            g, t = TILES[k]
+            gated = work_tile(F32, "gated")
+            cand = ring.tile([P, J], F32, name="cand", tag="cand", bufs=3)
+            for half, (hn, xn) in enumerate(banks):
+                cols = slice(COLS * half, COLS * (half + 1))
+                nc.vector.scalar_tensor_tensor(gated[:, cols], stay[:, cols], 1.0, hn[:], ALU.subtract, ALU.mult)
+            for half, (hn, xn) in enumerate(banks):
+                cols = slice(COLS * half, COLS * (half + 1))
+                nc.vector.scalar_tensor_tensor(cand[:, cols], gated[:, cols], -1.0, xn[:], ALU.mult, ALU.add)
+            nc.scalar.activation(cand[:], cand[:], ACT.Tanh, bias=bn_sb[:, g, t : t + 1])
+            return cand
+
+        def blend(k, stay, cand):
+            rows = work_tile(F32, "rows")
+            mid = ring.tile([P, J], F32, name="mid", tag="mid", bufs=1)
+            nc.vector.tensor_tensor(rows[:], state[k][:].indirect(offsets[:]), cand[:], ALU.subtract)
+            nc.gpsimd.tensor_tensor(mid[:], rows[:], stay[:], ALU.mult)
+            if k == LAST:
+                nc.gpsimd.tensor_tensor(rows[:], mid[:], cand[:], ALU.add)
+            else:
+                nc.gpsimd.tensor_tensor(mid[:], mid[:], cand[:], ALU.add)
+                nc.gpsimd.tensor_tensor(rows[:], mid[:], wgo_sb[:], ALU.mult)
+            return rows
+
+        def scatter(k, rows):
+            window = pages[k % PAGES][:].indirect(offsets[:])
+            if k == LAST:
+                nc.vector.tensor_tensor(window, rows[:], wgo_sb[:], ALU.mult)
+            else:
+                nc.vector.tensor_copy(window, rows[:])
 
         woven = {}
-        done = {k: 0 for k in range(8)}
 
-        def blend(item, keepw, cd, last):
-            k, halves = item
-            j0, j1 = H * halves[0], H * (halves[-1] + 1)
-            w = j1 - j0
-            d = ring.tile([P, J], F32, name="d", tag="work", bufs=DEPTH, align_bytes=64)
-            mid = ring.tile([P, J], F32, name="mid", tag="mid", bufs=1)
-            nc.vector.tensor_tensor(d[:, 0:w], h_rows[k][:].indirect(listed(j0, j1)), cd[:, 0:w], ALU.subtract)
-            nc.gpsimd.tensor_tensor(mid[:, 0:w], d[:, 0:w], keepw[:, 0:w], ALU.mult)
-            if last:
-                nc.gpsimd.tensor_tensor(d[:, 0:w], mid[:, 0:w], cd[:, 0:w], ALU.add)
-            else:
-                nc.gpsimd.tensor_tensor(mid[:, 0:w], mid[:, 0:w], cd[:, 0:w], ALU.add)
-                nc.gpsimd.tensor_tensor(d[:, 0:w], mid[:, 0:w], wgo_sb[:, j0:j1], ALU.mult)
-            return d
-
-        def put(item, d, last):
-            k, halves = item
-            j0, j1 = H * halves[0], H * (halves[-1] + 1)
-            window = pages[k % NPAGE][:].indirect(listed(j0, j1))
-            if last:
-                nc.vector.tensor_tensor(window, d[:, 0 : j1 - j0], wgo_sb[:, j0:j1], ALU.mult)
-            else:
-                nc.vector.tensor_copy(window, d[:, 0 : j1 - j0])
-            done[k] = done[k] + len(halves)
-            return k if done[k] == 2 else None
-
-        def finish(k):
-            g, t = tiles[k]
-            page = pages[k % NPAGE]
+        def hand_out(k):
+            g, t = TILES[k]
+            page = pages[k % PAGES]
             nc.sync.dma_start(out_0.rearrange("(g p t) c -> g t p c", p=P, t=PACK)[g, t], page[:])
-            for c in range(T // H):
-                if k % 4 == 0:
-                    woven[g, c] = ring.tile([P, H, PACK], BF16, name="yb", tag="woven", bufs=8, align_bytes=64)
-                if k == 7 and c == 3:
-                    nc.vector.tensor_copy(woven[g, c][:, :, t], page[:, H * c : H * (c + 1)])
+            for c in range(CHUNKS):
+                if k % PACK == 0:
+                    woven[g, c] = woven_tile("y_rounded")
+                if k == LAST and c == VECTOR_CHUNK:
+                    nc.vector.tensor_copy(woven[g, c][:, :, t], page[:, COLS * c : COLS * (c + 1)])
                 else:
-                    nc.scalar.copy(woven[g, c][:, :, t], page[:, H * c : H * (c + 1)])
+                    nc.scalar.copy(woven[g, c][:, :, t], page[:, COLS * c : COLS * (c + 1)])
 
-        def planes(g, y_sc, chunks):
-            codes = ring.tile([P, T], U32, name="y_codes", tag="big", bufs=5, align_bytes=64)
+        def quantise_out(g, y_sc, chunks):
+            codes = big([P, T], U32, "y_codes")
             for c in chunks:
-                cols = slice(H * c, H * (c + 1))
+                cols = slice(COLS * c, COLS * (c + 1))
                 nc.vector.quantize_mx(out=codes[:, cols].bitcast(FP8X4), scales=y_sc[:, cols],
                                       in_=woven[g, c][:].rearrange("p c t -> p (c t)"))
-                nc.sync.dma_start(out_1[g].rearrange("p t b -> p (t b)")[:, 4 * H * c : 4 * H * (c + 1)].bitcast(I32),
-                                  codes[:, cols].bitcast(I32))
-            for q in range(4):
-                nc.sync.dma_start(out_2[g, 4 * q : 4 * q + 4, :].bitcast(I32), y_sc[32 * q : 32 * q + 4, :].bitcast(I32))
+                words = out_1[g].rearrange("p t b -> p (t b)")[:, PACK * COLS * c : PACK * COLS * (c + 1)]
+                nc.sync.dma_start(words.bitcast(I32), codes[:, cols].bitcast(I32))
+            for r in range(QUADS):
+                nc.sync.dma_start(out_2[g, r : QUADS * QUADS : QUADS, :].bitcast(I32), y_sc[r:P:QUAD, :].bitcast(I32))
 
-        late = keep.tile([P, 8, H], I32, name="late_dealt", align_bytes=64)
-        for n, (nm, words) in enumerate(all_words):
-            w_dealt[nm, 1] = late[:, 2 * n : 2 * n + 2, :]
-        for n in range(4):
-            nc.gpsimd.tensor_copy(late[:, 2 * n : 2 * n + 2, :].rearrange("p a (t c i) -> p a c t i", t=4, i=4),
-                                  late_raw[:, 2 * n : 2 * n + 2, :].rearrange("p a (c i t) -> p a c t i", t=4, i=4))
-        count = len(items)
-        gated, cands, news = {0: gates(items[0])}, {}, {}
-        for i in range(count + 3):
-            full = put(items[i - 3], news[i - 3], i - 3 == count - 1) if i >= 3 else None
-            if i < count:
-                cands[i] = candidate(items[i], *gated[i])
-            if 1 <= i <= count:
-                news[i - 1] = blend(items[i - 1], gated[i - 1][0], cands[i - 1], i == count)
-            if i + 1 < count:
-                gated[i + 1] = gates(items[i + 1])
-            if full is not None:
-                finish(full)
+        gates, cands, blended = {0: gate(0)}, {}, {}
+        for i in range(len(TILES) + LAG):
+            if i >= LAG:
+                scatter(i - LAG, blended[i - LAG])
+            if i <= LAST:
+                cands[i] = candidate(i, *gates[i])
+            if i == 0:
+                for name in words_of:
+                    dealt[name, 1] = deal_words(second_raw[name], name + "1", "raw_" + name)
+                blended[0] = blend(0, gates[0][0], cands[0])
+            if 2 <= i <= LAST + 1:
+                blended[i - 1] = blend(i - 1, gates[i - 1][0], cands[i - 1])
+            if i == PACK - 2:
+                second_sc = keep.tile([P, 2 * PASSES + 1, PASS], U8, name="second_sc", tag="state0", align_bytes=64)
+                planes_of[1] = {"uz": second_sc[:, 0:PASSES, :], "un": second_sc[:, PASSES : 2 * PASSES, :],
+                                "w": second_sc[:, 2 * PASSES, :]}
+                deal(planes_of[1]["uz"], u_sc_raw[0][:, :, PASS:N], LINE)
+                deal(planes_of[1]["un"], u_sc_raw[1][:, :, PASS:N], LINE)
+                deal(planes_of[1]["w"], w_sc_raw[:, PASS:N], LINE)
+            if i < LAST:
+                gates[i + 1] = gate(i + 1)
+            if i >= LAG:
+                hand_out(i - LAG)
+
         y_sc0 = keep.tile([P, T], U8, name="y_sc0", tag="wgo", align_bytes=64)
         y_sc1 = keep.tile([P, T], U8, name="y_sc1", align_bytes=64)
-        planes(0, y_sc0, (0, 1, 2, 3))
-        planes(1, y_sc1, (3, 0, 1, 2))
+        quantise_out(0, y_sc0, range(CHUNKS))
+        quantise_out(1, y_sc1, [VECTOR_CHUNK] + list(range(VECTOR_CHUNK)))

@@ -27,10 +27,13 @@ GROUPS = N // PASS
 HALVES = J // COLS
 CHUNKS = T // COLS
 LINE = 16
-PAGES = 2
-TILES = [(g, t) for g in range(GROUPS) for t in (0, 2, 1, 3)]
+PAGES = 3
+TILES = [(g, t) for g in range(GROUPS) for t in (2, 0, 1, 3)]
 LAST = len(TILES) - 1
 LAG = 3
+ENGINES = ["GGV"] + ["GGG"] * 6 + ["GGF"]
+SPLIT = 512
+PIECES = 1
 VECTOR_CHUNK = CHUNKS - 1
 
 
@@ -51,18 +54,16 @@ def tile_list_tgn_mguP_kernel(
             return ring.tile([P, COLS, PACK], BF16, name=name, tag="woven", bufs=8, align_bytes=64)
 
         def work_tile(dtype, name):
-            return ring.tile([P, J], dtype, name=name, tag="work", bufs=2, align_bytes=64)
+            return ring.tile([P, 2 * J], dtype, name=name, tag="work", bufs=2, align_bytes=64)
 
         offsets = keep.tile([P, J // 16], U16, name="offsets")
         nc.sync.dma_start(offsets[:], offs)
 
         tab_sc = keep.tile([P, PASSES, T], U8, name="tab_sc", align_bytes=64)
-        w_sc_raw = keep.tile([P, N], U8, name="w_sc_raw", align_bytes=64)
         u_sc_raw = [keep.tile([P, PASSES, N], U8, name="u_sc_raw%d" % n, align_bytes=64) for n in range(2)]
         nc.gpsimd.memset(tab_sc[:].rearrange("p a t -> p (a t)").bitcast(I32), 0)
         for raw in u_sc_raw:
             nc.vector.memset(raw[:].rearrange("p a t -> p (a t)").bitcast(I32), 0)
-        nc.vector.memset(w_sc_raw[:].bitcast(I32), 0)
 
         bz_sb = keep.tile([P, GROUPS, PACK], F32, name="bz_sb")
         bn_sb = keep.tile([P, GROUPS, PACK], F32, name="bn_sb")
@@ -75,17 +76,10 @@ def tile_list_tgn_mguP_kernel(
             nc.sync.dma_start(raw[:], rows.rearrange("(p i) c -> p i c", i=PACK))
             return raw
 
-        def load_planes(dst, scales):
+        def load_planes(dst, scales, first, queue):
             for r in range(QUADS):
-                nc.sync.dma_start(dst[r:P:QUAD, :, :].bitcast(I32),
+                queue.dma_start(dst[first + r : P : QUAD, :, :].bitcast(I32),
                                   scales[:, r : QUADS * QUADS : QUADS, :].rearrange("a q t -> q a t").bitcast(I32))
-
-        def load_packed_planes(n, scales):
-            rows = PASSES * QUADS
-            for q in range(QUADS):
-                first = QUAD * q + rows * n
-                nc.sync.dma_start(w_sc_raw[first : first + rows, :].bitcast(I32),
-                                  scales[:, QUADS * q : QUADS * (q + 1), :].bitcast(I32))
 
         def load_words(raw, words, g):
             columns = words.rearrange("a p n i -> p a (n i)")[:, :, PACK * PASS * g : PACK * PASS * (g + 1)]
@@ -121,43 +115,42 @@ def tile_list_tgn_mguP_kernel(
         x_raw[0, 0] = load_x(0, 0)
         nc.sync.dma_start(bz_sb[:], bz.rearrange("(g p t) -> p g t", p=P, t=PACK))
         nc.sync.dma_start(bn_sb[:], bn.rearrange("(g p t) -> p g t", p=P, t=PACK))
+        load_planes(tab_sc, tab_scales, 0, nc.sync)
         x_raw[1, 0] = load_x(1, 0)
-        load_planes(tab_sc, tab_scales)
         x_raw[0, 1] = load_x(0, 1)
-        load_planes(u_sc_raw[0], uz_scales)
+        load_planes(u_sc_raw[0], uz_scales, 0, nc.sync)
         first_raw["uz"] = load_first_words("uz")
+        load_planes(u_sc_raw[0], wz_scales, QUADS, nc.sync)
         first_raw["un"] = load_first_words("un")
-        load_planes(u_sc_raw[1], un_scales)
+        load_planes(u_sc_raw[1], un_scales, 0, nc.sync)
         x_raw[1, 1] = load_x(1, 1)
-        load_packed_planes(0, wz_scales)
+        load_planes(u_sc_raw[1], wn_scales, QUADS, nc.sync)
         first_raw["wz"] = load_first_words("wz")
-        load_packed_planes(1, wn_scales)
         first_raw["wn"] = load_first_words("wn")
-        second_raw = {
-            name: load_words(ring.tile([P, PASSES, PASS], I32, name="second_raw", tag="second", bufs=4, align_bytes=64),
-                             words, 1)
-            for name, words in words_of.items()
-        }
+        second_raw = {name: load_words(ring.tile([P, PASSES, PASS], I32, name="second_raw", tag="second", bufs=4,
+                                                 align_bytes=64), words, 1)
+                      for name, words in words_of.items()}
         state = {0: load_state(0, keep.tile([P, T], F32, name="state0", tag="state0", align_bytes=64))}
+        state[1] = load_state(1, big([P, T], F32, "state"))
         nc.sync.dma_start(wgo_sb[:], wgo)
-        for k in range(1, len(TILES)):
+        for k in range(2, len(TILES)):
             state[k] = load_state(k, big([P, T], F32, "state"))
 
         pages = [keep.tile([P, T], F32, name="page%d" % n, align_bytes=64) for n in range(PAGES)]
         for page in pages:
-            nc.vector.memset(page[:], 0.0)
+            (nc.vector if page is pages[0] else nc.gpsimd).memset(page[:], 0.0)
 
         bz_neg = keep.tile([P, GROUPS, PACK], F32, name="bz_neg")
         nc.scalar.activation(bz_neg[:], bz_sb[:], ACT.Copy, scale=-1.0)
 
-        picked = work_tile(U32, "picked")
+        picked = work_tile(U32, "picked")[:, 0:J]
         v_codes = keep.tile([P, PASSES, 2 * J], U8, name="v_codes", align_bytes=64)
         v_sc = keep.tile([P, PASSES, J], U8, name="v_sc", align_bytes=64)
-        nc.vector.tensor_copy(picked[:], tab_w[:].bitcast(U32).indirect(offsets[:]))
-        nc.vector.tensor_copy(v_sc[:, 0, :], tab_sc[:, 0, :].indirect(offsets[:]))
+        nc.vector.tensor_copy(picked, tab_w[:].bitcast(U32).indirect(offsets[:]))
         nc.vector.tensor_copy(v_codes[:].bitcast(U16).rearrange("p a (c i) -> p c a i", i=LINE // 2),
-                              picked[:].bitcast(U16).rearrange("p (c i a) -> p c a i", i=LINE // 2, a=PASSES))
-        nc.vector.tensor_copy(v_sc[:, 1, :], tab_sc[:, 1, :].indirect(offsets[:]))
+                              picked.bitcast(U16).rearrange("p (c i a) -> p c a i", i=LINE // 2, a=PASSES))
+        for a in range(PASSES):
+            nc.vector.tensor_copy(v_sc[:, a, :], tab_sc[:, a, :].indirect(offsets[:]))
 
         def quantise_x(half):
             for a in range(PASSES):
@@ -167,16 +160,13 @@ def tile_list_tgn_mguP_kernel(
                 nc.vector.quantize_mx(out=x_codes[half][:, a, :].bitcast(FP8X4), scales=x_sc[half][:, a, :],
                                       in_=rounded[:].rearrange("p c i -> p (c i)"))
 
-        planes_of = {0: {"uz": keep.tile([P, PASSES, PASS], U8, name="uz_sc0", align_bytes=64)[:],
-                         "un": keep.tile([P, PASSES, PASS], U8, name="un_sc0", align_bytes=64)[:],
-                         "w": keep.tile([P, PASS], U8, name="w_sc0", align_bytes=64)[:]}}
+        planes_of = {0: [keep.tile([P, PASSES, PASS], U8, name="first_sc%d" % n, align_bytes=64)[:] for n in range(2)]}
         dealt = {}
         for n, name in enumerate(("uz", "un")):
-            deal(planes_of[0][name], u_sc_raw[n][:, :, 0:PASS], LINE)
+            deal(planes_of[0][n], u_sc_raw[n][:, :, 0:PASS], LINE)
             dealt[name, 0] = deal_words(first_raw[name], name + "0", name + "0")
         for half in range(HALVES):
             quantise_x(half)
-        deal(planes_of[0]["w"], w_sc_raw[:, 0:PASS], LINE)
         for name in ("wz", "wn"):
             dealt[name, 0] = deal_words(first_raw[name], name + "0", name + "0")
 
@@ -187,14 +177,14 @@ def tile_list_tgn_mguP_kernel(
             def with_x(bank, name, n, opens):
                 for a in range(PASSES):
                     nc.tensor.matmul_mx(out=bank[:], lhsT=dealt[name, g][:, a, cols].bitcast(FP8X4),
-                                        lhsT_scale=planes_of[g]["w"][QUADS * (PASSES * n + a) : P, cols],
+                                        lhsT_scale=planes_of[g][n][QUADS:P, a, cols],
                                         rhs=x_codes[half][:, a, :].bitcast(FP8X4), rhs_scale=x_sc[half][:, a, :],
                                         start=opens and a == 0, stop=a == PASSES - 1)
 
-            def with_v(bank, name, closes):
+            def with_v(bank, name, n, closes):
                 for a in range(PASSES):
                     nc.tensor.matmul_mx(out=bank[:], lhsT=dealt[name, g][:, a, cols].bitcast(FP8X4),
-                                        lhsT_scale=planes_of[g][name][:, a, cols],
+                                        lhsT_scale=planes_of[g][n][:, a, cols],
                                         rhs=v_codes[:, a, 2 * COLS * half : 2 * COLS * (half + 1)].bitcast(FP4X4),
                                         rhs_scale=v_sc[:, a, COLS * half : COLS * (half + 1)],
                                         start=a == 0, stop=closes and a == PASSES - 1)
@@ -202,11 +192,13 @@ def tile_list_tgn_mguP_kernel(
             sz = psum.tile([P, COLS], F32, name="sz", tag="sz", bufs=2)
             hn = psum.tile([P, COLS], F32, name="hn", tag="hn", bufs=3)
             xn = psum.tile([P, COLS], F32, name="xn", tag="xn", bufs=3)
-            with_v(sz, "uz", False)
+            with_v(sz, "uz", 0, False)
+            with_v(hn, "un", 1, True)
             with_x(sz, "wz", 0, False)
-            with_v(hn, "un", True)
             with_x(xn, "wn", 1, True)
             return sz, hn, xn
+
+        spare = {}
 
         def gate(k):
             g, t = TILES[k]
@@ -221,8 +213,8 @@ def tile_list_tgn_mguP_kernel(
 
         def candidate(k, stay, banks):
             g, t = TILES[k]
-            gated = work_tile(F32, "gated")
-            cand = ring.tile([P, J], F32, name="cand", tag="cand", bufs=3)
+            cand = ring.tile([P, J], F32, name="cand", tag="cand", bufs=4)
+            gated = spare.get(k, cand)
             for half, (hn, xn) in enumerate(banks):
                 cols = slice(COLS * half, COLS * (half + 1))
                 nc.vector.scalar_tensor_tensor(gated[:, cols], stay[:, cols], 1.0, hn[:], ALU.subtract, ALU.mult)
@@ -232,24 +224,32 @@ def tile_list_tgn_mguP_kernel(
             nc.scalar.activation(cand[:], cand[:], ACT.Tanh, bias=bn_sb[:, g, t : t + 1])
             return cand
 
-        def blend(k, stay, cand):
-            rows = work_tile(F32, "rows")
+        def gather(k, cand):
+            both = work_tile(F32, "rows")
+            if k > 0:
+                spare[k + 2] = both[:, J : 2 * J]
+            nc.vector.tensor_tensor(both[:, 0:J], state[k][:].indirect(offsets[:]), cand[:], ALU.subtract)
+            return both[:, 0:J]
+
+        def blend(k, rows, stay, cand):
             mid = ring.tile([P, J], F32, name="mid", tag="mid", bufs=1)
-            nc.vector.tensor_tensor(rows[:], state[k][:].indirect(offsets[:]), cand[:], ALU.subtract)
-            nc.gpsimd.tensor_tensor(mid[:], rows[:], stay[:], ALU.mult)
+            nc.gpsimd.tensor_tensor(mid[:], rows, stay[:], ALU.mult)
+            nc.gpsimd.tensor_tensor(mid[:], mid[:], cand[:], ALU.add)
+            return mid
+
+        def weigh(k, rows, mid):
             if k == LAST:
-                nc.gpsimd.tensor_tensor(rows[:], mid[:], cand[:], ALU.add)
-            else:
-                nc.gpsimd.tensor_tensor(mid[:], mid[:], cand[:], ALU.add)
-                nc.gpsimd.tensor_tensor(rows[:], mid[:], wgo_sb[:], ALU.mult)
+                return mid[:]
+            engine = nc.vector if k == 0 else nc.gpsimd
+            engine.tensor_tensor(rows, mid[:], wgo_sb[:], ALU.mult)
             return rows
 
         def scatter(k, rows):
             window = pages[k % PAGES][:].indirect(offsets[:])
             if k == LAST:
-                nc.vector.tensor_tensor(window, rows[:], wgo_sb[:], ALU.mult)
+                nc.vector.tensor_tensor(window, rows, wgo_sb[:], ALU.mult)
             else:
-                nc.vector.tensor_copy(window, rows[:])
+                nc.vector.tensor_copy(window, rows)
 
         woven = {}
 
@@ -265,42 +265,50 @@ def tile_list_tgn_mguP_kernel(
                 else:
                     nc.scalar.copy(woven[g, c][:, :, t], page[:, COLS * c : COLS * (c + 1)])
 
-        def quantise_out(g, y_sc, chunks):
+        def quantise_out(g, y_sc, chunks, pieces):
             codes = big([P, T], U32, "y_codes")
-            for c in chunks:
+            for n, c in enumerate(chunks):
                 cols = slice(COLS * c, COLS * (c + 1))
-                nc.vector.quantize_mx(out=codes[:, cols].bitcast(FP8X4), scales=y_sc[:, cols],
+                nc.vector.quantize_mx(out=codes[:, cols].bitcast(FP8X4), scales=y_sc[:, g, cols],
                                       in_=woven[g, c][:].rearrange("p c t -> p (c t)"))
-                words = out_1[g].rearrange("p t b -> p (t b)")[:, PACK * COLS * c : PACK * COLS * (c + 1)]
-                nc.sync.dma_start(words.bitcast(I32), codes[:, cols].bitcast(I32))
-            for r in range(QUADS):
-                nc.sync.dma_start(out_2[g, r : QUADS * QUADS : QUADS, :].bitcast(I32), y_sc[r:P:QUAD, :].bitcast(I32))
+                if (n + 1) % pieces == 0:
+                    first = COLS * (c + 1 - pieces)
+                    words = out_1[g].rearrange("p t b -> p (t b)")[:, PACK * first : PACK * cols.stop]
+                    nc.sync.dma_start(words.bitcast(I32), codes[:, first : cols.stop].bitcast(I32))
 
         gates, cands, blended = {0: gate(0)}, {}, {}
-        for i in range(len(TILES) + LAG):
-            if i >= LAG:
-                scatter(i - LAG, blended[i - LAG])
+        second_sc = keep.tile([P, 2 * PASSES, PASS], U8, name="second_sc", align_bytes=64)
+        planes_of[1] = [second_sc[:, PASSES * n : PASSES * (n + 1), :] for n in range(2)]
+        for n in range(2):
+            deal(planes_of[1][n], u_sc_raw[n][:, :, PASS:N], LINE)
+        cands[0] = candidate(0, *gates[0])
+        for name in words_of:
+            dealt[name, 1] = deal_words(second_raw[name], name + "1", "raw_" + name)
+        gates[1] = gate(1)
+        rows = {0: gather(0, cands[0])}
+        mid = blend(0, rows[0], gates[0][0], cands[0])
+        early = keep.tile([P, 2 * J], F32, name="early", tag="state0", align_bytes=64)
+        spare[1], spare[2] = early[:, 0:J], early[:, J : 2 * J]
+        for k in (1, 2):
+            cands[k] = candidate(k, *gates[k])
+            gates[k + 1] = gate(k + 1)
+        for i in range(1, len(TILES) + 1):
             if i <= LAST:
-                cands[i] = candidate(i, *gates[i])
-            if i == 0:
-                for name in words_of:
-                    dealt[name, 1] = deal_words(second_raw[name], name + "1", "raw_" + name)
-                blended[0] = blend(0, gates[0][0], cands[0])
-            if 2 <= i <= LAST + 1:
-                blended[i - 1] = blend(i - 1, gates[i - 1][0], cands[i - 1])
-            if i == PACK - 2:
-                second_sc = keep.tile([P, 2 * PASSES + 1, PASS], U8, name="second_sc", tag="state0", align_bytes=64)
-                planes_of[1] = {"uz": second_sc[:, 0:PASSES, :], "un": second_sc[:, PASSES : 2 * PASSES, :],
-                                "w": second_sc[:, 2 * PASSES, :]}
-                deal(planes_of[1]["uz"], u_sc_raw[0][:, :, PASS:N], LINE)
-                deal(planes_of[1]["un"], u_sc_raw[1][:, :, PASS:N], LINE)
-                deal(planes_of[1]["w"], w_sc_raw[:, PASS:N], LINE)
-            if i < LAST:
-                gates[i + 1] = gate(i + 1)
-            if i >= LAG:
-                hand_out(i - LAG)
+                rows[i] = gather(i, cands[i])
+            if i == 1:
+                blended[0] = weigh(0, rows[0], mid)
+            if i <= LAST:
+                blended[i] = weigh(i, rows[i], blend(i, rows[i], gates[i][0], cands[i]))
+            scatter(i - 1, blended[i - 1])
+            if i + 2 <= LAST:
+                cands[i + 2] = candidate(i + 2, *gates[i + 2])
+            if i + 3 <= LAST:
+                gates[i + 3] = gate(i + 3)
+            hand_out(i - 1)
 
-        y_sc0 = keep.tile([P, T], U8, name="y_sc0", tag="wgo", align_bytes=64)
-        y_sc1 = keep.tile([P, T], U8, name="y_sc1", align_bytes=64)
-        quantise_out(0, y_sc0, range(CHUNKS))
-        quantise_out(1, y_sc1, [VECTOR_CHUNK] + list(range(VECTOR_CHUNK)))
+        y_sc = keep.tile([P, GROUPS, T], U8, name="y_sc", tag="wgo", align_bytes=64)
+        quantise_out(0, y_sc, range(CHUNKS), PIECES)
+        quantise_out(1, y_sc, [VECTOR_CHUNK] + list(range(VECTOR_CHUNK)), 1)
+        for r in range(QUADS):
+            nc.sync.dma_start(out_2[:, r : QUADS * QUADS : QUADS, :].rearrange("g q t -> q g t").bitcast(I32),
+                              y_sc[r:P:QUAD, :, :].bitcast(I32))

@@ -34,6 +34,7 @@ LAG = 3
 ENGINES = ["GGV"] + ["GGG"] * 6 + ["GGF"]
 SPLIT = 512
 PIECES = 1
+ON_VECTOR = (0, 6)
 VECTOR_CHUNK = CHUNKS - 1
 
 
@@ -202,7 +203,7 @@ def tile_list_tgn_mguP_kernel(
 
         def gate(k):
             g, t = TILES[k]
-            stay = ring.tile([P, J], F32, name="stay", tag="stay", bufs=4, align_bytes=64)
+            stay = ring.tile([P, J], F32, name="stay", tag="stay", bufs=3, align_bytes=64)
             banks = []
             for half in range(HALVES):
                 sz, hn, xn = products(k, half)
@@ -221,7 +222,7 @@ def tile_list_tgn_mguP_kernel(
             for half, (hn, xn) in enumerate(banks):
                 cols = slice(COLS * half, COLS * (half + 1))
                 nc.vector.scalar_tensor_tensor(cand[:, cols], gated[:, cols], -1.0, xn[:], ALU.mult, ALU.add)
-            nc.scalar.activation(cand[:], cand[:], ACT.Tanh, bias=bn_sb[:, g, t : t + 1])
+                nc.scalar.activation(cand[:, cols], cand[:, cols], ACT.Tanh, bias=bn_sb[:, g, t : t + 1])
             return cand
 
         def gather(k, cand):
@@ -240,7 +241,7 @@ def tile_list_tgn_mguP_kernel(
         def weigh(k, rows, mid):
             if k == LAST:
                 return mid[:]
-            engine = nc.vector if k == 0 else nc.gpsimd
+            engine = nc.vector if k in ON_VECTOR else nc.gpsimd
             engine.tensor_tensor(rows, mid[:], wgo_sb[:], ALU.mult)
             return rows
 
@@ -295,13 +296,15 @@ def tile_list_tgn_mguP_kernel(
         for i in range(1, len(TILES) + 1):
             if i <= LAST:
                 rows[i] = gather(i, cands[i])
-            if i == 1:
-                blended[0] = weigh(0, rows[0], mid)
+            if i - 1 in ON_VECTOR:
+                blended[i - 1] = weigh(i - 1, rows[i - 1], mid)
             if i <= LAST:
-                blended[i] = weigh(i, rows[i], blend(i, rows[i], gates[i][0], cands[i]))
-            scatter(i - 1, blended[i - 1])
+                mid = blend(i, rows[i], gates[i][0], cands[i])
+                if i not in ON_VECTOR:
+                    blended[i] = weigh(i, rows[i], mid)
             if i + 2 <= LAST:
                 cands[i + 2] = candidate(i + 2, *gates[i + 2])
+            scatter(i - 1, blended[i - 1])
             if i + 3 <= LAST:
                 gates[i + 3] = gate(i + 3)
             hand_out(i - 1)

@@ -1,6 +1,7 @@
 from contextlib import ExitStack
 
 import concourse.mybir as mybir
+from concourse.masks import make_identity
 
 K, M, N, T, J = 1024, 1024, 1024, 2048, 1024
 FLOPS = 2 * (2 * K + 2 * M) * N * J
@@ -23,19 +24,15 @@ COLS = 512
 QUADS = 4
 QUAD = 32
 PASSES = K // PASS
-GROUPS = N // PASS
 HALVES = J // COLS
-CHUNKS = T // COLS
+TILES = N // P
+LAST = TILES - 1
 LINE = 16
 PAGES = 3
-TILES = [(g, t) for g in range(GROUPS) for t in (2, 0, 1, 3)]
-LAST = len(TILES) - 1
-LAG = 3
-ENGINES = ["GGV"] + ["GGG"] * 6 + ["GGF"]
-SPLIT = 512
-PIECES = 1
 ON_VECTOR = (0, 6)
-VECTOR_CHUNK = CHUNKS - 1
+SLOTS = 4
+EARLY = 768
+WEIGHT_CUTS = (0, 256, 512, 1024)
 
 
 def tile_list_tgn_mguP_kernel(
@@ -54,179 +51,189 @@ def tile_list_tgn_mguP_kernel(
         def woven_tile(name):
             return ring.tile([P, COLS, PACK], BF16, name=name, tag="woven", bufs=8, align_bytes=64)
 
-        def work_tile(dtype, name):
-            return ring.tile([P, 2 * J], dtype, name=name, tag="work", bufs=2, align_bytes=64)
+        def bank(tag):
+            return psum.tile([P, COLS], F32, name=tag, tag=tag, bufs=2 if tag == "sz" else 3)
 
         offsets = keep.tile([P, J // 16], U16, name="offsets")
         nc.sync.dma_start(offsets[:], offs)
 
         tab_sc = keep.tile([P, PASSES, T], U8, name="tab_sc", align_bytes=64)
-        u_sc_raw = [keep.tile([P, PASSES, N], U8, name="u_sc_raw%d" % n, align_bytes=64) for n in range(2)]
-        nc.gpsimd.memset(tab_sc[:].rearrange("p a t -> p (a t)").bitcast(I32), 0)
-        for raw in u_sc_raw:
-            nc.vector.memset(raw[:].rearrange("p a t -> p (a t)").bitcast(I32), 0)
-
-        bz_sb = keep.tile([P, GROUPS, PACK], F32, name="bz_sb")
-        bn_sb = keep.tile([P, GROUPS, PACK], F32, name="bn_sb")
-        x_codes = [keep.tile([P, PASSES, COLS], U32, name="x_codes%d" % half, align_bytes=64) for half in range(HALVES)]
-        x_sc = [keep.tile([P, PASSES, COLS], U8, name="x_sc%d" % half, align_bytes=64) for half in range(HALVES)]
+        planes = [keep.tile([P, PASSES, N], U8, name="planes%d" % n, align_bytes=64) for n in range(2)]
+        for tile in [tab_sc] + planes:
+            nc.vector.memset(tile[:].rearrange("p a t -> p (a t)").bitcast(I32), 0)
+        bias_rows = keep.tile([P, P], F32, name="bias_rows")
+        nc.gpsimd.memset(bias_rows[:], 0.0)
+        identity = keep.tile([P, P], F32, name="identity")
+        make_identity(nc, identity[:])
 
         def load_x(a, half):
-            raw = big([P, PACK, COLS], F32, "x_raw")
+            if a + half == 2:
+                raw = keep.tile([P, PACK, COLS], F32, name="x_raw", tag="last_x", align_bytes=64)
+            else:
+                raw = big([P, PACK, COLS], F32, "x_raw")
             rows = x[PASS * a : PASS * (a + 1), COLS * half : COLS * (half + 1)]
             nc.sync.dma_start(raw[:], rows.rearrange("(p i) c -> p i c", i=PACK))
             return raw
 
-        def load_planes(dst, scales, first, queue):
+        def load_planes(dst, scales, first):
             for r in range(QUADS):
-                queue.dma_start(dst[first + r : P : QUAD, :, :].bitcast(I32),
+                nc.sync.dma_start(dst[first + r : P : QUAD, :, :].bitcast(I32),
                                   scales[:, r : QUADS * QUADS : QUADS, :].rearrange("a q t -> q a t").bitcast(I32))
 
-        def load_words(raw, words, g):
-            columns = words.rearrange("a p n i -> p a (n i)")[:, :, PACK * PASS * g : PACK * PASS * (g + 1)]
-            nc.sync.dma_start(raw[:], columns.bitcast(I32))
-            return raw
+        words_of = {"uz": uz_words, "un": un_words, "wz": wz_words, "wn": wn_words}
+        weights = {}
 
-        def load_first_words(name):
-            raw = keep.tile([P, PASSES, PASS], I32, name="first_raw", tag="raw_" + name, align_bytes=64)
-            return load_words(raw, words_of[name], 0)
+        def load_words(name, piece):
+            lo, hi = WEIGHT_CUTS[piece], WEIGHT_CUTS[piece + 1]
+            tile = keep.tile([P, PASSES, hi - lo], I32, name="%s%d" % (name, piece), align_bytes=64)
+            columns = words_of[name].rearrange("a p n i -> p a (n i)")[:, :, PACK * lo : PACK * hi]
+            nc.sync.dma_start(tile[:], columns.bitcast(I32))
+            for k in range(lo // P, hi // P):
+                weights[name, k] = tile[:, :, P * k - lo : P * (k + 1) - lo]
 
-        def load_state(k, rows):
-            g, t = TILES[k]
-            nc.sync.dma_start(rows[:], hT.rearrange("(g p t) c -> g t p c", p=P, t=PACK)[g, t])
+        def load_state(k):
+            if k == 0:
+                rows = keep.tile([P, T], F32, name="state0", tag="state0", align_bytes=64)
+            else:
+                rows = big([P, T], F32, "state")
+            nc.sync.dma_start(rows[:], hT[P * k : P * (k + 1), :])
             return rows
 
-        def deal(dst, src, run):
-            lead = "p a" if len(src.shape) == 3 else "p"
-            nc.vector.tensor_copy(dst.rearrange("%s (t c i) -> %s c t i" % (lead, lead), t=PACK, i=run),
-                                  src.rearrange("%s (c i t) -> %s c t i" % (lead, lead), t=PACK, i=run))
-
-        def deal_words(raw, name, tag):
-            dealt = keep.tile([P, PASSES, PASS], I32, name=name, tag=tag, align_bytes=64)
-            deal(dealt[:], raw[:], LINE // 4)
-            return dealt
-
-        words_of = {"uz": uz_words, "wz": wz_words, "un": un_words, "wn": wn_words}
         tab_w = big([P, T], I32, "tab_w")
         tab_rows = tab_words[0].rearrange("p t b -> p (t b)").bitcast(I32)
-        for c in range(CHUNKS):
-            nc.sync.dma_start(tab_w[:, COLS * c : COLS * (c + 1)], tab_rows[:, COLS * c : COLS * (c + 1)])
-        wgo_sb = keep.tile([P, J], F32, name="wgo_sb", tag="wgo", align_bytes=64)
-        x_raw, first_raw = {}, {}
+        for c in range(2):
+            nc.sync.dma_start(tab_w[:, J * c : J * (c + 1)], tab_rows[:, J * c : J * (c + 1)])
+        x_raw, state = {}, {}
         x_raw[0, 0] = load_x(0, 0)
-        nc.sync.dma_start(bz_sb[:], bz.rearrange("(g p t) -> p g t", p=P, t=PACK))
-        nc.sync.dma_start(bn_sb[:], bn.rearrange("(g p t) -> p g t", p=P, t=PACK))
-        load_planes(tab_sc, tab_scales, 0, nc.sync)
+        nc.sync.dma_start(bias_rows[0:TILES, :], bz.rearrange("(k p) -> k p", p=P))
+        nc.sync.dma_start(bias_rows[TILES : 2 * TILES, :], bn.rearrange("(k p) -> k p", p=P))
+        load_planes(tab_sc, tab_scales, 0)
         x_raw[1, 0] = load_x(1, 0)
+        load_planes(planes[0], uz_scales, 0)
+        load_words("uz", 0)
+        load_words("un", 0)
+        load_planes(planes[1], un_scales, 0)
+        load_words("wz", 0)
+        load_words("wn", 0)
+        load_planes(planes[0], wz_scales, QUADS)
         x_raw[0, 1] = load_x(0, 1)
-        load_planes(u_sc_raw[0], uz_scales, 0, nc.sync)
-        first_raw["uz"] = load_first_words("uz")
-        load_planes(u_sc_raw[0], wz_scales, QUADS, nc.sync)
-        first_raw["un"] = load_first_words("un")
-        load_planes(u_sc_raw[1], un_scales, 0, nc.sync)
+        load_planes(planes[1], wn_scales, QUADS)
         x_raw[1, 1] = load_x(1, 1)
-        load_planes(u_sc_raw[1], wn_scales, QUADS, nc.sync)
-        first_raw["wz"] = load_first_words("wz")
-        first_raw["wn"] = load_first_words("wn")
-        second_raw = {name: load_words(ring.tile([P, PASSES, PASS], I32, name="second_raw", tag="second", bufs=4,
-                                                 align_bytes=64), words, 1)
-                      for name, words in words_of.items()}
-        state = {0: load_state(0, keep.tile([P, T], F32, name="state0", tag="state0", align_bytes=64))}
-        state[1] = load_state(1, big([P, T], F32, "state"))
+        state[0] = load_state(0)
+        for name in words_of:
+            load_words(name, 1)
+        state[1] = load_state(1)
+        wgo_sb = keep.tile([P, J], F32, name="wgo_sb", tag="wgo", align_bytes=64)
         nc.sync.dma_start(wgo_sb[:], wgo)
-        for k in range(2, len(TILES)):
-            state[k] = load_state(k, big([P, T], F32, "state"))
+        for name in words_of:
+            load_words(name, 2)
+        for k in range(2, TILES):
+            state[k] = load_state(k)
 
-        pages = [keep.tile([P, T], F32, name="page%d" % n, align_bytes=64) for n in range(PAGES)]
-        for page in pages:
-            (nc.vector if page is pages[0] else nc.gpsimd).memset(page[:], 0.0)
+        turned_bias = bank("sz")
+        nc.tensor.transpose(turned_bias[:, 0:P], bias_rows[:], identity[:])
+        bias = keep.tile([P, TILES], F32, name="bias")
+        bz_neg = keep.tile([P, TILES], F32, name="bz_neg")
+        nc.scalar.copy(bias[:], turned_bias[:, TILES : 2 * TILES])
+        nc.scalar.activation(bz_neg[:], turned_bias[:, 0:TILES], ACT.Copy, scale=-1.0)
 
-        bz_neg = keep.tile([P, GROUPS, PACK], F32, name="bz_neg")
-        nc.scalar.activation(bz_neg[:], bz_sb[:], ACT.Copy, scale=-1.0)
+        v_codes, v_sc, x_codes, x_sc = {}, {}, {}, {}
 
-        picked = work_tile(U32, "picked")[:, 0:J]
-        v_codes = keep.tile([P, PASSES, 2 * J], U8, name="v_codes", align_bytes=64)
-        v_sc = keep.tile([P, PASSES, J], U8, name="v_sc", align_bytes=64)
-        nc.vector.tensor_copy(picked, tab_w[:].bitcast(U32).indirect(offsets[:]))
-        nc.vector.tensor_copy(v_codes[:].bitcast(U16).rearrange("p a (c i) -> p c a i", i=LINE // 2),
-                              picked.bitcast(U16).rearrange("p (c i a) -> p c a i", i=LINE // 2, a=PASSES))
-        for a in range(PASSES):
-            nc.vector.tensor_copy(v_sc[:, a, :], tab_sc[:, a, :].indirect(offsets[:]))
+        def pick_table(half):
+            entries = offsets[:, COLS // 16 * half : COLS // 16 * (half + 1)]
+            picked = keep.tile([P, COLS], U32, name="picked", tag="picked", align_bytes=64)
+            v_codes[half] = keep.tile([P, PASSES, 2 * COLS], U8, name="v_codes%d" % half, align_bytes=64)
+            v_sc[half] = keep.tile([P, PASSES, COLS], U8, name="v_sc%d" % half, align_bytes=64)
+            nc.vector.tensor_copy(picked[:], tab_w[:].bitcast(U32).indirect(entries))
+            for a in range(PASSES):
+                nc.vector.tensor_copy(v_sc[half][:, a, :], tab_sc[:, a, :].indirect(entries))
+            nc.vector.tensor_copy(v_codes[half][:].bitcast(U16).rearrange("p a (c i) -> p c a i", i=LINE // 2),
+                                  picked[:].bitcast(U16).rearrange("p (c i a) -> p c a i", i=LINE // 2, a=PASSES))
+
+        def copy_on(engine, out, in_):
+            if engine is nc.scalar:
+                nc.scalar.copy(out, in_)
+            else:
+                nc.vector.tensor_copy(out, in_)
 
         def quantise_x(half):
+            x_codes[half] = keep.tile([P, PASSES, COLS], U32, name="x_codes%d" % half, align_bytes=64)
+            x_sc[half] = keep.tile([P, PASSES, COLS], U8, name="x_sc%d" % half, align_bytes=64)
             for a in range(PASSES):
-                rounded = woven_tile("x_rounded")
-                nc.scalar.copy(rounded[:].rearrange("p (c n) i -> p c i n", n=LINE // 4),
-                               x_raw[a, half][:].rearrange("p i (c n) -> p c i n", n=LINE // 4))
-                nc.vector.quantize_mx(out=x_codes[half][:, a, :].bitcast(FP8X4), scales=x_sc[half][:, a, :],
-                                      in_=rounded[:].rearrange("p c i -> p (c i)"))
+                last = a + half == 2
+                width = COLS // 2 if last else COLS
+                for n in range(COLS // width):
+                    cols = slice(width * n, width * (n + 1))
+                    if last:
+                        rounded = keep.tile([P, width, PACK], BF16, name="x_last", tag="page%d" % n, align_bytes=64)
+                    else:
+                        rounded = woven_tile("x_rounded")
+                    copy_on(nc.vector if half else nc.scalar,
+                            rounded[:].rearrange("p (c n) i -> p c i n", n=LINE // 4),
+                            x_raw[a, half][:, :, cols].rearrange("p i (c n) -> p c i n", n=LINE // 4))
+                    nc.vector.quantize_mx(out=x_codes[half][:, a, cols].bitcast(FP8X4), scales=x_sc[half][:, a, cols],
+                                          in_=rounded[:].rearrange("p c i -> p (c i)"))
 
-        planes_of = {0: [keep.tile([P, PASSES, PASS], U8, name="first_sc%d" % n, align_bytes=64)[:] for n in range(2)]}
-        dealt = {}
-        for n, name in enumerate(("uz", "un")):
-            deal(planes_of[0][n], u_sc_raw[n][:, :, 0:PASS], LINE)
-            dealt[name, 0] = deal_words(first_raw[name], name + "0", name + "0")
         for half in range(HALVES):
+            pick_table(half)
             quantise_x(half)
-        for name in ("wz", "wn"):
-            dealt[name, 0] = deal_words(first_raw[name], name + "0", name + "0")
+        pages = [keep.tile([P, T], F32, name="page", tag="page%d" % n, align_bytes=64) for n in range(2)]
+        for page in pages:
+            nc.gpsimd.memset(page[:], 0.0)
 
         def products(k, half):
-            g, t = TILES[k]
-            cols = slice(P * t, P * (t + 1))
+            cols = slice(P * k, P * (k + 1))
 
-            def with_x(bank, name, n, opens):
+            def with_x(acc, name, n, opens):
                 for a in range(PASSES):
-                    nc.tensor.matmul_mx(out=bank[:], lhsT=dealt[name, g][:, a, cols].bitcast(FP8X4),
-                                        lhsT_scale=planes_of[g][n][QUADS:P, a, cols],
+                    nc.tensor.matmul_mx(out=acc[:], lhsT=weights[name, k][:, a, :].bitcast(FP8X4),
+                                        lhsT_scale=planes[n][QUADS:P, a, cols],
                                         rhs=x_codes[half][:, a, :].bitcast(FP8X4), rhs_scale=x_sc[half][:, a, :],
                                         start=opens and a == 0, stop=a == PASSES - 1)
 
-            def with_v(bank, name, n, closes):
+            def with_v(acc, name, n, closes):
                 for a in range(PASSES):
-                    nc.tensor.matmul_mx(out=bank[:], lhsT=dealt[name, g][:, a, cols].bitcast(FP8X4),
-                                        lhsT_scale=planes_of[g][n][:, a, cols],
-                                        rhs=v_codes[:, a, 2 * COLS * half : 2 * COLS * (half + 1)].bitcast(FP4X4),
-                                        rhs_scale=v_sc[:, a, COLS * half : COLS * (half + 1)],
+                    nc.tensor.matmul_mx(out=acc[:], lhsT=weights[name, k][:, a, :].bitcast(FP8X4),
+                                        lhsT_scale=planes[n][:, a, cols],
+                                        rhs=v_codes[half][:, a, :].bitcast(FP4X4), rhs_scale=v_sc[half][:, a, :],
                                         start=a == 0, stop=closes and a == PASSES - 1)
 
-            sz = psum.tile([P, COLS], F32, name="sz", tag="sz", bufs=2)
-            hn = psum.tile([P, COLS], F32, name="hn", tag="hn", bufs=3)
-            xn = psum.tile([P, COLS], F32, name="xn", tag="xn", bufs=3)
+            sz, hn, xn = bank("sz"), bank("hn"), bank("xn")
             with_v(sz, "uz", 0, False)
             with_v(hn, "un", 1, True)
             with_x(sz, "wz", 0, False)
             with_x(xn, "wn", 1, True)
             return sz, hn, xn
 
+        def work_tile(name):
+            return ring.tile([P, 2 * J], F32, name=name, tag="work", bufs=2, align_bytes=64)
+
         spare = {}
 
         def gate(k):
-            g, t = TILES[k]
             stay = ring.tile([P, J], F32, name="stay", tag="stay", bufs=3, align_bytes=64)
             banks = []
             for half in range(HALVES):
                 sz, hn, xn = products(k, half)
                 nc.scalar.activation(stay[:, COLS * half : COLS * (half + 1)], sz[:], ACT.Sigmoid,
-                                     bias=bz_neg[:, g, t : t + 1], scale=-1.0)
+                                     bias=bz_neg[:, k : k + 1], scale=-1.0)
                 banks.append((hn, xn))
             return stay, banks
 
         def candidate(k, stay, banks):
-            g, t = TILES[k]
             cand = ring.tile([P, J], F32, name="cand", tag="cand", bufs=4)
-            gated = spare.get(k, cand)
+            gated = spare[k]
             for half, (hn, xn) in enumerate(banks):
                 cols = slice(COLS * half, COLS * (half + 1))
                 nc.vector.scalar_tensor_tensor(gated[:, cols], stay[:, cols], 1.0, hn[:], ALU.subtract, ALU.mult)
             for half, (hn, xn) in enumerate(banks):
                 cols = slice(COLS * half, COLS * (half + 1))
                 nc.vector.scalar_tensor_tensor(cand[:, cols], gated[:, cols], -1.0, xn[:], ALU.mult, ALU.add)
-                nc.scalar.activation(cand[:, cols], cand[:, cols], ACT.Tanh, bias=bn_sb[:, g, t : t + 1])
+                nc.scalar.activation(cand[:, cols], cand[:, cols], ACT.Tanh, bias=bias[:, k : k + 1])
             return cand
 
         def gather(k, cand):
-            both = work_tile(F32, "rows")
+            both = work_tile("rows")
             if k > 0:
                 spare[k + 2] = both[:, J : 2 * J]
             nc.vector.tensor_tensor(both[:, 0:J], state[k][:].indirect(offsets[:]), cand[:], ALU.subtract)
@@ -255,36 +262,48 @@ def tile_list_tgn_mguP_kernel(
         woven = {}
 
         def hand_out(k):
-            g, t = TILES[k]
             page = pages[k % PAGES]
-            nc.sync.dma_start(out_0.rearrange("(g p t) c -> g t p c", p=P, t=PACK)[g, t], page[:])
-            for c in range(CHUNKS):
-                if k % PACK == 0:
-                    woven[g, c] = woven_tile("y_rounded")
-                if k == LAST and c == VECTOR_CHUNK:
-                    nc.vector.tensor_copy(woven[g, c][:, :, t], page[:, COLS * c : COLS * (c + 1)])
-                else:
-                    nc.scalar.copy(woven[g, c][:, :, t], page[:, COLS * c : COLS * (c + 1)])
+            nc.sync.dma_start(out_0[P * k : P * (k + 1), :], page[:])
+            if k == PACK - 1:
+                for c in range(QUADS):
+                    again = big([P, PACK, COLS], F32, "again")
+                    rows = out_0[0:PASS, COLS * c : COLS * (c + 1)]
+                    nc.sync.dma_start(again[:], rows.rearrange("(p i) c -> p i c", i=PACK))
+                    woven[c] = woven_tile("y_rounded")
+                    nc.scalar.copy(woven[c][:].rearrange("p (c n) i -> p c i n", n=LINE // 4),
+                                   again[:].rearrange("p i (c n) -> p c i n", n=LINE // 4))
+            if k < PACK:
+                return
+            woven[k] = woven_tile("y_rounded")
+            words = woven[k][:].rearrange("p c i -> p (c i)").bitcast(F32)
+            rounded = []
+            for c in range(QUADS):
+                turned = bank(("hn", "xn")[c % 2])
+                for q in range(QUADS):
+                    first = COLS * q + P * c
+                    nc.tensor.transpose(turned[:, P * q : P * (q + 1)], page[:, first : first + P], identity[:])
+                rows = ring.tile([P, COLS], BF16, name="rows", tag="rows", bufs=4, align_bytes=64)
+                copy_on(nc.scalar,
+                        rows[:].rearrange("t (u m e) -> t u m e", u=2, e=2),
+                        turned[:].rearrange("t (m u e) -> t u m e", u=2, e=2))
+                rounded.append(rows)
+            for pair in range(2):
+                back = bank("sz")
+                for c in range(2):
+                    for u in range(2):
+                        first = P * (2 * c + u)
+                        nc.tensor.transpose(back[:, first : first + P],
+                                            rounded[2 * pair + c][:].bitcast(F32)[:, P * u : P * (u + 1)], identity[:])
+                copy_on(nc.scalar,
+                        words[:, COLS * pair : COLS * (pair + 1)].rearrange("m (c t u) -> m c t u", c=2, u=2),
+                        back[:].rearrange("m (c u t) -> m c t u", c=2, u=2))
 
-        def quantise_out(g, y_sc, chunks, pieces):
-            codes = big([P, T], U32, "y_codes")
-            for n, c in enumerate(chunks):
-                cols = slice(COLS * c, COLS * (c + 1))
-                nc.vector.quantize_mx(out=codes[:, cols].bitcast(FP8X4), scales=y_sc[:, g, cols],
-                                      in_=woven[g, c][:].rearrange("p c t -> p (c t)"))
-                if (n + 1) % pieces == 0:
-                    first = COLS * (c + 1 - pieces)
-                    words = out_1[g].rearrange("p t b -> p (t b)")[:, PACK * first : PACK * cols.stop]
-                    nc.sync.dma_start(words.bitcast(I32), codes[:, first : cols.stop].bitcast(I32))
-
+        first_gated = keep.tile([P, J], F32, name="first_gated", tag="last_x", align_bytes=64)
+        spare[0] = first_gated[:]
         gates, cands, blended = {0: gate(0)}, {}, {}
-        second_sc = keep.tile([P, 2 * PASSES, PASS], U8, name="second_sc", align_bytes=64)
-        planes_of[1] = [second_sc[:, PASSES * n : PASSES * (n + 1), :] for n in range(2)]
-        for n in range(2):
-            deal(planes_of[1][n], u_sc_raw[n][:, :, PASS:N], LINE)
         cands[0] = candidate(0, *gates[0])
-        for name in words_of:
-            dealt[name, 1] = deal_words(second_raw[name], name + "1", "raw_" + name)
+        pages.append(keep.tile([P, T], F32, name="page", tag="last_x", align_bytes=64))
+        nc.gpsimd.memset(pages[2][:], 0.0)
         gates[1] = gate(1)
         rows = {0: gather(0, cands[0])}
         mid = blend(0, rows[0], gates[0][0], cands[0])
@@ -293,7 +312,7 @@ def tile_list_tgn_mguP_kernel(
         for k in (1, 2):
             cands[k] = candidate(k, *gates[k])
             gates[k + 1] = gate(k + 1)
-        for i in range(1, len(TILES) + 1):
+        for i in range(1, TILES + 1):
             if i <= LAST:
                 rows[i] = gather(i, cands[i])
             if i - 1 in ON_VECTOR:
@@ -309,9 +328,28 @@ def tile_list_tgn_mguP_kernel(
                 gates[i + 3] = gate(i + 3)
             hand_out(i - 1)
 
-        y_sc = keep.tile([P, GROUPS, T], U8, name="y_sc", tag="wgo", align_bytes=64)
-        quantise_out(0, y_sc, range(CHUNKS), PIECES)
-        quantise_out(1, y_sc, [VECTOR_CHUNK] + list(range(VECTOR_CHUNK)), 1)
-        for r in range(QUADS):
-            nc.sync.dma_start(out_2[:, r : QUADS * QUADS : QUADS, :].rearrange("g q t -> q g t").bitcast(I32),
-                              y_sc[r:P:QUAD, :, :].bitcast(I32))
+        y_sc = keep.tile([P, T + COLS], U8, name="y_sc", tag="wgo", align_bytes=64)
+        codes = big([P, T], U32, "y_codes")
+        words = out_1[0].rearrange("p t b -> p (t b)").bitcast(I32)
+        for c in range(QUADS):
+            cols = slice(COLS * c, COLS * (c + 1))
+            nc.vector.quantize_mx(out=codes[:, cols].bitcast(FP8X4), scales=y_sc[:, cols],
+                                  in_=woven[c][:].rearrange("p c i -> p (c i)"))
+        nc.sync.dma_start(words, codes[:].bitcast(I32))
+        for q in range(QUADS):
+            nc.sync.dma_start(out_2[0, QUADS * q : QUADS * (q + 1), :].bitcast(I32),
+                              y_sc[QUAD * q : QUAD * q + QUADS, 0:T].bitcast(I32))
+        codes = big([P, PACK, COLS], U32, "y_codes")
+        words = out_1[1].rearrange("(k p) t b -> p k (t b)", p=QUAD).bitcast(I32)
+        stored = 0
+        for row in range(PACK):
+            nc.vector.quantize_mx(out=codes[:, row, :].bitcast(FP8X4), scales=y_sc[QUADS * row : P, T : T + COLS],
+                                  in_=woven[PACK + row][:].rearrange("p c i -> p (c i)"))
+            if row >= PACK - 2:
+                for q in range(QUADS):
+                    nc.sync.dma_start(words[:, stored : row + 1, COLS * q : COLS * (q + 1)],
+                                      codes[QUAD * q : QUAD * (q + 1), stored : row + 1, :].bitcast(I32))
+                stored = row + 1
+        for q in range(QUADS):
+            nc.sync.dma_start(out_2[1, :, COLS * q : COLS * (q + 1)].bitcast(I32),
+                              y_sc[QUAD * q : QUAD * q + QUADS * PACK, T : T + COLS].bitcast(I32))

@@ -46,7 +46,7 @@ def tile_list_tgn_mguP_kernel(
         psum = ctx.enter_context(tc.psum_pool(name="psum", bufs=2))
 
         def big(shape, dtype, name):
-            return ring.tile(shape, dtype, name=name, tag="big", bufs=5, align_bytes=64)
+            return ring.tile(shape, dtype, name=name, tag="big", bufs=4, align_bytes=64)
 
         def woven_tile(name):
             return ring.tile([P, COLS, PACK], BF16, name=name, tag="woven", bufs=8, align_bytes=64)
@@ -58,17 +58,19 @@ def tile_list_tgn_mguP_kernel(
         nc.sync.dma_start(offsets[:], offs)
 
         tab_sc = keep.tile([P, PASSES, T], U8, name="tab_sc", align_bytes=64)
-        planes = [keep.tile([P, PASSES, N], U8, name="planes%d" % n, align_bytes=64) for n in range(2)]
+        planes = [keep.tile([P, PASSES, N], U8, name="planes%d" % n, align_bytes=64) for n in range(4)]
         for tile in [tab_sc] + planes:
             nc.vector.memset(tile[:].rearrange("p a t -> p (a t)").bitcast(I32), 0)
         bias_rows = keep.tile([P, P], F32, name="bias_rows")
         nc.gpsimd.memset(bias_rows[:], 0.0)
         identity = keep.tile([P, P], F32, name="identity")
         make_identity(nc, identity[:])
+        warm = keep.tile([P, 1], F32, name="warm")
+        nc.scalar.activation(warm[:], identity[:, 0:1], ACT.Sigmoid)
 
         def load_x(a, half):
-            if a + half == 2:
-                raw = keep.tile([P, PACK, COLS], F32, name="x_raw", tag="last_x", align_bytes=64)
+            if half:
+                raw = keep.tile([P, PACK, COLS], F32, name="x_raw", tag=("third_x", "last_x")[a], align_bytes=64)
             else:
                 raw = big([P, PACK, COLS], F32, "x_raw")
             rows = x[PASS * a : PASS * (a + 1), COLS * half : COLS * (half + 1)]
@@ -110,23 +112,23 @@ def tile_list_tgn_mguP_kernel(
         load_planes(tab_sc, tab_scales, 0)
         x_raw[1, 0] = load_x(1, 0)
         load_planes(planes[0], uz_scales, 0)
+        x_raw[0, 1] = load_x(0, 1)
         load_words("uz", 0)
         load_words("un", 0)
         load_planes(planes[1], un_scales, 0)
+        x_raw[1, 1] = load_x(1, 1)
+        load_planes(planes[2], wz_scales, QUADS)
         load_words("wz", 0)
         load_words("wn", 0)
-        load_planes(planes[0], wz_scales, QUADS)
-        x_raw[0, 1] = load_x(0, 1)
-        load_planes(planes[1], wn_scales, QUADS)
-        x_raw[1, 1] = load_x(1, 1)
+        load_planes(planes[3], wn_scales, QUADS)
         state[0] = load_state(0)
         for name in words_of:
             load_words(name, 1)
+        for name in words_of:
+            load_words(name, 2)
         state[1] = load_state(1)
         wgo_sb = keep.tile([P, J], F32, name="wgo_sb", tag="wgo", align_bytes=64)
         nc.sync.dma_start(wgo_sb[:], wgo)
-        for name in words_of:
-            load_words(name, 2)
         for k in range(2, TILES):
             state[k] = load_state(k)
 
@@ -168,7 +170,7 @@ def tile_list_tgn_mguP_kernel(
                         rounded = keep.tile([P, width, PACK], BF16, name="x_last", tag="page%d" % n, align_bytes=64)
                     else:
                         rounded = woven_tile("x_rounded")
-                    copy_on(nc.vector if half else nc.scalar,
+                    copy_on(nc.vector if last else nc.scalar,
                             rounded[:].rearrange("p (c n) i -> p c i n", n=LINE // 4),
                             x_raw[a, half][:, :, cols].rearrange("p i (c n) -> p c i n", n=LINE // 4))
                     nc.vector.quantize_mx(out=x_codes[half][:, a, cols].bitcast(FP8X4), scales=x_sc[half][:, a, cols],
@@ -187,7 +189,7 @@ def tile_list_tgn_mguP_kernel(
             def with_x(acc, name, n, opens):
                 for a in range(PASSES):
                     nc.tensor.matmul_mx(out=acc[:], lhsT=weights[name, k][:, a, :].bitcast(FP8X4),
-                                        lhsT_scale=planes[n][QUADS:P, a, cols],
+                                        lhsT_scale=planes[2 + n][QUADS:P, a, cols],
                                         rhs=x_codes[half][:, a, :].bitcast(FP8X4), rhs_scale=x_sc[half][:, a, :],
                                         start=opens and a == 0, stop=a == PASSES - 1)
 
@@ -211,7 +213,10 @@ def tile_list_tgn_mguP_kernel(
         spare = {}
 
         def gate(k):
-            stay = ring.tile([P, J], F32, name="stay", tag="stay", bufs=3, align_bytes=64)
+            if k == 0:
+                stay = keep.tile([P, J], F32, name="stay", tag="third_x", align_bytes=64)
+            else:
+                stay = ring.tile([P, J], F32, name="stay", tag="stay", bufs=3, align_bytes=64)
             banks = []
             for half in range(HALVES):
                 sz, hn, xn = products(k, half)

@@ -29,10 +29,8 @@ TILES = N // P
 LAST = TILES - 1
 LINE = 16
 PAGES = 3
-ON_VECTOR = (0, 6)
-SLOTS = 4
-EARLY = 768
-WEIGHT_CUTS = (0, 256, 512, 1024)
+ON_VECTOR = (0,)
+WEIGHT_CUTS = (0, 2 * P, 4 * P, N)
 
 
 def tile_list_tgn_mguP_kernel(
@@ -134,9 +132,9 @@ def tile_list_tgn_mguP_kernel(
 
         turned_bias = bank("sz")
         nc.tensor.transpose(turned_bias[:, 0:P], bias_rows[:], identity[:])
-        bias = keep.tile([P, TILES], F32, name="bias")
+        bn_sb = keep.tile([P, TILES], F32, name="bias")
         bz_neg = keep.tile([P, TILES], F32, name="bz_neg")
-        nc.scalar.copy(bias[:], turned_bias[:, TILES : 2 * TILES])
+        nc.scalar.copy(bn_sb[:], turned_bias[:, TILES : 2 * TILES])
         nc.scalar.activation(bz_neg[:], turned_bias[:, 0:TILES], ACT.Copy, scale=-1.0)
 
         v_codes, v_sc, x_codes, x_sc = {}, {}, {}, {}
@@ -152,34 +150,28 @@ def tile_list_tgn_mguP_kernel(
             nc.vector.tensor_copy(v_codes[half][:].bitcast(U16).rearrange("p a (c i) -> p c a i", i=LINE // 2),
                                   picked[:].bitcast(U16).rearrange("p (c i a) -> p c a i", i=LINE // 2, a=PASSES))
 
-        def copy_on(engine, out, in_):
-            if engine is nc.scalar:
-                nc.scalar.copy(out, in_)
-            else:
-                nc.vector.tensor_copy(out, in_)
-
         def quantise_x(half):
             x_codes[half] = keep.tile([P, PASSES, COLS], U32, name="x_codes%d" % half, align_bytes=64)
             x_sc[half] = keep.tile([P, PASSES, COLS], U8, name="x_sc%d" % half, align_bytes=64)
             for a in range(PASSES):
-                last = a + half == 2
+                last = a == PASSES - 1 and half == HALVES - 1
                 width = COLS // 2 if last else COLS
+                copy = nc.vector.tensor_copy if last else nc.scalar.copy
                 for n in range(COLS // width):
                     cols = slice(width * n, width * (n + 1))
                     if last:
                         rounded = keep.tile([P, width, PACK], BF16, name="x_last", tag="page%d" % n, align_bytes=64)
                     else:
                         rounded = woven_tile("x_rounded")
-                    copy_on(nc.vector if last else nc.scalar,
-                            rounded[:].rearrange("p (c n) i -> p c i n", n=LINE // 4),
-                            x_raw[a, half][:, :, cols].rearrange("p i (c n) -> p c i n", n=LINE // 4))
+                    copy(rounded[:].rearrange("p (c n) i -> p c i n", n=LINE // 4),
+                         x_raw[a, half][:, :, cols].rearrange("p i (c n) -> p c i n", n=LINE // 4))
                     nc.vector.quantize_mx(out=x_codes[half][:, a, cols].bitcast(FP8X4), scales=x_sc[half][:, a, cols],
                                           in_=rounded[:].rearrange("p c i -> p (c i)"))
 
         for half in range(HALVES):
             pick_table(half)
             quantise_x(half)
-        pages = [keep.tile([P, T], F32, name="page", tag="page%d" % n, align_bytes=64) for n in range(2)]
+        pages = [keep.tile([P, T], F32, name="page", tag="page%d" % n, align_bytes=64) for n in range(PAGES - 1)]
         for page in pages:
             nc.gpsimd.memset(page[:], 0.0)
 
@@ -207,9 +199,6 @@ def tile_list_tgn_mguP_kernel(
             with_x(xn, "wn", 1, True)
             return sz, hn, xn
 
-        def work_tile(name):
-            return ring.tile([P, 2 * J], F32, name=name, tag="work", bufs=2, align_bytes=64)
-
         spare = {}
 
         def gate(k):
@@ -234,17 +223,17 @@ def tile_list_tgn_mguP_kernel(
             for half, (hn, xn) in enumerate(banks):
                 cols = slice(COLS * half, COLS * (half + 1))
                 nc.vector.scalar_tensor_tensor(cand[:, cols], gated[:, cols], -1.0, xn[:], ALU.mult, ALU.add)
-                nc.scalar.activation(cand[:, cols], cand[:, cols], ACT.Tanh, bias=bias[:, k : k + 1])
+                nc.scalar.activation(cand[:, cols], cand[:, cols], ACT.Tanh, bias=bn_sb[:, k : k + 1])
             return cand
 
         def gather(k, cand):
-            both = work_tile("rows")
+            both = ring.tile([P, 2 * J], F32, name="rows", tag="work", bufs=2, align_bytes=64)
             if k > 0:
                 spare[k + 2] = both[:, J : 2 * J]
             nc.vector.tensor_tensor(both[:, 0:J], state[k][:].indirect(offsets[:]), cand[:], ALU.subtract)
             return both[:, 0:J]
 
-        def blend(k, rows, stay, cand):
+        def blend(rows, stay, cand):
             mid = ring.tile([P, J], F32, name="mid", tag="mid", bufs=1)
             nc.gpsimd.tensor_tensor(mid[:], rows, stay[:], ALU.mult)
             nc.gpsimd.tensor_tensor(mid[:], mid[:], cand[:], ALU.add)
@@ -266,19 +255,16 @@ def tile_list_tgn_mguP_kernel(
 
         woven = {}
 
-        def hand_out(k):
-            page = pages[k % PAGES]
-            nc.sync.dma_start(out_0[P * k : P * (k + 1), :], page[:])
-            if k == PACK - 1:
-                for c in range(QUADS):
-                    again = big([P, PACK, COLS], F32, "again")
-                    rows = out_0[0:PASS, COLS * c : COLS * (c + 1)]
-                    nc.sync.dma_start(again[:], rows.rearrange("(p i) c -> p i c", i=PACK))
-                    woven[c] = woven_tile("y_rounded")
-                    nc.scalar.copy(woven[c][:].rearrange("p (c n) i -> p c i n", n=LINE // 4),
-                                   again[:].rearrange("p i (c n) -> p c i n", n=LINE // 4))
-            if k < PACK:
-                return
+        def read_back():
+            for c in range(QUADS):
+                again = big([P, PACK, COLS], F32, "again")
+                rows = out_0[0:PASS, COLS * c : COLS * (c + 1)]
+                nc.sync.dma_start(again[:], rows.rearrange("(p i) c -> p i c", i=PACK))
+                woven[c] = woven_tile("y_rounded")
+                nc.scalar.copy(woven[c][:].rearrange("p (c n) i -> p c i n", n=LINE // 4),
+                               again[:].rearrange("p i (c n) -> p c i n", n=LINE // 4))
+
+        def turn_twice(k, page):
             woven[k] = woven_tile("y_rounded")
             words = woven[k][:].rearrange("p c i -> p (c i)").bitcast(F32)
             rounded = []
@@ -287,10 +273,9 @@ def tile_list_tgn_mguP_kernel(
                 for q in range(QUADS):
                     first = COLS * q + P * c
                     nc.tensor.transpose(turned[:, P * q : P * (q + 1)], page[:, first : first + P], identity[:])
-                rows = ring.tile([P, COLS], BF16, name="rows", tag="rows", bufs=4, align_bytes=64)
-                copy_on(nc.scalar,
-                        rows[:].rearrange("t (u m e) -> t u m e", u=2, e=2),
-                        turned[:].rearrange("t (m u e) -> t u m e", u=2, e=2))
+                rows = ring.tile([P, COLS], BF16, name="rows", tag="rows", bufs=QUADS, align_bytes=64)
+                nc.scalar.copy(rows[:].rearrange("t (u m e) -> t u m e", u=2, e=2),
+                               turned[:].rearrange("t (m u e) -> t u m e", u=2, e=2))
                 rounded.append(rows)
             for pair in range(2):
                 back = bank("sz")
@@ -299,19 +284,26 @@ def tile_list_tgn_mguP_kernel(
                         first = P * (2 * c + u)
                         nc.tensor.transpose(back[:, first : first + P],
                                             rounded[2 * pair + c][:].bitcast(F32)[:, P * u : P * (u + 1)], identity[:])
-                copy_on(nc.scalar,
-                        words[:, COLS * pair : COLS * (pair + 1)].rearrange("m (c t u) -> m c t u", c=2, u=2),
-                        back[:].rearrange("m (c u t) -> m c t u", c=2, u=2))
+                nc.scalar.copy(words[:, COLS * pair : COLS * (pair + 1)].rearrange("m (c t u) -> m c t u", c=2, u=2),
+                               back[:].rearrange("m (c u t) -> m c t u", c=2, u=2))
+
+        def hand_out(k):
+            page = pages[k % PAGES]
+            nc.sync.dma_start(out_0[P * k : P * (k + 1), :], page[:])
+            if k == PACK - 1:
+                read_back()
+            if k >= PACK:
+                turn_twice(k, page)
 
         first_gated = keep.tile([P, J], F32, name="first_gated", tag="last_x", align_bytes=64)
         spare[0] = first_gated[:]
         gates, cands, blended = {0: gate(0)}, {}, {}
         cands[0] = candidate(0, *gates[0])
         pages.append(keep.tile([P, T], F32, name="page", tag="last_x", align_bytes=64))
-        nc.gpsimd.memset(pages[2][:], 0.0)
+        nc.gpsimd.memset(pages[PAGES - 1][:], 0.0)
         gates[1] = gate(1)
         rows = {0: gather(0, cands[0])}
-        mid = blend(0, rows[0], gates[0][0], cands[0])
+        mid = blend(rows[0], gates[0][0], cands[0])
         early = keep.tile([P, 2 * J], F32, name="early", tag="state0", align_bytes=64)
         spare[1], spare[2] = early[:, 0:J], early[:, J : 2 * J]
         for k in (1, 2):
@@ -323,7 +315,7 @@ def tile_list_tgn_mguP_kernel(
             if i - 1 in ON_VECTOR:
                 blended[i - 1] = weigh(i - 1, rows[i - 1], mid)
             if i <= LAST:
-                mid = blend(i, rows[i], gates[i][0], cands[i])
+                mid = blend(rows[i], gates[i][0], cands[i])
                 if i not in ON_VECTOR:
                     blended[i] = weigh(i, rows[i], mid)
             if i + 2 <= LAST:

@@ -47,7 +47,7 @@ def tile_list_tgn_mguP_kernel(
             return ring.tile(shape, dtype, name=name, tag="big", bufs=4, align_bytes=64)
 
         def woven_tile(name):
-            return ring.tile([P, COLS, PACK], BF16, name=name, tag="woven", bufs=8, align_bytes=64)
+            return ring.tile([P, COLS, PACK], BF16, name=name, tag="woven", bufs=5, align_bytes=64)
 
         def bank(tag):
             return psum.tile([P, COLS], F32, name=tag, tag=tag, bufs=2 if tag == "sz" else 3)
@@ -75,21 +75,31 @@ def tile_list_tgn_mguP_kernel(
             nc.sync.dma_start(raw[:], rows.rearrange("(p i) c -> p i c", i=PACK))
             return raw
 
-        def load_planes(dst, scales, first):
-            for r in range(QUADS):
-                nc.sync.dma_start(dst[first + r : P : QUAD, :, :].bitcast(I32),
-                                  scales[:, r : QUADS * QUADS : QUADS, :].rearrange("a q t -> q a t").bitcast(I32))
+        def load_rows(dst, scales, first, r):
+            nc.sync.dma_start(dst[first + r : P : QUAD, :, :].bitcast(I32),
+                              scales[:, r : QUADS * QUADS : QUADS, :].rearrange("a q t -> q a t").bitcast(I32))
+
+        def load_planes(n, rows):
+            for r in rows:
+                load_rows(planes[n], (uz_scales, un_scales)[n], 0, r)
+                load_rows(planes[2 + n], (wz_scales, wn_scales)[n], QUADS, r)
 
         words_of = {"uz": uz_words, "un": un_words, "wz": wz_words, "wn": wn_words}
         weights = {}
 
-        def load_words(name, piece):
-            lo, hi = WEIGHT_CUTS[piece], WEIGHT_CUTS[piece + 1]
-            tile = keep.tile([P, PASSES, hi - lo], I32, name="%s%d" % (name, piece), align_bytes=64)
+        def load_words(name, lo, hi):
+            tile = keep.tile([P, PASSES, hi - lo], I32, name="words", tag="%s%d" % (name, lo // P), align_bytes=64)
             columns = words_of[name].rearrange("a p n i -> p a (n i)")[:, :, PACK * lo : PACK * hi]
             nc.sync.dma_start(tile[:], columns.bitcast(I32))
             for k in range(lo // P, hi // P):
                 weights[name, k] = tile[:, :, P * k - lo : P * (k + 1) - lo]
+
+        def load_piece(piece):
+            lo, hi = WEIGHT_CUTS[piece], WEIGHT_CUTS[piece + 1]
+            for name in words_of:
+                step = P if name == "un" and piece else hi - lo
+                for first in range(lo, hi, step):
+                    load_words(name, first, first + step)
 
         def load_state(k):
             if k == 0:
@@ -105,25 +115,24 @@ def tile_list_tgn_mguP_kernel(
             nc.sync.dma_start(tab_w[:, J * c : J * (c + 1)], tab_rows[:, J * c : J * (c + 1)])
         x_raw, state = {}, {}
         x_raw[0, 0] = load_x(0, 0)
+        for r in range(QUADS):
+            load_rows(tab_sc, tab_scales, 0, r)
         nc.sync.dma_start(bias_rows[0:TILES, :], bz.rearrange("(k p) -> k p", p=P))
         nc.sync.dma_start(bias_rows[TILES : 2 * TILES, :], bn.rearrange("(k p) -> k p", p=P))
-        load_planes(tab_sc, tab_scales, 0)
         x_raw[1, 0] = load_x(1, 0)
-        load_planes(planes[0], uz_scales, 0)
+        load_planes(0, (0, 1, 2))
         x_raw[0, 1] = load_x(0, 1)
-        load_words("uz", 0)
-        load_words("un", 0)
-        load_planes(planes[1], un_scales, 0)
+        load_planes(0, (3,))
+        load_planes(1, (0, 1))
+        load_words("uz", 0, WEIGHT_CUTS[1])
+        load_planes(1, (2, 3))
+        load_words("un", 0, WEIGHT_CUTS[1])
         x_raw[1, 1] = load_x(1, 1)
-        load_planes(planes[2], wz_scales, QUADS)
-        load_words("wz", 0)
-        load_words("wn", 0)
-        load_planes(planes[3], wn_scales, QUADS)
+        load_words("wz", 0, WEIGHT_CUTS[1])
+        load_words("wn", 0, WEIGHT_CUTS[1])
         state[0] = load_state(0)
-        for name in words_of:
-            load_words(name, 1)
-        for name in words_of:
-            load_words(name, 2)
+        load_piece(1)
+        load_piece(2)
         state[1] = load_state(1)
         wgo_sb = keep.tile([P, J], F32, name="wgo_sb", tag="wgo", align_bytes=64)
         nc.sync.dma_start(wgo_sb[:], wgo)
@@ -194,8 +203,11 @@ def tile_list_tgn_mguP_kernel(
 
             sz, hn, xn = bank("sz"), bank("hn"), bank("xn")
             with_v(sz, "uz", 0, False)
-            with_v(hn, "un", 1, True)
+            if k == 0:
+                with_v(hn, "un", 1, True)
             with_x(sz, "wz", 0, False)
+            if k > 0:
+                with_v(hn, "un", 1, True)
             with_x(xn, "wn", 1, True)
             return sz, hn, xn
 
@@ -243,8 +255,11 @@ def tile_list_tgn_mguP_kernel(
             if k == LAST:
                 return mid[:]
             engine = nc.vector if k in ON_VECTOR else nc.gpsimd
-            engine.tensor_tensor(rows, mid[:], wgo_sb[:], ALU.mult)
-            return rows
+            into = rows
+            if k + 3 <= LAST:
+                into = keep.tile([P, J], F32, name="weighed", tag="un%d" % (k + 3), align_bytes=64)[:]
+            engine.tensor_tensor(into, mid[:], wgo_sb[:], ALU.mult)
+            return into
 
         def scatter(k, rows):
             window = pages[k % PAGES][:].indirect(offsets[:])
@@ -265,7 +280,11 @@ def tile_list_tgn_mguP_kernel(
                                again[:].rearrange("p i (c n) -> p c i n", n=LINE // 4))
 
         def turn_twice(k, page):
-            woven[k] = woven_tile("y_rounded")
+            if k == PACK:
+                woven[k] = woven_tile("y_rounded")
+            else:
+                woven[k] = keep.tile([P, COLS, PACK], BF16, name="y_turned", tag=("uz4", "wz4", "wn4")[k - PACK - 1],
+                                     align_bytes=64)
             words = woven[k][:].rearrange("p c i -> p (c i)").bitcast(F32)
             rounded = []
             for c in range(QUADS):
@@ -316,13 +335,13 @@ def tile_list_tgn_mguP_kernel(
                 blended[i - 1] = weigh(i - 1, rows[i - 1], mid)
             if i <= LAST:
                 mid = blend(rows[i], gates[i][0], cands[i])
-                if i not in ON_VECTOR:
-                    blended[i] = weigh(i, rows[i], mid)
             if i + 2 <= LAST:
                 cands[i + 2] = candidate(i + 2, *gates[i + 2])
             scatter(i - 1, blended[i - 1])
             if i + 3 <= LAST:
                 gates[i + 3] = gate(i + 3)
+            if i <= LAST and i not in ON_VECTOR:
+                blended[i] = weigh(i, rows[i], mid)
             hand_out(i - 1)
 
         y_sc = keep.tile([P, T + COLS], U8, name="y_sc", tag="wgo", align_bytes=64)

@@ -30,7 +30,6 @@ LAST = TILES - 1
 LINE = 16
 PAGES = 3
 ON_VECTOR = (0,)
-WEIGHT_CUTS = (0, 2 * P, 4 * P, N)
 
 
 def tile_list_tgn_mguP_kernel(
@@ -47,7 +46,7 @@ def tile_list_tgn_mguP_kernel(
             return ring.tile(shape, dtype, name=name, tag="big", bufs=4, align_bytes=64)
 
         def woven_tile(name):
-            return ring.tile([P, COLS, PACK], BF16, name=name, tag="woven", bufs=5, align_bytes=64)
+            return ring.tile([P, COLS, PACK], BF16, name=name, tag="woven", bufs=6, align_bytes=64)
 
         def bank(tag):
             return psum.tile([P, COLS], F32, name=tag, tag=tag, bufs=2 if tag == "sz" else 3)
@@ -75,31 +74,21 @@ def tile_list_tgn_mguP_kernel(
             nc.sync.dma_start(raw[:], rows.rearrange("(p i) c -> p i c", i=PACK))
             return raw
 
-        def load_rows(dst, scales, first, r):
-            nc.sync.dma_start(dst[first + r : P : QUAD, :, :].bitcast(I32),
-                              scales[:, r : QUADS * QUADS : QUADS, :].rearrange("a q t -> q a t").bitcast(I32))
-
-        def load_planes(n, rows):
-            for r in rows:
-                load_rows(planes[n], (uz_scales, un_scales)[n], 0, r)
-                load_rows(planes[2 + n], (wz_scales, wn_scales)[n], QUADS, r)
+        def load_planes(queue, dst, scales, first):
+            for r in range(QUADS):
+                queue.dma_start(dst[first + r : P : QUAD, :, :].bitcast(I32),
+                                scales[:, r : QUADS * QUADS : QUADS, :].rearrange("a q t -> q a t").bitcast(I32))
 
         words_of = {"uz": uz_words, "un": un_words, "wz": wz_words, "wn": wn_words}
         weights = {}
 
-        def load_words(name, lo, hi):
+        def load_words(name, first, count):
+            lo, hi = P * first, P * (first + count)
             tile = keep.tile([P, PASSES, hi - lo], I32, name="words", tag="%s%d" % (name, lo // P), align_bytes=64)
             columns = words_of[name].rearrange("a p n i -> p a (n i)")[:, :, PACK * lo : PACK * hi]
             nc.sync.dma_start(tile[:], columns.bitcast(I32))
             for k in range(lo // P, hi // P):
                 weights[name, k] = tile[:, :, P * k - lo : P * (k + 1) - lo]
-
-        def load_piece(piece):
-            lo, hi = WEIGHT_CUTS[piece], WEIGHT_CUTS[piece + 1]
-            for name in words_of:
-                step = P if name == "un" and piece else hi - lo
-                for first in range(lo, hi, step):
-                    load_words(name, first, first + step)
 
         def load_state(k):
             if k == 0:
@@ -115,28 +104,36 @@ def tile_list_tgn_mguP_kernel(
             nc.sync.dma_start(tab_w[:, J * c : J * (c + 1)], tab_rows[:, J * c : J * (c + 1)])
         x_raw, state = {}, {}
         x_raw[0, 0] = load_x(0, 0)
-        for r in range(QUADS):
-            load_rows(tab_sc, tab_scales, 0, r)
         nc.sync.dma_start(bias_rows[0:TILES, :], bz.rearrange("(k p) -> k p", p=P))
         nc.sync.dma_start(bias_rows[TILES : 2 * TILES, :], bn.rearrange("(k p) -> k p", p=P))
+        load_planes(nc.sync, tab_sc, tab_scales, 0)
         x_raw[1, 0] = load_x(1, 0)
-        load_planes(0, (0, 1, 2))
+        load_planes(nc.sync, planes[0], uz_scales, 0)
         x_raw[0, 1] = load_x(0, 1)
-        load_planes(0, (3,))
-        load_planes(1, (0, 1))
-        load_words("uz", 0, WEIGHT_CUTS[1])
-        load_planes(1, (2, 3))
-        load_words("un", 0, WEIGHT_CUTS[1])
+        load_words("uz", 0, 2)
+        load_words("un", 0, 2)
+        load_planes(nc.sync, planes[1], un_scales, 0)
         x_raw[1, 1] = load_x(1, 1)
-        load_words("wz", 0, WEIGHT_CUTS[1])
-        load_words("wn", 0, WEIGHT_CUTS[1])
+        load_planes(nc.sync, planes[2], wz_scales, QUADS)
+        load_words("wz", 0, 2)
+        load_words("wn", 0, 2)
+        load_planes(nc.sync, planes[3], wn_scales, QUADS)
         state[0] = load_state(0)
-        load_piece(1)
-        load_piece(2)
+        load_words("uz", 2, 1)
+        for name in ("un", "wz", "wn"):
+            load_words(name, 2, 2)
+        load_words("uz", 3, 2)
         state[1] = load_state(1)
         wgo_sb = keep.tile([P, J], F32, name="wgo_sb", tag="wgo", align_bytes=64)
         nc.sync.dma_start(wgo_sb[:], wgo)
-        for k in range(2, TILES):
+        state[2] = load_state(2)
+        load_words("un", 4, 2)
+        load_words("wz", 4, 4)
+        load_words("wn", 4, 4)
+        load_words("uz", 5, 2)
+        load_words("un", 6, 2)
+        load_words("uz", 7, 1)
+        for k in range(3, TILES):
             state[k] = load_state(k)
 
         turned_bias = bank("sz")
@@ -257,7 +254,7 @@ def tile_list_tgn_mguP_kernel(
             engine = nc.vector if k in ON_VECTOR else nc.gpsimd
             into = rows
             if k + 3 <= LAST:
-                into = keep.tile([P, J], F32, name="weighed", tag="un%d" % (k + 3), align_bytes=64)[:]
+                into = keep.tile([P, J], F32, name="weighed", tag=("un%d", "uz%d")[k % 2] % (k + 2), align_bytes=64)[:]
             engine.tensor_tensor(into, mid[:], wgo_sb[:], ALU.mult)
             return into
 
@@ -280,10 +277,10 @@ def tile_list_tgn_mguP_kernel(
                                again[:].rearrange("p i (c n) -> p c i n", n=LINE // 4))
 
         def turn_twice(k, page):
-            if k == PACK:
+            if k < LAST - 1:
                 woven[k] = woven_tile("y_rounded")
             else:
-                woven[k] = keep.tile([P, COLS, PACK], BF16, name="y_turned", tag=("uz4", "wz4", "wn4")[k - PACK - 1],
+                woven[k] = keep.tile([P, COLS, PACK], BF16, name="y_turned", tag=("wz4", "wn4")[k - LAST + 1],
                                      align_bytes=64)
             words = woven[k][:].rearrange("p c i -> p (c i)").bitcast(F32)
             rounded = []

@@ -209,12 +209,16 @@ def tile_list_tgn_mguP_kernel(
             return sz, hn, xn
 
         spare = {}
+        first_tile = keep.tile([P, 2 * J], F32, name="first_tile", tag="third_x", align_bytes=64)
+
+        def handed_on(k):
+            return ("un%d", "uz%d")[k % 2] % (k + 2)
 
         def gate(k):
             if k == 0:
-                stay = keep.tile([P, J], F32, name="stay", tag="third_x", align_bytes=64)
+                stay = first_tile[:, 0:J]
             else:
-                stay = ring.tile([P, J], F32, name="stay", tag="stay", bufs=3, align_bytes=64)
+                stay = ring.tile([P, J], F32, name="stay", tag="stay", bufs=3, align_bytes=64)[:]
             banks = []
             for half in range(HALVES):
                 sz, hn, xn = products(k, half)
@@ -236,15 +240,18 @@ def tile_list_tgn_mguP_kernel(
             return cand
 
         def gather(k, cand):
-            both = ring.tile([P, 2 * J], F32, name="rows", tag="work", bufs=2, align_bytes=64)
-            if k > 0:
-                spare[k + 2] = both[:, J : 2 * J]
-            nc.vector.tensor_tensor(both[:, 0:J], state[k][:].indirect(offsets[:]), cand[:], ALU.subtract)
-            return both[:, 0:J]
+            if k == 0:
+                rows = first_tile[:, J : 2 * J]
+            else:
+                tag = "second_tile" if k == 1 else handed_on(k - 2 if k < LAST else k - 4)
+                both = keep.tile([P, 2 * J], F32, name="rows", tag=tag, align_bytes=64)
+                rows, spare[k + 2] = both[:, 0:J], both[:, J : 2 * J]
+            nc.vector.tensor_tensor(rows, state[k][:].indirect(offsets[:]), cand[:], ALU.subtract)
+            return rows
 
         def blend(rows, stay, cand):
             mid = ring.tile([P, J], F32, name="mid", tag="mid", bufs=1)
-            nc.gpsimd.tensor_tensor(mid[:], rows, stay[:], ALU.mult)
+            nc.gpsimd.tensor_tensor(mid[:], rows, stay, ALU.mult)
             nc.gpsimd.tensor_tensor(mid[:], mid[:], cand[:], ALU.add)
             return mid
 
@@ -254,7 +261,7 @@ def tile_list_tgn_mguP_kernel(
             engine = nc.vector if k in ON_VECTOR else nc.gpsimd
             into = rows
             if k + 3 <= LAST:
-                into = keep.tile([P, J], F32, name="weighed", tag=("un%d", "uz%d")[k % 2] % (k + 2), align_bytes=64)[:]
+                into = keep.tile([P, J], F32, name="weighed", tag=handed_on(k), align_bytes=64)[:]
             engine.tensor_tensor(into, mid[:], wgo_sb[:], ALU.mult)
             return into
 
@@ -269,7 +276,10 @@ def tile_list_tgn_mguP_kernel(
 
         def read_back():
             for c in range(QUADS):
-                again = big([P, PACK, COLS], F32, "again")
+                if c < 2:
+                    again = keep.tile([P, PACK, COLS], F32, name="again", tag=("state0", "third_x")[c], align_bytes=64)
+                else:
+                    again = big([P, PACK, COLS], F32, "again")
                 rows = out_0[0:PASS, COLS * c : COLS * (c + 1)]
                 nc.sync.dma_start(again[:], rows.rearrange("(p i) c -> p i c", i=PACK))
                 woven[c] = woven_tile("y_rounded")

@@ -29,6 +29,7 @@ TILES = N // P
 LAST = TILES - 1
 LINE = 16
 PAGES = 3
+FIRST_SHARED = 3
 ON_VECTOR = (0,)
 
 
@@ -104,12 +105,13 @@ def tile_list_tgn_mguP_kernel(
             nc.sync.dma_start(tab_w[:, J * c : J * (c + 1)], tab_rows[:, J * c : J * (c + 1)])
         x_raw, state = {}, {}
         x_raw[0, 0] = load_x(0, 0)
-        nc.sync.dma_start(bias_rows[0:TILES, :], bz.rearrange("(k p) -> k p", p=P))
-        nc.sync.dma_start(bias_rows[TILES : 2 * TILES, :], bn.rearrange("(k p) -> k p", p=P))
         load_planes(nc.sync, tab_sc, tab_scales, 0)
         x_raw[1, 0] = load_x(1, 0)
         load_planes(nc.sync, planes[0], uz_scales, 0)
         x_raw[0, 1] = load_x(0, 1)
+        nc.sync.dma_start(bias_rows[0:TILES, :], bz.rearrange("(k p) -> k p", p=P))
+        nc.sync.dma_start(bias_rows[TILES : 2 * TILES, :], bn.rearrange("(k p) -> k p", p=P))
+        nc.sync.dma_start(bias_rows[2 * TILES : 3 * TILES, :], wgo[0].rearrange("(b p) -> b p", p=P))
         load_words("uz", 0, 2)
         load_words("un", 0, 2)
         load_planes(nc.sync, planes[1], un_scales, 0)
@@ -142,6 +144,8 @@ def tile_list_tgn_mguP_kernel(
         bz_neg = keep.tile([P, TILES], F32, name="bz_neg")
         nc.scalar.copy(bn_sb[:], turned_bias[:, TILES : 2 * TILES])
         nc.scalar.activation(bz_neg[:], turned_bias[:, 0:TILES], ACT.Copy, scale=-1.0)
+        wgo_turned = keep.tile([P, TILES], F32, name="wgo_turned")
+        nc.scalar.copy(wgo_turned[:], turned_bias[:, 2 * TILES : 3 * TILES])
 
         v_codes, v_sc, x_codes, x_sc = {}, {}, {}, {}
 
@@ -181,34 +185,19 @@ def tile_list_tgn_mguP_kernel(
         for page in pages:
             nc.gpsimd.memset(page[:], 0.0)
 
-        def products(k, half):
-            cols = slice(P * k, P * (k + 1))
-
-            def with_x(acc, name, n, opens):
-                for a in range(PASSES):
-                    nc.tensor.matmul_mx(out=acc[:], lhsT=weights[name, k][:, a, :].bitcast(FP8X4),
-                                        lhsT_scale=planes[2 + n][QUADS:P, a, cols],
-                                        rhs=x_codes[half][:, a, :].bitcast(FP8X4), rhs_scale=x_sc[half][:, a, :],
-                                        start=opens and a == 0, stop=a == PASSES - 1)
-
-            def with_v(acc, name, n, closes):
-                for a in range(PASSES):
-                    nc.tensor.matmul_mx(out=acc[:], lhsT=weights[name, k][:, a, :].bitcast(FP8X4),
-                                        lhsT_scale=planes[n][:, a, cols],
-                                        rhs=v_codes[half][:, a, :].bitcast(FP4X4), rhs_scale=v_sc[half][:, a, :],
-                                        start=a == 0, stop=closes and a == PASSES - 1)
-
-            sz, hn, xn = bank("sz"), bank("hn"), bank("xn")
-            with_v(sz, "uz", 0, False)
-            if k == 0:
-                with_v(hn, "un", 1, True)
-            with_x(sz, "wz", 0, False)
-            if k > 0:
-                with_v(hn, "un", 1, True)
-            with_x(xn, "wn", 1, True)
-            return sz, hn, xn
+        def passes(acc, name, k, half, opens, closes):
+            n, cols = list(words_of).index(name), slice(P * k, P * (k + 1))
+            for a in range(PASSES):
+                if n < 2:
+                    plane, moving, moving_sc = planes[n][:, a, cols], v_codes[half][:, a, :].bitcast(FP4X4), v_sc[half]
+                else:
+                    plane, moving, moving_sc = planes[n][QUADS:P, a, cols], x_codes[half][:, a, :].bitcast(FP8X4), x_sc[half]
+                nc.tensor.matmul_mx(out=acc[:], lhsT=weights[name, k][:, a, :].bitcast(FP8X4), lhsT_scale=plane,
+                                    rhs=moving, rhs_scale=moving_sc[:, a, :],
+                                    start=opens and a == 0, stop=closes and a == PASSES - 1)
 
         spare = {}
+        cands = {}
         first_tile = keep.tile([P, 2 * J], F32, name="first_tile", tag="third_x", align_bytes=64)
 
         def handed_on(k):
@@ -219,24 +208,38 @@ def tile_list_tgn_mguP_kernel(
                 stay = first_tile[:, 0:J]
             else:
                 stay = ring.tile([P, J], F32, name="stay", tag="stay", bufs=3, align_bytes=64)[:]
-            banks = []
+            hn, xn = [], []
             for half in range(HALVES):
-                sz, hn, xn = products(k, half)
+                sz = bank("sz")
+                hn.append(bank("hn"))
+                passes(sz, "uz", k, half, True, False)
+                passes(sz, "wz", k, half, False, True)
+                passes(hn[half], "un", k, half, True, True)
                 nc.scalar.activation(stay[:, COLS * half : COLS * (half + 1)], sz[:], ACT.Sigmoid,
                                      bias=bz_neg[:, k : k + 1], scale=-1.0)
-                banks.append((hn, xn))
-            return stay, banks
+            for half in range(HALVES):
+                xn.append(bank("xn"))
+                passes(xn[half], "wn", k, half, True, True)
+            cands[k] = ring.tile([P, J], F32, name="cand", tag="cand", bufs=4)
+            if k >= FIRST_SHARED:
+                nc.scalar.copy(cands[k][:, COLS:J], xn[1][:])
+            return stay, list(zip(hn, xn))
 
         def candidate(k, stay, banks):
-            cand = ring.tile([P, J], F32, name="cand", tag="cand", bufs=4)
+            cand = cands[k]
             gated = spare[k]
             for half, (hn, xn) in enumerate(banks):
                 cols = slice(COLS * half, COLS * (half + 1))
                 nc.vector.scalar_tensor_tensor(gated[:, cols], stay[:, cols], 1.0, hn[:], ALU.subtract, ALU.mult)
             for half, (hn, xn) in enumerate(banks):
                 cols = slice(COLS * half, COLS * (half + 1))
-                nc.vector.scalar_tensor_tensor(cand[:, cols], gated[:, cols], -1.0, xn[:], ALU.mult, ALU.add)
-                nc.scalar.activation(cand[:, cols], cand[:, cols], ACT.Tanh, bias=bn_sb[:, k : k + 1])
+                if k >= FIRST_SHARED and half == 1:
+                    total = rows[k - 2][:, 0:COLS]
+                    nc.gpsimd.tensor_tensor(total, cand[:, cols], gated[:, cols], ALU.subtract)
+                else:
+                    total = cand[:, cols]
+                    nc.vector.scalar_tensor_tensor(total, gated[:, cols], -1.0, xn[:], ALU.mult, ALU.add)
+                nc.scalar.activation(cand[:, cols], total, ACT.Tanh, bias=bn_sb[:, k : k + 1])
             return cand
 
         def gather(k, cand):
@@ -245,24 +248,41 @@ def tile_list_tgn_mguP_kernel(
             else:
                 tag = "second_tile" if k == 1 else handed_on(k - 2 if k < LAST else k - 4)
                 both = keep.tile([P, 2 * J], F32, name="rows", tag=tag, align_bytes=64)
-                rows, spare[k + 2] = both[:, 0:J], both[:, J : 2 * J]
+                rows, spare[k + 3] = both[:, 0:J], both[:, J : 2 * J]
             nc.vector.tensor_tensor(rows, state[k][:].indirect(offsets[:]), cand[:], ALU.subtract)
             return rows
 
-        def blend(rows, stay, cand):
+        def blend(k, rows, stay, cand):
             mid = ring.tile([P, J], F32, name="mid", tag="mid", bufs=1)
             nc.gpsimd.tensor_tensor(mid[:], rows, stay, ALU.mult)
-            nc.gpsimd.tensor_tensor(mid[:], mid[:], cand[:], ALU.add)
+            cols = slice(0, COLS if 0 < k < LAST else J)
+            nc.gpsimd.tensor_tensor(mid[:, cols], mid[:, cols], cand[:, cols], ALU.add)
             return mid
 
         def weigh(k, rows, mid):
             if k == LAST:
                 return mid[:]
-            engine = nc.vector if k in ON_VECTOR else nc.gpsimd
             into = rows
             if k + 3 <= LAST:
                 into = keep.tile([P, J], F32, name="weighed", tag=handed_on(k), align_bytes=64)[:]
-            engine.tensor_tensor(into, mid[:], wgo_sb[:], ALU.mult)
+            if k == 0:
+                nc.vector.tensor_tensor(into, mid[:], wgo_sb[:], ALU.mult)
+                return into
+            nc.gpsimd.tensor_tensor(into[:, 0:COLS], mid[:, 0:COLS], wgo_sb[:, 0:COLS], ALU.mult)
+            turned, back = bank("xn"), bank("xn")
+            for n, term in enumerate((cands[k], mid)):
+                for b in range(QUADS):
+                    nc.tensor.matmul(turned[:, P * b : P * (b + 1)], lhsT=term[:, COLS + P * b : COLS + P * (b + 1)],
+                                     rhs=identity[:], is_transpose=True,
+                                     start=n == 0 and b == 0, stop=n == 1 and b == QUADS - 1)
+            for b in range(QUADS):
+                block = spare[k + 3][:, P * b : P * (b + 1)]
+                nc.scalar.activation(block, turned[:, P * b : P * (b + 1)], ACT.Copy,
+                                     scale=wgo_turned[:, QUADS + b : QUADS + b + 1])
+            for b in range(QUADS):
+                block = spare[k + 3][:, P * b : P * (b + 1)]
+                nc.tensor.transpose(back[:, P * b : P * (b + 1)], block, identity[:])
+            nc.scalar.copy(into[:, COLS:J], back[:])
             return into
 
         def scatter(k, rows):
@@ -323,15 +343,15 @@ def tile_list_tgn_mguP_kernel(
 
         first_gated = keep.tile([P, J], F32, name="first_gated", tag="last_x", align_bytes=64)
         spare[0] = first_gated[:]
-        gates, cands, blended = {0: gate(0)}, {}, {}
+        gates, blended = {0: gate(0)}, {}
         cands[0] = candidate(0, *gates[0])
         pages.append(keep.tile([P, T], F32, name="page", tag="last_x", align_bytes=64))
         nc.gpsimd.memset(pages[PAGES - 1][:], 0.0)
         gates[1] = gate(1)
         rows = {0: gather(0, cands[0])}
-        mid = blend(rows[0], gates[0][0], cands[0])
+        mid = blend(0, rows[0], gates[0][0], cands[0])
         early = keep.tile([P, 2 * J], F32, name="early", tag="state0", align_bytes=64)
-        spare[1], spare[2] = early[:, 0:J], early[:, J : 2 * J]
+        spare[1], spare[2], spare[3] = early[:, 0:J], early[:, J : 2 * J], early[:, 0:J]
         for k in (1, 2):
             cands[k] = candidate(k, *gates[k])
             gates[k + 1] = gate(k + 1)
@@ -341,7 +361,7 @@ def tile_list_tgn_mguP_kernel(
             if i - 1 in ON_VECTOR:
                 blended[i - 1] = weigh(i - 1, rows[i - 1], mid)
             if i <= LAST:
-                mid = blend(rows[i], gates[i][0], cands[i])
+                mid = blend(i, rows[i], gates[i][0], cands[i])
             if i + 2 <= LAST:
                 cands[i + 2] = candidate(i + 2, *gates[i + 2])
             scatter(i - 1, blended[i - 1])

@@ -315,7 +315,7 @@ def tile_list_tgn_mguP_kernel(
             words = woven[k][:].rearrange("p c i -> p (c i)").bitcast(F32)
             rounded = []
             for c in range(QUADS):
-                turned = bank(("hn", "xn")[c % 2])
+                turned = bank("sz")
                 for q in range(QUADS):
                     first = COLS * q + P * c
                     nc.tensor.transpose(turned[:, P * q : P * (q + 1)], page[:, first : first + P], identity[:])

@@ -28,8 +28,9 @@ HALVES = J // COLS
 TILES = N // P
 LAST = TILES - 1
 LINE = 16
+BANK = 2048
 PAGES = 3
-FIRST_SHARED = 3
+FIRST_SHARED = 2
 ON_VECTOR = (0,)
 
 
@@ -50,7 +51,8 @@ def tile_list_tgn_mguP_kernel(
             return ring.tile([P, COLS, PACK], BF16, name=name, tag="woven", bufs=6, align_bytes=64)
 
         def bank(tag):
-            return psum.tile([P, COLS], F32, name=tag, tag=tag, bufs=2 if tag == "sz" else 3)
+            return psum.tile([P, COLS], F32, name=tag, tag=tag, bufs=2 if tag == "sz" else 3,
+                             offset={"sz": 0, "hn": 2, "xn": 5}[tag] * BANK)
 
         offsets = keep.tile([P, J // 16], U16, name="offsets")
         nc.sync.dma_start(offsets[:], offs)
@@ -315,23 +317,25 @@ def tile_list_tgn_mguP_kernel(
             words = woven[k][:].rearrange("p c i -> p (c i)").bitcast(F32)
             rounded = []
             for c in range(QUADS):
-                turned = bank("sz")
+                turned = psum.tile([P, COLS], F32, name="turned", tag="turned%d" % c, bufs=1,
+                                   offset=(2 * (c % 2) + c // 2) * BANK)[:]
                 for q in range(QUADS):
                     first = COLS * q + P * c
                     nc.tensor.transpose(turned[:, P * q : P * (q + 1)], page[:, first : first + P], identity[:])
                 rows = ring.tile([P, COLS], BF16, name="rows", tag="rows", bufs=QUADS, align_bytes=64)
                 nc.scalar.copy(rows[:].rearrange("t (u m e) -> t u m e", u=2, e=2),
-                               turned[:].rearrange("t (m u e) -> t u m e", u=2, e=2))
+                               turned.rearrange("t (m u e) -> t u m e", u=2, e=2))
                 rounded.append(rows)
             for pair in range(2):
-                back = bank("sz")
+                back = psum.tile([P, 2, COLS], F32, name="back", tag="back%d" % pair, bufs=1,
+                                 offset=2 * pair * BANK)[:, 0, :]
                 for c in range(2):
                     for u in range(2):
                         first = P * (2 * c + u)
                         nc.tensor.transpose(back[:, first : first + P],
                                             rounded[2 * pair + c][:].bitcast(F32)[:, P * u : P * (u + 1)], identity[:])
                 nc.scalar.copy(words[:, COLS * pair : COLS * (pair + 1)].rearrange("m (c t u) -> m c t u", c=2, u=2),
-                               back[:].rearrange("m (c u t) -> m c t u", c=2, u=2))
+                               back.rearrange("m (c u t) -> m c t u", c=2, u=2))
 
         def hand_out(k):
             page = pages[k % PAGES]
@@ -390,9 +394,10 @@ def tile_list_tgn_mguP_kernel(
                                   in_=woven[PACK + row][:].rearrange("p c i -> p (c i)"))
             if row >= PACK - 2:
                 for q in range(QUADS):
-                    nc.sync.dma_start(words[:, stored : row + 1, COLS * q : COLS * (q + 1)],
-                                      codes[QUAD * q : QUAD * (q + 1), stored : row + 1, :].bitcast(I32))
+                    queue = nc.scalar if row == PACK - 1 and q >= 2 else nc.sync
+                    queue.dma_start(words[:, stored : row + 1, COLS * q : COLS * (q + 1)],
+                                    codes[QUAD * q : QUAD * (q + 1), stored : row + 1, :].bitcast(I32))
                 stored = row + 1
         for q in range(QUADS):
-            nc.sync.dma_start(out_2[1, :, COLS * q : COLS * (q + 1)].bitcast(I32),
+            (nc.scalar if q >= 2 else nc.sync).dma_start(out_2[1, :, COLS * q : COLS * (q + 1)].bitcast(I32),
                               y_sc[QUAD * q : QUAD * q + QUADS * PACK, T : T + COLS].bitcast(I32))

@@ -30,7 +30,8 @@ LAST = TILES - 1
 LINE = 16
 BANK = 2048
 PAGES = 3
-FIRST_SHARED = 2
+FIRST_TURNED = 2
+FIRST_SHARED = FIRST_TURNED + 2
 ON_VECTOR = (0,)
 
 
@@ -257,8 +258,8 @@ def tile_list_tgn_mguP_kernel(
         def blend(k, rows, stay, cand):
             mid = ring.tile([P, J], F32, name="mid", tag="mid", bufs=1)
             nc.gpsimd.tensor_tensor(mid[:], rows, stay, ALU.mult)
-            cols = slice(0, COLS if 0 < k < LAST else J)
-            nc.gpsimd.tensor_tensor(mid[:, cols], mid[:, cols], cand[:, cols], ALU.add)
+            if k < FIRST_TURNED or k == LAST:
+                nc.gpsimd.tensor_tensor(mid[:], mid[:], cand[:], ALU.add)
             return mid
 
         def weigh(k, rows, mid):
@@ -267,9 +268,10 @@ def tile_list_tgn_mguP_kernel(
             into = rows
             if k + 3 <= LAST:
                 into = keep.tile([P, J], F32, name="weighed", tag=handed_on(k), align_bytes=64)[:]
-            if k == 0:
-                nc.vector.tensor_tensor(into, mid[:], wgo_sb[:], ALU.mult)
+            if k < FIRST_TURNED:
+                (nc.gpsimd if k else nc.vector).tensor_tensor(into, mid[:], wgo_sb[:], ALU.mult)
                 return into
+            nc.gpsimd.tensor_tensor(mid[:, 0:COLS], mid[:, 0:COLS], cands[k][:, 0:COLS], ALU.add)
             nc.gpsimd.tensor_tensor(into[:, 0:COLS], mid[:, 0:COLS], wgo_sb[:, 0:COLS], ALU.mult)
             turned, back = bank("xn"), bank("xn")
             for n, term in enumerate((cands[k], mid)):
@@ -394,10 +396,9 @@ def tile_list_tgn_mguP_kernel(
                                   in_=woven[PACK + row][:].rearrange("p c i -> p (c i)"))
             if row >= PACK - 2:
                 for q in range(QUADS):
-                    queue = nc.scalar if row == PACK - 1 and q >= 2 else nc.sync
-                    queue.dma_start(words[:, stored : row + 1, COLS * q : COLS * (q + 1)],
+                    nc.sync.dma_start(words[:, stored : row + 1, COLS * q : COLS * (q + 1)],
                                     codes[QUAD * q : QUAD * (q + 1), stored : row + 1, :].bitcast(I32))
                 stored = row + 1
         for q in range(QUADS):
-            (nc.scalar if q >= 2 else nc.sync).dma_start(out_2[1, :, COLS * q : COLS * (q + 1)].bitcast(I32),
+            nc.sync.dma_start(out_2[1, :, COLS * q : COLS * (q + 1)].bitcast(I32),
                               y_sc[QUAD * q : QUAD * q + QUADS * PACK, T : T + COLS].bitcast(I32))

@@ -49,7 +49,7 @@ def tile_list_tgn_mguP_kernel(
             return ring.tile(shape, dtype, name=name, tag="big", bufs=4, align_bytes=64)
 
         def woven_tile(name):
-            return ring.tile([P, COLS, PACK], BF16, name=name, tag="woven", bufs=6, align_bytes=64)
+            return ring.tile([P, COLS, PACK], BF16, name=name, tag="woven", bufs=3, align_bytes=64)
 
         def bank(tag):
             return psum.tile([P, COLS], F32, name=tag, tag=tag, bufs=2 if tag == "sz" else 3,
@@ -58,7 +58,7 @@ def tile_list_tgn_mguP_kernel(
         offsets = keep.tile([P, J // 16], U16, name="offsets")
         nc.sync.dma_start(offsets[:], offs)
 
-        tab_sc = keep.tile([P, PASSES, T], U8, name="tab_sc", align_bytes=64)
+        tab_sc = keep.tile([P, PASSES, T], U8, name="tab_sc", tag="tab_sc", align_bytes=64)
         planes = [keep.tile([P, PASSES, N], U8, name="planes%d" % n, align_bytes=64) for n in range(4)]
         for tile in [tab_sc] + planes:
             nc.vector.memset(tile[:].rearrange("p a t -> p (a t)").bitcast(I32), 0)
@@ -223,26 +223,26 @@ def tile_list_tgn_mguP_kernel(
             for half in range(HALVES):
                 xn.append(bank("xn"))
                 passes(xn[half], "wn", k, half, True, True)
-            cands[k] = ring.tile([P, J], F32, name="cand", tag="cand", bufs=4)
             if k >= FIRST_SHARED:
-                nc.scalar.copy(cands[k][:, COLS:J], xn[1][:])
+                emptied = keep.tile([P, J], F32, name="xn_sb", tag="cand%d" % (k % 2), align_bytes=64)
+                for half in range(HALVES):
+                    nc.scalar.copy(emptied[:, COLS * half : COLS * (half + 1)], xn[half][:])
+                xn = [emptied, emptied]
             return stay, list(zip(hn, xn))
 
         def candidate(k, stay, banks):
-            cand = cands[k]
+            cand = keep.tile([P, J], F32, name="cand", tag="cand%d" % (k if k < 2 else 2 + k % 2), align_bytes=64)
             gated = spare[k]
             for half, (hn, xn) in enumerate(banks):
                 cols = slice(COLS * half, COLS * (half + 1))
                 nc.vector.scalar_tensor_tensor(gated[:, cols], stay[:, cols], 1.0, hn[:], ALU.subtract, ALU.mult)
+            if k >= FIRST_SHARED:
+                nc.gpsimd.tensor_tensor(rows[k - 2], banks[0][1][:], gated, ALU.subtract)
+                return cand
             for half, (hn, xn) in enumerate(banks):
                 cols = slice(COLS * half, COLS * (half + 1))
-                if k >= FIRST_SHARED and half == 1:
-                    total = rows[k - 2][:, 0:COLS]
-                    nc.gpsimd.tensor_tensor(total, cand[:, cols], gated[:, cols], ALU.subtract)
-                else:
-                    total = cand[:, cols]
-                    nc.vector.scalar_tensor_tensor(total, gated[:, cols], -1.0, xn[:], ALU.mult, ALU.add)
-                nc.scalar.activation(cand[:, cols], total, ACT.Tanh, bias=bn_sb[:, k : k + 1])
+                nc.vector.scalar_tensor_tensor(cand[:, cols], gated[:, cols], -1.0, xn[:], ALU.mult, ALU.add)
+                nc.scalar.activation(cand[:, cols], cand[:, cols], ACT.Tanh, bias=bn_sb[:, k : k + 1])
             return cand
 
         def gather(k, cand):
@@ -251,7 +251,7 @@ def tile_list_tgn_mguP_kernel(
             else:
                 tag = "second_tile" if k == 1 else handed_on(k - 2 if k < LAST else k - 4)
                 both = keep.tile([P, 2 * J], F32, name="rows", tag=tag, align_bytes=64)
-                rows, spare[k + 3] = both[:, 0:J], both[:, J : 2 * J]
+                rows, spare[k + 2] = both[:, 0:J], both[:, J : 2 * J]
             nc.vector.tensor_tensor(rows, state[k][:].indirect(offsets[:]), cand[:], ALU.subtract)
             return rows
 
@@ -271,22 +271,31 @@ def tile_list_tgn_mguP_kernel(
             if k < FIRST_TURNED:
                 (nc.gpsimd if k else nc.vector).tensor_tensor(into, mid[:], wgo_sb[:], ALU.mult)
                 return into
-            nc.gpsimd.tensor_tensor(mid[:, 0:COLS], mid[:, 0:COLS], cands[k][:, 0:COLS], ALU.add)
-            nc.gpsimd.tensor_tensor(into[:, 0:COLS], mid[:, 0:COLS], wgo_sb[:, 0:COLS], ALU.mult)
-            turned, back = bank("xn"), bank("xn")
-            for n, term in enumerate((cands[k], mid)):
+            halves = range(HALVES)
+            if k == LAST - 1:
+                halves = (1,)
+                nc.gpsimd.tensor_tensor(mid[:, 0:COLS], mid[:, 0:COLS], cands[k][:, 0:COLS], ALU.add)
+                nc.gpsimd.tensor_tensor(into[:, 0:COLS], mid[:, 0:COLS], wgo_sb[:, 0:COLS], ALU.mult)
+            for half in halves:
+                turned = bank("xn")
+                for n, term in enumerate((cands[k], mid)):
+                    for b in range(QUADS):
+                        first = COLS * half + P * b
+                        nc.tensor.matmul(turned[:, P * b : P * (b + 1)], lhsT=term[:, first : first + P],
+                                         rhs=identity[:], is_transpose=True,
+                                         start=n == 0 and b == 0, stop=n == 1 and b == QUADS - 1)
                 for b in range(QUADS):
-                    nc.tensor.matmul(turned[:, P * b : P * (b + 1)], lhsT=term[:, COLS + P * b : COLS + P * (b + 1)],
-                                     rhs=identity[:], is_transpose=True,
-                                     start=n == 0 and b == 0, stop=n == 1 and b == QUADS - 1)
-            for b in range(QUADS):
-                block = spare[k + 3][:, P * b : P * (b + 1)]
-                nc.scalar.activation(block, turned[:, P * b : P * (b + 1)], ACT.Copy,
-                                     scale=wgo_turned[:, QUADS + b : QUADS + b + 1])
-            for b in range(QUADS):
-                block = spare[k + 3][:, P * b : P * (b + 1)]
-                nc.tensor.transpose(back[:, P * b : P * (b + 1)], block, identity[:])
-            nc.scalar.copy(into[:, COLS:J], back[:])
+                    block = QUADS * half + b
+                    nc.scalar.activation(mid[:, P * block : P * (block + 1)], turned[:, P * b : P * (b + 1)],
+                                         ACT.Copy, scale=wgo_turned[:, block : block + 1])
+            if k + 2 <= LAST:
+                nc.scalar.activation(cands[k + 2][:], rows, ACT.Tanh, bias=bn_sb[:, k + 2 : k + 3])
+            for half in halves:
+                back = bank("xn")
+                for b in range(QUADS):
+                    first = COLS * half + P * b
+                    nc.tensor.transpose(back[:, P * b : P * (b + 1)], mid[:, first : first + P], identity[:])
+                nc.scalar.copy(into[:, COLS * half : COLS * (half + 1)], back[:])
             return into
 
         def scatter(k, rows):
@@ -298,17 +307,19 @@ def tile_list_tgn_mguP_kernel(
 
         woven = {}
 
-        def read_back():
-            for c in range(QUADS):
-                if c < 2:
-                    again = keep.tile([P, PACK, COLS], F32, name="again", tag=("state0", "third_x")[c], align_bytes=64)
-                else:
-                    again = big([P, PACK, COLS], F32, "again")
-                rows = out_0[0:PASS, COLS * c : COLS * (c + 1)]
-                nc.sync.dma_start(again[:], rows.rearrange("(p i) c -> p i c", i=PACK))
+        def read_back(c):
+            again = keep.tile([P, PACK, COLS], F32, name="again", tag=("state0", "state0", "third_x", "second_tile")[c],
+                              align_bytes=64)
+            rows = out_0[0:PASS, COLS * c : COLS * (c + 1)]
+            nc.sync.dma_start(again[:], rows.rearrange("(p i) c -> p i c", i=PACK))
+            if c == 1:
                 woven[c] = woven_tile("y_rounded")
-                nc.scalar.copy(woven[c][:].rearrange("p (c n) i -> p c i n", n=LINE // 4),
-                               again[:].rearrange("p i (c n) -> p c i n", n=LINE // 4))
+            elif c == QUADS - 1:
+                woven[c] = keep.tile([P, COLS, PACK], BF16, name="y_rounded", tag="tab_sc", align_bytes=64)
+            else:
+                woven[c] = ring.tile([P, COLS, PACK], BF16, name="y_rounded", tag="stay", bufs=3, align_bytes=64)
+            nc.scalar.copy(woven[c][:].rearrange("p (c n) i -> p c i n", n=LINE // 4),
+                           again[:].rearrange("p i (c n) -> p c i n", n=LINE // 4))
 
         def turn_twice(k, page):
             if k < LAST - 1:
@@ -317,17 +328,16 @@ def tile_list_tgn_mguP_kernel(
                 woven[k] = keep.tile([P, COLS, PACK], BF16, name="y_turned", tag=("wz4", "wn4")[k - LAST + 1],
                                      align_bytes=64)
             words = woven[k][:].rearrange("p c i -> p (c i)").bitcast(F32)
-            rounded = []
+            rounded = keep.tile([P, QUADS, COLS], BF16, name="rounded", align_bytes=64,
+                                tag="tab_sc" if k == PACK else "rounded")
             for c in range(QUADS):
                 turned = psum.tile([P, COLS], F32, name="turned", tag="turned%d" % c, bufs=1,
                                    offset=(2 * (c % 2) + c // 2) * BANK)[:]
                 for q in range(QUADS):
                     first = COLS * q + P * c
                     nc.tensor.transpose(turned[:, P * q : P * (q + 1)], page[:, first : first + P], identity[:])
-                rows = ring.tile([P, COLS], BF16, name="rows", tag="rows", bufs=QUADS, align_bytes=64)
-                nc.scalar.copy(rows[:].rearrange("t (u m e) -> t u m e", u=2, e=2),
+                nc.scalar.copy(rounded[:, c, :].rearrange("t (u m e) -> t u m e", u=2, e=2),
                                turned.rearrange("t (m u e) -> t u m e", u=2, e=2))
-                rounded.append(rows)
             for pair in range(2):
                 back = psum.tile([P, 2, COLS], F32, name="back", tag="back%d" % pair, bufs=1,
                                  offset=2 * pair * BANK)[:, 0, :]
@@ -335,17 +345,20 @@ def tile_list_tgn_mguP_kernel(
                     for u in range(2):
                         first = P * (2 * c + u)
                         nc.tensor.transpose(back[:, first : first + P],
-                                            rounded[2 * pair + c][:].bitcast(F32)[:, P * u : P * (u + 1)], identity[:])
+                                            rounded[:, 2 * pair + c, :].bitcast(F32)[:, P * u : P * (u + 1)], identity[:])
                 nc.scalar.copy(words[:, COLS * pair : COLS * (pair + 1)].rearrange("m (c t u) -> m c t u", c=2, u=2),
                                back.rearrange("m (c u t) -> m c t u", c=2, u=2))
 
         def hand_out(k):
             page = pages[k % PAGES]
             nc.sync.dma_start(out_0[P * k : P * (k + 1), :], page[:])
-            if k == PACK - 1:
-                read_back()
+            if k == PACK:
+                read_back(0)
+                read_back(1)
             if k >= PACK:
                 turn_twice(k, page)
+            if k in (PACK, PACK + 1):
+                read_back(LAST - k)
 
         first_gated = keep.tile([P, J], F32, name="first_gated", tag="last_x", align_bytes=64)
         spare[0] = first_gated[:]
@@ -357,7 +370,7 @@ def tile_list_tgn_mguP_kernel(
         rows = {0: gather(0, cands[0])}
         mid = blend(0, rows[0], gates[0][0], cands[0])
         early = keep.tile([P, 2 * J], F32, name="early", tag="state0", align_bytes=64)
-        spare[1], spare[2], spare[3] = early[:, 0:J], early[:, J : 2 * J], early[:, 0:J]
+        spare[1], spare[2] = early[:, 0:J], early[:, J : 2 * J]
         for k in (1, 2):
             cands[k] = candidate(k, *gates[k])
             gates[k + 1] = gate(k + 1)

@@ -30,9 +30,7 @@ LAST = TILES - 1
 LINE = 16
 BANK = 2048
 PAGES = 3
-FIRST_TURNED = 2
-FIRST_SHARED = FIRST_TURNED + 2
-ON_VECTOR = (0,)
+FIRST_SHARED = 3
 
 
 def tile_list_tgn_mguP_kernel(
@@ -47,6 +45,9 @@ def tile_list_tgn_mguP_kernel(
 
         def big(shape, dtype, name):
             return ring.tile(shape, dtype, name=name, tag="big", bufs=4, align_bytes=64)
+
+        def bank_pair(n):
+            return psum.tile([P, 2, COLS], F32, name="back", tag="back%d" % n, bufs=1, offset=2 * n * BANK)[:, 0, :]
 
         def woven_tile(name):
             return ring.tile([P, COLS, PACK], BF16, name=name, tag="woven", bufs=3, align_bytes=64)
@@ -78,10 +79,10 @@ def tile_list_tgn_mguP_kernel(
             nc.sync.dma_start(raw[:], rows.rearrange("(p i) c -> p i c", i=PACK))
             return raw
 
-        def load_planes(queue, dst, scales, first):
+        def load_planes(dst, scales, first):
             for r in range(QUADS):
-                queue.dma_start(dst[first + r : P : QUAD, :, :].bitcast(I32),
-                                scales[:, r : QUADS * QUADS : QUADS, :].rearrange("a q t -> q a t").bitcast(I32))
+                nc.sync.dma_start(dst[first + r : P : QUAD, :, :].bitcast(I32),
+                                  scales[:, r : QUADS * QUADS : QUADS, :].rearrange("a q t -> q a t").bitcast(I32))
 
         words_of = {"uz": uz_words, "un": un_words, "wz": wz_words, "wn": wn_words}
         weights = {}
@@ -108,21 +109,21 @@ def tile_list_tgn_mguP_kernel(
             nc.sync.dma_start(tab_w[:, J * c : J * (c + 1)], tab_rows[:, J * c : J * (c + 1)])
         x_raw, state = {}, {}
         x_raw[0, 0] = load_x(0, 0)
-        load_planes(nc.sync, tab_sc, tab_scales, 0)
+        load_planes(tab_sc, tab_scales, 0)
         x_raw[1, 0] = load_x(1, 0)
-        load_planes(nc.sync, planes[0], uz_scales, 0)
+        load_planes(planes[0], uz_scales, 0)
         x_raw[0, 1] = load_x(0, 1)
         nc.sync.dma_start(bias_rows[0:TILES, :], bz.rearrange("(k p) -> k p", p=P))
         nc.sync.dma_start(bias_rows[TILES : 2 * TILES, :], bn.rearrange("(k p) -> k p", p=P))
         nc.sync.dma_start(bias_rows[2 * TILES : 3 * TILES, :], wgo[0].rearrange("(b p) -> b p", p=P))
         load_words("uz", 0, 2)
         load_words("un", 0, 2)
-        load_planes(nc.sync, planes[1], un_scales, 0)
+        load_planes(planes[1], un_scales, 0)
         x_raw[1, 1] = load_x(1, 1)
-        load_planes(nc.sync, planes[2], wz_scales, QUADS)
+        load_planes(planes[2], wz_scales, QUADS)
         load_words("wz", 0, 2)
         load_words("wn", 0, 2)
-        load_planes(nc.sync, planes[3], wn_scales, QUADS)
+        load_planes(planes[3], wn_scales, QUADS)
         state[0] = load_state(0)
         load_words("uz", 2, 1)
         for name in ("un", "wz", "wn"):
@@ -192,9 +193,11 @@ def tile_list_tgn_mguP_kernel(
             n, cols = list(words_of).index(name), slice(P * k, P * (k + 1))
             for a in range(PASSES):
                 if n < 2:
-                    plane, moving, moving_sc = planes[n][:, a, cols], v_codes[half][:, a, :].bitcast(FP4X4), v_sc[half]
+                    plane, moving_sc = planes[n][:, a, cols], v_sc[half]
+                    moving = v_codes[half][:, a, :].bitcast(FP4X4)
                 else:
-                    plane, moving, moving_sc = planes[n][QUADS:P, a, cols], x_codes[half][:, a, :].bitcast(FP8X4), x_sc[half]
+                    plane, moving_sc = planes[n][QUADS:P, a, cols], x_sc[half]
+                    moving = x_codes[half][:, a, :].bitcast(FP8X4)
                 nc.tensor.matmul_mx(out=acc[:], lhsT=weights[name, k][:, a, :].bitcast(FP8X4), lhsT_scale=plane,
                                     rhs=moving, rhs_scale=moving_sc[:, a, :],
                                     start=opens and a == 0, stop=closes and a == PASSES - 1)
@@ -224,24 +227,24 @@ def tile_list_tgn_mguP_kernel(
                 xn.append(bank("xn"))
                 passes(xn[half], "wn", k, half, True, True)
             if k >= FIRST_SHARED:
-                emptied = keep.tile([P, J], F32, name="xn_sb", tag="cand%d" % (k % 2), align_bytes=64)
+                emptied = keep.tile([P, J], F32, name="xn_sb", tag="cand%d" % (3 * (k % 2)), align_bytes=64)
                 for half in range(HALVES):
                     nc.scalar.copy(emptied[:, COLS * half : COLS * (half + 1)], xn[half][:])
-                xn = [emptied, emptied]
-            return stay, list(zip(hn, xn))
+                xn = emptied
+            return stay, hn, xn
 
-        def candidate(k, stay, banks):
-            cand = keep.tile([P, J], F32, name="cand", tag="cand%d" % (k if k < 2 else 2 + k % 2), align_bytes=64)
+        def candidate(k, stay, hn, xn):
+            cand = keep.tile([P, J], F32, name="cand", tag="cand%d" % (2 - k % 2 if k else 0), align_bytes=64)
             gated = spare[k]
-            for half, (hn, xn) in enumerate(banks):
+            for half in range(HALVES):
                 cols = slice(COLS * half, COLS * (half + 1))
-                nc.vector.scalar_tensor_tensor(gated[:, cols], stay[:, cols], 1.0, hn[:], ALU.subtract, ALU.mult)
+                nc.vector.scalar_tensor_tensor(gated[:, cols], stay[:, cols], 1.0, hn[half][:], ALU.subtract, ALU.mult)
             if k >= FIRST_SHARED:
-                nc.gpsimd.tensor_tensor(rows[k - 2], banks[0][1][:], gated, ALU.subtract)
+                nc.gpsimd.tensor_tensor(rows[k - 2], xn[:], gated, ALU.subtract)
                 return cand
-            for half, (hn, xn) in enumerate(banks):
+            for half in range(HALVES):
                 cols = slice(COLS * half, COLS * (half + 1))
-                nc.vector.scalar_tensor_tensor(cand[:, cols], gated[:, cols], -1.0, xn[:], ALU.mult, ALU.add)
+                nc.vector.scalar_tensor_tensor(cand[:, cols], gated[:, cols], -1.0, xn[half][:], ALU.mult, ALU.add)
                 nc.scalar.activation(cand[:, cols], cand[:, cols], ACT.Tanh, bias=bn_sb[:, k : k + 1])
             return cand
 
@@ -258,7 +261,7 @@ def tile_list_tgn_mguP_kernel(
         def blend(k, rows, stay, cand):
             mid = ring.tile([P, J], F32, name="mid", tag="mid", bufs=1)
             nc.gpsimd.tensor_tensor(mid[:], rows, stay, ALU.mult)
-            if k < FIRST_TURNED or k == LAST:
+            if k in (0, LAST):
                 nc.gpsimd.tensor_tensor(mid[:], mid[:], cand[:], ALU.add)
             return mid
 
@@ -268,8 +271,8 @@ def tile_list_tgn_mguP_kernel(
             into = rows
             if k + 3 <= LAST:
                 into = keep.tile([P, J], F32, name="weighed", tag=handed_on(k), align_bytes=64)[:]
-            if k < FIRST_TURNED:
-                (nc.gpsimd if k else nc.vector).tensor_tensor(into, mid[:], wgo_sb[:], ALU.mult)
+            if k == 0:
+                nc.vector.tensor_tensor(into, mid[:], wgo_sb[:], ALU.mult)
                 return into
             halves = range(HALVES)
             if k == LAST - 1:
@@ -291,7 +294,7 @@ def tile_list_tgn_mguP_kernel(
             if k + 2 <= LAST:
                 nc.scalar.activation(cands[k + 2][:], rows, ACT.Tanh, bias=bn_sb[:, k + 2 : k + 3])
             for half in halves:
-                back = bank("xn")
+                back = bank_pair(half) if k == PACK + 1 else bank("xn")
                 for b in range(QUADS):
                     first = COLS * half + P * b
                     nc.tensor.transpose(back[:, P * b : P * (b + 1)], mid[:, first : first + P], identity[:])
@@ -308,8 +311,8 @@ def tile_list_tgn_mguP_kernel(
         woven = {}
 
         def read_back(c):
-            again = keep.tile([P, PACK, COLS], F32, name="again", tag=("state0", "state0", "third_x", "second_tile")[c],
-                              align_bytes=64)
+            again = keep.tile([P, PACK, COLS], F32, name="again", align_bytes=64,
+                              tag=("state0", "state0", "third_x", "second_tile")[c])
             rows = out_0[0:PASS, COLS * c : COLS * (c + 1)]
             nc.sync.dma_start(again[:], rows.rearrange("(p i) c -> p i c", i=PACK))
             if c == 1:
@@ -339,13 +342,12 @@ def tile_list_tgn_mguP_kernel(
                 nc.scalar.copy(rounded[:, c, :].rearrange("t (u m e) -> t u m e", u=2, e=2),
                                turned.rearrange("t (m u e) -> t u m e", u=2, e=2))
             for pair in range(2):
-                back = psum.tile([P, 2, COLS], F32, name="back", tag="back%d" % pair, bufs=1,
-                                 offset=2 * pair * BANK)[:, 0, :]
+                back = bank_pair(pair)
                 for c in range(2):
                     for u in range(2):
                         first = P * (2 * c + u)
-                        nc.tensor.transpose(back[:, first : first + P],
-                                            rounded[:, 2 * pair + c, :].bitcast(F32)[:, P * u : P * (u + 1)], identity[:])
+                        pairs = rounded[:, 2 * pair + c, :].bitcast(F32)
+                        nc.tensor.transpose(back[:, first : first + P], pairs[:, P * u : P * (u + 1)], identity[:])
                 nc.scalar.copy(words[:, COLS * pair : COLS * (pair + 1)].rearrange("m (c t u) -> m c t u", c=2, u=2),
                                back.rearrange("m (c u t) -> m c t u", c=2, u=2))
 
@@ -377,8 +379,8 @@ def tile_list_tgn_mguP_kernel(
         for i in range(1, TILES + 1):
             if i <= LAST:
                 rows[i] = gather(i, cands[i])
-            if i - 1 in ON_VECTOR:
-                blended[i - 1] = weigh(i - 1, rows[i - 1], mid)
+            if i == 1:
+                blended[0] = weigh(0, rows[0], mid)
             if i <= LAST:
                 mid = blend(i, rows[i], gates[i][0], cands[i])
             if i + 2 <= LAST:
@@ -386,7 +388,7 @@ def tile_list_tgn_mguP_kernel(
             scatter(i - 1, blended[i - 1])
             if i + 3 <= LAST:
                 gates[i + 3] = gate(i + 3)
-            if i <= LAST and i not in ON_VECTOR:
+            if i <= LAST:
                 blended[i] = weigh(i, rows[i], mid)
             hand_out(i - 1)
 
@@ -410,7 +412,7 @@ def tile_list_tgn_mguP_kernel(
             if row >= PACK - 2:
                 for q in range(QUADS):
                     nc.sync.dma_start(words[:, stored : row + 1, COLS * q : COLS * (q + 1)],
-                                    codes[QUAD * q : QUAD * (q + 1), stored : row + 1, :].bitcast(I32))
+                                      codes[QUAD * q : QUAD * (q + 1), stored : row + 1, :].bitcast(I32))
                 stored = row + 1
         for q in range(QUADS):
             nc.sync.dma_start(out_2[1, :, COLS * q : COLS * (q + 1)].bitcast(I32),

@@ -148,6 +148,8 @@ def tile_list_tgn_mguP_kernel(
         bz_neg = keep.tile([P, TILES], F32, name="bz_neg")
         nc.scalar.copy(bn_sb[:], turned_bias[:, TILES : 2 * TILES])
         nc.scalar.activation(bz_neg[:], turned_bias[:, 0:TILES], ACT.Copy, scale=-1.0)
+        bz_sb = keep.tile([P, TILES], F32, name="bz_sb")
+        nc.scalar.copy(bz_sb[:], turned_bias[:, 0:TILES])
         wgo_turned = keep.tile([P, TILES], F32, name="wgo_turned")
         nc.scalar.copy(wgo_turned[:], turned_bias[:, 2 * TILES : 3 * TILES])
 
@@ -223,6 +225,11 @@ def tile_list_tgn_mguP_kernel(
                 passes(hn[half], "un", k, half, True, True)
                 nc.scalar.activation(stay[:, COLS * half : COLS * (half + 1)], sz[:], ACT.Sigmoid,
                                      bias=bz_neg[:, k : k + 1], scale=-1.0)
+                if k >= FIRST_SHARED and half:
+                    factors = ring.tile([P, 2, COLS], F32, name="factors", tag="factors", bufs=2, align_bytes=64)
+                    nc.scalar.activation(factors[:, 0, :], sz[:], ACT.Sigmoid, bias=bz_sb[:, k : k + 1])
+                    nc.scalar.copy(factors[:, 1, :], hn[half][:])
+                    hn[half] = factors
             for half in range(HALVES):
                 xn.append(bank("xn"))
                 passes(xn[half], "wn", k, half, True, True)
@@ -236,11 +243,14 @@ def tile_list_tgn_mguP_kernel(
         def candidate(k, stay, hn, xn):
             cand = keep.tile([P, J], F32, name="cand", tag="cand%d" % (2 - k % 2 if k else 0), align_bytes=64)
             gated = spare[k]
-            for half in range(HALVES):
+            for half in range(1 if k >= FIRST_SHARED else HALVES):
                 cols = slice(COLS * half, COLS * (half + 1))
                 nc.vector.scalar_tensor_tensor(gated[:, cols], stay[:, cols], 1.0, hn[half][:], ALU.subtract, ALU.mult)
             if k >= FIRST_SHARED:
-                nc.gpsimd.tensor_tensor(rows[k - 2], xn[:], gated, ALU.subtract)
+                total = rows[k - 2]
+                nc.gpsimd.tensor_tensor(total[:, COLS:J], hn[1][:, 0, :], hn[1][:, 1, :], ALU.mult)
+                nc.gpsimd.tensor_tensor(total[:, COLS:J], total[:, COLS:J], xn[:, COLS:J], ALU.add)
+                nc.gpsimd.tensor_tensor(total[:, 0:COLS], xn[:, 0:COLS], gated[:, 0:COLS], ALU.subtract)
                 return cand
             for half in range(HALVES):
                 cols = slice(COLS * half, COLS * (half + 1))
@@ -354,6 +364,9 @@ def tile_list_tgn_mguP_kernel(
         def hand_out(k):
             page = pages[k % PAGES]
             nc.sync.dma_start(out_0[P * k : P * (k + 1), :], page[:])
+
+        def prepare(k):
+            page = pages[k % PAGES]
             if k == PACK:
                 read_back(0)
                 read_back(1)
@@ -391,6 +404,10 @@ def tile_list_tgn_mguP_kernel(
             if i <= LAST:
                 blended[i] = weigh(i, rows[i], mid)
             hand_out(i - 1)
+            if i == LAST - 1:
+                prepare(PACK)
+            if i >= LAST - 1:
+                prepare(i - 1)
 
         y_sc = keep.tile([P, T + COLS], U8, name="y_sc", tag="wgo", align_bytes=64)
         codes = big([P, T], U32, "y_codes")

@@ -46,15 +46,14 @@ def tile_list_tgn_mguP_kernel(
         def big(shape, dtype, name):
             return ring.tile(shape, dtype, name=name, tag="big", bufs=4, align_bytes=64)
 
-        def bank_pair(n):
-            return psum.tile([P, 2, COLS], F32, name="back", tag="back%d" % n, bufs=1, offset=2 * n * BANK)[:, 0, :]
+        def bank(n, first=None, last=None):
+            first, last = n if first is None else first, n if last is None else last
+            tile = psum.tile([P, last - first + 1, COLS], F32, name="bank", tag="bank%d_%d" % (first, last), bufs=1,
+                             offset=first * BANK)
+            return tile[:, n - first, :]
 
         def woven_tile(name):
             return ring.tile([P, COLS, PACK], BF16, name=name, tag="woven", bufs=3, align_bytes=64)
-
-        def bank(tag):
-            return psum.tile([P, COLS], F32, name=tag, tag=tag, bufs=2 if tag == "sz" else 3,
-                             offset={"sz": 0, "hn": 2, "xn": 5}[tag] * BANK)
 
         offsets = keep.tile([P, J // 16], U16, name="offsets")
         nc.sync.dma_start(offsets[:], offs)
@@ -142,7 +141,7 @@ def tile_list_tgn_mguP_kernel(
         for k in range(3, TILES):
             state[k] = load_state(k)
 
-        turned_bias = bank("sz")
+        turned_bias = bank(7)
         nc.tensor.transpose(turned_bias[:, 0:P], bias_rows[:], identity[:])
         bn_sb = keep.tile([P, TILES], F32, name="bias")
         bz_neg = keep.tile([P, TILES], F32, name="bz_neg")
@@ -200,7 +199,7 @@ def tile_list_tgn_mguP_kernel(
                 else:
                     plane, moving_sc = planes[n][QUADS:P, a, cols], x_sc[half]
                     moving = x_codes[half][:, a, :].bitcast(FP8X4)
-                nc.tensor.matmul_mx(out=acc[:], lhsT=weights[name, k][:, a, :].bitcast(FP8X4), lhsT_scale=plane,
+                nc.tensor.matmul_mx(out=acc, lhsT=weights[name, k][:, a, :].bitcast(FP8X4), lhsT_scale=plane,
                                     rhs=moving, rhs_scale=moving_sc[:, a, :],
                                     start=opens and a == 0, stop=closes and a == PASSES - 1)
 
@@ -215,29 +214,30 @@ def tile_list_tgn_mguP_kernel(
             if k == 0:
                 stay = first_tile[:, 0:J]
             else:
-                stay = ring.tile([P, J], F32, name="stay", tag="stay", bufs=3, align_bytes=64)[:]
-            hn, xn = [], []
+                stay = ring.tile([P, J], F32, name="stay", tag="stay", bufs=4, align_bytes=64)[:]
+            shared = k >= FIRST_SHARED
+            hn = [bank(n) for n in ((2 - 2 * (k % 2), 3) if shared else ((0, 3), (2, 0), (3, 2))[k])]
+            xn = [bank(n) for n in ((5, 6) if shared else ((5, 6), (7, 5), (6, 7))[k])]
             for half in range(HALVES):
-                sz = bank("sz")
-                hn.append(bank("hn"))
+                sz = bank(1 + 3 * half)
                 passes(sz, "uz", k, half, True, False)
                 passes(sz, "wz", k, half, False, True)
-                passes(hn[half], "un", k, half, True, True)
-                nc.scalar.activation(stay[:, COLS * half : COLS * (half + 1)], sz[:], ACT.Sigmoid,
+                if not shared:
+                    passes(hn[half], "un", k, half, True, True)
+                nc.scalar.activation(stay[:, COLS * half : COLS * (half + 1)], sz, ACT.Sigmoid,
                                      bias=bz_neg[:, k : k + 1], scale=-1.0)
-                if k >= FIRST_SHARED and half:
-                    factors = ring.tile([P, 2, COLS], F32, name="factors", tag="factors", bufs=2, align_bytes=64)
-                    nc.scalar.activation(factors[:, 0, :], sz[:], ACT.Sigmoid, bias=bz_sb[:, k : k + 1])
-                    nc.scalar.copy(factors[:, 1, :], hn[half][:])
-                    hn[half] = factors
+            if shared:
+                factors = ring.tile([P, 2, COLS], F32, name="factors", tag="factors", bufs=2, align_bytes=64)
+                nc.scalar.activation(factors[:, 0, :], sz, ACT.Sigmoid, bias=bz_sb[:, k : k + 1])
             for half in range(HALVES):
-                xn.append(bank("xn"))
                 passes(xn[half], "wn", k, half, True, True)
-            if k >= FIRST_SHARED:
+            if shared:
                 emptied = keep.tile([P, J], F32, name="xn_sb", tag="cand%d" % (3 * (k % 2)), align_bytes=64)
                 for half in range(HALVES):
-                    nc.scalar.copy(emptied[:, COLS * half : COLS * (half + 1)], xn[half][:])
-                xn = emptied
+                    nc.scalar.copy(emptied[:, COLS * half : COLS * (half + 1)], xn[half])
+                    passes(hn[half], "un", k, half, True, True)
+                nc.scalar.copy(factors[:, 1, :], hn[1])
+                xn, hn[1] = emptied, factors
             return stay, hn, xn
 
         def candidate(k, stay, hn, xn):
@@ -245,7 +245,7 @@ def tile_list_tgn_mguP_kernel(
             gated = spare[k]
             for half in range(1 if k >= FIRST_SHARED else HALVES):
                 cols = slice(COLS * half, COLS * (half + 1))
-                nc.vector.scalar_tensor_tensor(gated[:, cols], stay[:, cols], 1.0, hn[half][:], ALU.subtract, ALU.mult)
+                nc.vector.scalar_tensor_tensor(gated[:, cols], stay[:, cols], 1.0, hn[half], ALU.subtract, ALU.mult)
             if k >= FIRST_SHARED:
                 total = rows[k - 2]
                 nc.gpsimd.tensor_tensor(total[:, COLS:J], hn[1][:, 0, :], hn[1][:, 1, :], ALU.mult)
@@ -254,7 +254,7 @@ def tile_list_tgn_mguP_kernel(
                 return cand
             for half in range(HALVES):
                 cols = slice(COLS * half, COLS * (half + 1))
-                nc.vector.scalar_tensor_tensor(cand[:, cols], gated[:, cols], -1.0, xn[half][:], ALU.mult, ALU.add)
+                nc.vector.scalar_tensor_tensor(cand[:, cols], gated[:, cols], -1.0, xn[half], ALU.mult, ALU.add)
                 nc.scalar.activation(cand[:, cols], cand[:, cols], ACT.Tanh, bias=bn_sb[:, k : k + 1])
             return cand
 
@@ -262,35 +262,42 @@ def tile_list_tgn_mguP_kernel(
             if k == 0:
                 rows = first_tile[:, J : 2 * J]
             else:
-                tag = "second_tile" if k == 1 else handed_on(k - 2 if k < LAST else k - 4)
-                both = keep.tile([P, 2 * J], F32, name="rows", tag=tag, align_bytes=64)
-                rows, spare[k + 2] = both[:, 0:J], both[:, J : 2 * J]
+                tag = "second_tile" if k == 1 else handed_on(k - 2)
+                width = J + COLS if k + 2 <= LAST else J
+                both = keep.tile([P, width], F32, name="rows", tag=tag, align_bytes=64)
+                rows = both[:, 0:J]
+                if k + 2 <= LAST:
+                    spare[k + 2] = both[:, J:width]
             nc.vector.tensor_tensor(rows, state[k][:].indirect(offsets[:]), cand[:], ALU.subtract)
             return rows
 
         def blend(k, rows, stay, cand):
             mid = ring.tile([P, J], F32, name="mid", tag="mid", bufs=1)
+            if k >= LAST - 1:
+                for half in (1, 0):
+                    cols = slice(COLS * half, COLS * (half + 1))
+                    nc.gpsimd.tensor_tensor(mid[:, cols], rows[:, cols], stay[:, cols], ALU.mult)
+                return mid
             nc.gpsimd.tensor_tensor(mid[:], rows, stay, ALU.mult)
-            if k in (0, LAST):
+            if k == 0:
                 nc.gpsimd.tensor_tensor(mid[:], mid[:], cand[:], ALU.add)
             return mid
 
         def weigh(k, rows, mid):
-            if k == LAST:
-                return mid[:]
             into = rows
-            if k + 3 <= LAST:
+            if k + 2 <= LAST:
                 into = keep.tile([P, J], F32, name="weighed", tag=handed_on(k), align_bytes=64)[:]
             if k == 0:
                 nc.vector.tensor_tensor(into, mid[:], wgo_sb[:], ALU.mult)
                 return into
             halves = range(HALVES)
-            if k == LAST - 1:
+            weighed = cands[k]
+            if k >= LAST - 1:
                 halves = (1,)
                 nc.gpsimd.tensor_tensor(mid[:, 0:COLS], mid[:, 0:COLS], cands[k][:, 0:COLS], ALU.add)
                 nc.gpsimd.tensor_tensor(into[:, 0:COLS], mid[:, 0:COLS], wgo_sb[:, 0:COLS], ALU.mult)
             for half in halves:
-                turned = bank("xn")
+                turned = bank(5 if k == LAST else 5 + half)
                 for n, term in enumerate((cands[k], mid)):
                     for b in range(QUADS):
                         first = COLS * half + P * b
@@ -299,38 +306,37 @@ def tile_list_tgn_mguP_kernel(
                                          start=n == 0 and b == 0, stop=n == 1 and b == QUADS - 1)
                 for b in range(QUADS):
                     block = QUADS * half + b
-                    nc.scalar.activation(mid[:, P * block : P * (block + 1)], turned[:, P * b : P * (b + 1)],
+                    nc.scalar.activation(weighed[:, P * block : P * (block + 1)], turned[:, P * b : P * (b + 1)],
                                          ACT.Copy, scale=wgo_turned[:, block : block + 1])
-            if k + 2 <= LAST:
-                nc.scalar.activation(cands[k + 2][:], rows, ACT.Tanh, bias=bn_sb[:, k + 2 : k + 3])
             for half in halves:
-                back = bank_pair(half) if k == PACK + 1 else bank("xn")
+                if k == LAST - 1:
+                    back = bank(5, 0, 5)
+                elif k == LAST:
+                    back = bank(4, 4, 7)
+                elif half:
+                    back = bank(4, 3, 6)
+                else:
+                    back = bank(1, 0, 2) if k == PACK + 1 else bank(1, 1 - k % 2, 2 - k % 2)
                 for b in range(QUADS):
                     first = COLS * half + P * b
-                    nc.tensor.transpose(back[:, P * b : P * (b + 1)], mid[:, first : first + P], identity[:])
-                nc.scalar.copy(into[:, COLS * half : COLS * (half + 1)], back[:])
+                    nc.tensor.transpose(back[:, P * b : P * (b + 1)], weighed[:, first : first + P], identity[:])
+                nc.scalar.copy(into[:, COLS * half : COLS * (half + 1)], back)
+            if k + 2 <= LAST:
+                nc.scalar.activation(cands[k + 2][:], rows, ACT.Tanh, bias=bn_sb[:, k + 2 : k + 3])
             return into
 
         def scatter(k, rows):
-            window = pages[k % PAGES][:].indirect(offsets[:])
-            if k == LAST:
-                nc.vector.tensor_tensor(window, rows, wgo_sb[:], ALU.mult)
-            else:
-                nc.vector.tensor_copy(window, rows)
+            nc.vector.tensor_copy(pages[k % PAGES][:].indirect(offsets[:]), rows)
 
         woven = {}
 
         def read_back(c):
             again = keep.tile([P, PACK, COLS], F32, name="again", align_bytes=64,
-                              tag=("state0", "state0", "third_x", "second_tile")[c])
+                              tag=("state0", "third_x", "second_tile", "state0")[c])
             rows = out_0[0:PASS, COLS * c : COLS * (c + 1)]
             nc.sync.dma_start(again[:], rows.rearrange("(p i) c -> p i c", i=PACK))
-            if c == 1:
-                woven[c] = woven_tile("y_rounded")
-            elif c == QUADS - 1:
-                woven[c] = keep.tile([P, COLS, PACK], BF16, name="y_rounded", tag="tab_sc", align_bytes=64)
-            else:
-                woven[c] = ring.tile([P, COLS, PACK], BF16, name="y_rounded", tag="stay", bufs=3, align_bytes=64)
+            woven[c] = keep.tile([P, COLS, PACK], BF16, name="y_rounded", align_bytes=64,
+                                 tag=(handed_on(PACK - 1), "cand2", "cand1", "tab_sc")[c])
             nc.scalar.copy(woven[c][:].rearrange("p (c n) i -> p c i n", n=LINE // 4),
                            again[:].rearrange("p i (c n) -> p c i n", n=LINE // 4))
 
@@ -342,17 +348,17 @@ def tile_list_tgn_mguP_kernel(
                                      align_bytes=64)
             words = woven[k][:].rearrange("p c i -> p (c i)").bitcast(F32)
             rounded = keep.tile([P, QUADS, COLS], BF16, name="rounded", align_bytes=64,
-                                tag="tab_sc" if k == PACK else "rounded")
+                                tag="rounded" if k % 2 else "tab_sc")
+            base = 0 if k < LAST - 1 else QUADS
             for c in range(QUADS):
-                turned = psum.tile([P, COLS], F32, name="turned", tag="turned%d" % c, bufs=1,
-                                   offset=(2 * (c % 2) + c // 2) * BANK)[:]
+                turned = bank(base + 2 * (c % 2) + c // 2)
                 for q in range(QUADS):
                     first = COLS * q + P * c
                     nc.tensor.transpose(turned[:, P * q : P * (q + 1)], page[:, first : first + P], identity[:])
                 nc.scalar.copy(rounded[:, c, :].rearrange("t (u m e) -> t u m e", u=2, e=2),
                                turned.rearrange("t (m u e) -> t u m e", u=2, e=2))
             for pair in range(2):
-                back = bank_pair(pair)
+                back = bank(base + 2 * pair, base + 2 * pair, base + 2 * pair + 1)
                 for c in range(2):
                     for u in range(2):
                         first = P * (2 * c + u)
@@ -364,16 +370,6 @@ def tile_list_tgn_mguP_kernel(
         def hand_out(k):
             page = pages[k % PAGES]
             nc.sync.dma_start(out_0[P * k : P * (k + 1), :], page[:])
-
-        def prepare(k):
-            page = pages[k % PAGES]
-            if k == PACK:
-                read_back(0)
-                read_back(1)
-            if k >= PACK:
-                turn_twice(k, page)
-            if k in (PACK, PACK + 1):
-                read_back(LAST - k)
 
         first_gated = keep.tile([P, J], F32, name="first_gated", tag="last_x", align_bytes=64)
         spare[0] = first_gated[:]
@@ -404,12 +400,15 @@ def tile_list_tgn_mguP_kernel(
             if i <= LAST:
                 blended[i] = weigh(i, rows[i], mid)
             hand_out(i - 1)
-            if i == LAST - 1:
-                prepare(PACK)
-            if i >= LAST - 1:
-                prepare(i - 1)
+            if i > PACK:
+                turn_twice(i - 1, pages[(i - 1) % PAGES])
+            if PACK < i < LAST:
+                read_back(i - PACK - 1)
+            if i == LAST:
+                read_back(2)
+                read_back(3)
 
-        y_sc = keep.tile([P, T + COLS], U8, name="y_sc", tag="wgo", align_bytes=64)
+        y_sc = keep.tile([P, T + COLS], U8, name="y_sc", tag=handed_on(LAST - 2), align_bytes=64)
         codes = big([P, T], U32, "y_codes")
         words = out_1[0].rearrange("p t b -> p (t b)").bitcast(I32)
         for c in range(QUADS):

@@ -141,7 +141,7 @@ def tile_list_tgn_mguP_kernel(
         for k in range(3, TILES):
             state[k] = load_state(k)
 
-        turned_bias = bank(7)
+        turned_bias = bank(1)
         nc.tensor.transpose(turned_bias[:, 0:P], bias_rows[:], identity[:])
         bn_sb = keep.tile([P, TILES], F32, name="bias")
         bz_neg = keep.tile([P, TILES], F32, name="bz_neg")
@@ -216,32 +216,43 @@ def tile_list_tgn_mguP_kernel(
             else:
                 stay = ring.tile([P, J], F32, name="stay", tag="stay", bufs=4, align_bytes=64)[:]
             shared = k >= FIRST_SHARED
-            hn = [bank(n) for n in ((2 - 2 * (k % 2), 3) if shared else ((0, 3), (2, 0), (3, 2))[k])]
-            xn = [bank(n) for n in ((5, 6) if shared else ((5, 6), (7, 5), (6, 7))[k])]
+            if shared:
+                late = psum.tile([P, 2, COLS], F32, name="late", tag="late%d" % (k % 2), bufs=1,
+                                 offset=(6 - k % 2) * BANK)
+                hn, xn = [bank(5 + 2 * (k % 2)), late[:, 0, :]], [bank(4), late[:, 1, :]]
+                passes(hn[0], "un", k, 0, True, True)
+            else:
+                hn = [bank(n) for n in ((5, 6), (7, 5), (6, 7))[k]]
+                xn = [bank(n) for n in ((4, 3), (1, 4), (3, 1))[k]]
             for half in range(HALVES):
-                sz = bank(1 + 3 * half)
+                sz = bank(2 * half)
                 passes(sz, "uz", k, half, True, False)
                 passes(sz, "wz", k, half, False, True)
                 if not shared:
                     passes(hn[half], "un", k, half, True, True)
                 nc.scalar.activation(stay[:, COLS * half : COLS * (half + 1)], sz, ACT.Sigmoid,
                                      bias=bz_neg[:, k : k + 1], scale=-1.0)
-            if shared:
-                factors = ring.tile([P, 2, COLS], F32, name="factors", tag="factors", bufs=2, align_bytes=64)
-                nc.scalar.activation(factors[:, 0, :], sz, ACT.Sigmoid, bias=bz_sb[:, k : k + 1])
-            for half in range(HALVES):
-                passes(xn[half], "wn", k, half, True, True)
-            if shared:
-                emptied = keep.tile([P, J], F32, name="xn_sb", tag="cand%d" % (3 * (k % 2)), align_bytes=64)
+            if not shared:
                 for half in range(HALVES):
-                    nc.scalar.copy(emptied[:, COLS * half : COLS * (half + 1)], xn[half])
-                    passes(hn[half], "un", k, half, True, True)
-                nc.scalar.copy(factors[:, 1, :], hn[1])
-                xn, hn[1] = emptied, factors
-            return stay, hn, xn
+                    passes(xn[half], "wn", k, half, True, True)
+                return stay, hn, xn
+            factors = ring.tile([P, 2, COLS], F32, name="factors", tag="factors", bufs=2, align_bytes=64)
+            emptied = keep.tile([P, J], F32, name="xn_sb", tag="cand%d" % (3 * (k % 2)), align_bytes=64)
+            nc.scalar.activation(factors[:, 0, :], sz, ACT.Sigmoid, bias=bz_sb[:, k : k + 1])
+            passes(xn[0], "wn", k, 0, True, True)
+            nc.scalar.copy(emptied[:, 0:COLS], xn[0])
+            passes(hn[1], "un", k, 1, True, True)
+            passes(xn[1], "wn", k, 1, True, True)
+            nc.scalar.copy(factors[:, 1, :], hn[1])
+            nc.scalar.copy(emptied[:, COLS:J], xn[1])
+            return stay, [hn[0], factors], emptied
 
         def candidate(k, stay, hn, xn):
-            cand = keep.tile([P, J], F32, name="cand", tag="cand%d" % (2 - k % 2 if k else 0), align_bytes=64)
+            width = J + COLS if FIRST_SHARED <= k + 1 <= LAST else J
+            both = keep.tile([P, width], F32, name="cand", tag="cand%d" % (2 - k % 2 if k else 0), align_bytes=64)
+            cand = both[:, 0:J]
+            if width > J:
+                spare[k + 1] = both[:, J:width]
             gated = spare[k]
             for half in range(1 if k >= FIRST_SHARED else HALVES):
                 cols = slice(COLS * half, COLS * (half + 1))
@@ -263,12 +274,8 @@ def tile_list_tgn_mguP_kernel(
                 rows = first_tile[:, J : 2 * J]
             else:
                 tag = "second_tile" if k == 1 else handed_on(k - 2)
-                width = J + COLS if k + 2 <= LAST else J
-                both = keep.tile([P, width], F32, name="rows", tag=tag, align_bytes=64)
-                rows = both[:, 0:J]
-                if k + 2 <= LAST:
-                    spare[k + 2] = both[:, J:width]
-            nc.vector.tensor_tensor(rows, state[k][:].indirect(offsets[:]), cand[:], ALU.subtract)
+                rows = keep.tile([P, J], F32, name="rows", tag=tag, align_bytes=64)[:]
+            nc.vector.tensor_tensor(rows, state[k][:].indirect(offsets[:]), cand, ALU.subtract)
             return rows
 
         def blend(k, rows, stay, cand):
@@ -280,7 +287,7 @@ def tile_list_tgn_mguP_kernel(
                 return mid
             nc.gpsimd.tensor_tensor(mid[:], rows, stay, ALU.mult)
             if k == 0:
-                nc.gpsimd.tensor_tensor(mid[:], mid[:], cand[:], ALU.add)
+                nc.gpsimd.tensor_tensor(mid[:], mid[:], cand, ALU.add)
             return mid
 
         def weigh(k, rows, mid):
@@ -297,7 +304,10 @@ def tile_list_tgn_mguP_kernel(
                 nc.gpsimd.tensor_tensor(mid[:, 0:COLS], mid[:, 0:COLS], cands[k][:, 0:COLS], ALU.add)
                 nc.gpsimd.tensor_tensor(into[:, 0:COLS], mid[:, 0:COLS], wgo_sb[:, 0:COLS], ALU.mult)
             for half in halves:
-                turned = bank(5 if k == LAST else 5 + half)
+                if k >= LAST - 1:
+                    turned = bank(5 if k == LAST else 6)
+                else:
+                    turned = bank(3, 3, 4) if half else bank(1, 0, 2)
                 for n, term in enumerate((cands[k], mid)):
                     for b in range(QUADS):
                         first = COLS * half + P * b
@@ -314,31 +324,34 @@ def tile_list_tgn_mguP_kernel(
                 elif k == LAST:
                     back = bank(4, 4, 7)
                 elif half:
-                    back = bank(4, 3, 6)
+                    back = bank(3, 3, 6) if k == PACK + 1 else bank(3)
                 else:
-                    back = bank(1, 0, 2) if k == PACK + 1 else bank(1, 1 - k % 2, 2 - k % 2)
+                    back = bank(1, 0, 2) if k == PACK + 1 else bank(1)
                 for b in range(QUADS):
                     first = COLS * half + P * b
                     nc.tensor.transpose(back[:, P * b : P * (b + 1)], weighed[:, first : first + P], identity[:])
                 nc.scalar.copy(into[:, COLS * half : COLS * (half + 1)], back)
             if k + 2 <= LAST:
-                nc.scalar.activation(cands[k + 2][:], rows, ACT.Tanh, bias=bn_sb[:, k + 2 : k + 3])
+                nc.scalar.activation(cands[k + 2], rows, ACT.Tanh, bias=bn_sb[:, k + 2 : k + 3])
             return into
 
         def scatter(k, rows):
             nc.vector.tensor_copy(pages[k % PAGES][:].indirect(offsets[:]), rows)
 
+        again = {}
         woven = {}
 
         def read_back(c):
-            again = keep.tile([P, PACK, COLS], F32, name="again", align_bytes=64,
-                              tag=("state0", "third_x", "second_tile", "state0")[c])
+            again[c] = keep.tile([P, PACK, COLS], F32, name="again", align_bytes=64,
+                                 tag=("state0", "third_x", "second_tile", "again")[c])
             rows = out_0[0:PASS, COLS * c : COLS * (c + 1)]
-            nc.sync.dma_start(again[:], rows.rearrange("(p i) c -> p i c", i=PACK))
+            nc.sync.dma_start(again[c][:], rows.rearrange("(p i) c -> p i c", i=PACK))
+
+        def round_back(c):
             woven[c] = keep.tile([P, COLS, PACK], BF16, name="y_rounded", align_bytes=64,
                                  tag=(handed_on(PACK - 1), "cand2", "cand1", "tab_sc")[c])
             nc.scalar.copy(woven[c][:].rearrange("p (c n) i -> p c i n", n=LINE // 4),
-                           again[:].rearrange("p i (c n) -> p c i n", n=LINE // 4))
+                           again[c][:].rearrange("p i (c n) -> p c i n", n=LINE // 4))
 
         def turn_twice(k, page):
             if k < LAST - 1:
@@ -400,13 +413,16 @@ def tile_list_tgn_mguP_kernel(
             if i <= LAST:
                 blended[i] = weigh(i, rows[i], mid)
             hand_out(i - 1)
+            if i == PACK:
+                for c in range(QUADS):
+                    read_back(c)
             if i > PACK:
                 turn_twice(i - 1, pages[(i - 1) % PAGES])
             if PACK < i < LAST:
-                read_back(i - PACK - 1)
+                round_back(i - PACK - 1)
             if i == LAST:
-                read_back(2)
-                read_back(3)
+                round_back(2)
+                round_back(3)
 
         y_sc = keep.tile([P, T + COLS], U8, name="y_sc", tag=handed_on(LAST - 2), align_bytes=64)
         codes = big([P, T], U32, "y_codes")

@@ -322,7 +322,7 @@ def tile_list_tgn_mguP_kernel(
                 if k == LAST - 1:
                     back = bank(5, 0, 5)
                 elif k == LAST:
-                    back = bank(4, 4, 7)
+                    back = bank(4, 0, 7)
                 elif half:
                     back = bank(3, 3, 6) if k == PACK + 1 else bank(3)
                 else:
@@ -380,6 +380,18 @@ def tile_list_tgn_mguP_kernel(
                 nc.scalar.copy(words[:, COLS * pair : COLS * (pair + 1)].rearrange("m (c t u) -> m c t u", c=2, u=2),
                                back.rearrange("m (c u t) -> m c t u", c=2, u=2))
 
+        def quantise_y(codes, scales, n):
+            nc.vector.quantize_mx(out=codes.bitcast(FP8X4), scales=scales, in_=woven[n][:].rearrange("p c i -> p (c i)"))
+
+        def store_tiles(first, count):
+            codes = big([P, count, COLS], U32, "y_codes")
+            words = out_1[1].rearrange("(k p) t b -> p k (t b)", p=QUAD).bitcast(I32)
+            for row in range(count):
+                quantise_y(codes[:, row, :], late_sc[QUADS * (first + row) : P, :], PACK + first + row)
+            for q in (0, 2, 1, 3):
+                nc.sync.dma_start(words[:, first : first + count, COLS * q : COLS * (q + 1)],
+                                  codes[QUAD * q : QUAD * (q + 1), :, :].bitcast(I32))
+
         def hand_out(k):
             page = pages[k % PAGES]
             nc.sync.dma_start(out_0[P * k : P * (k + 1), :], page[:])
@@ -407,6 +419,9 @@ def tile_list_tgn_mguP_kernel(
                 mid = blend(i, rows[i], gates[i][0], cands[i])
             if i + 2 <= LAST:
                 cands[i + 2] = candidate(i + 2, *gates[i + 2])
+            if i == TILES:
+                late_sc = keep.tile([P, COLS], U8, name="late_sc", tag=handed_on(LAST - 3), align_bytes=64)
+                store_tiles(0, 2)
             scatter(i - 1, blended[i - 1])
             if i + 3 <= LAST:
                 gates[i + 3] = gate(i + 3)
@@ -424,28 +439,16 @@ def tile_list_tgn_mguP_kernel(
                 round_back(2)
                 round_back(3)
 
-        y_sc = keep.tile([P, T + COLS], U8, name="y_sc", tag=handed_on(LAST - 2), align_bytes=64)
+        store_tiles(2, 1)
+        early_sc = keep.tile([P, COLS], U8, name="early_sc", tag=handed_on(LAST - 2), align_bytes=64)
         codes = big([P, T], U32, "y_codes")
-        words = out_1[0].rearrange("p t b -> p (t b)").bitcast(I32)
         for c in range(QUADS):
-            cols = slice(COLS * c, COLS * (c + 1))
-            nc.vector.quantize_mx(out=codes[:, cols].bitcast(FP8X4), scales=y_sc[:, cols],
-                                  in_=woven[c][:].rearrange("p c i -> p (c i)"))
-        nc.sync.dma_start(words, codes[:].bitcast(I32))
-        for q in range(QUADS):
-            nc.sync.dma_start(out_2[0, QUADS * q : QUADS * (q + 1), :].bitcast(I32),
-                              y_sc[QUAD * q : QUAD * q + QUADS, 0:T].bitcast(I32))
-        codes = big([P, PACK, COLS], U32, "y_codes")
-        words = out_1[1].rearrange("(k p) t b -> p k (t b)", p=QUAD).bitcast(I32)
-        stored = 0
-        for row in range(PACK):
-            nc.vector.quantize_mx(out=codes[:, row, :].bitcast(FP8X4), scales=y_sc[QUADS * row : P, T : T + COLS],
-                                  in_=woven[PACK + row][:].rearrange("p c i -> p (c i)"))
-            if row >= PACK - 2:
-                for q in range(QUADS):
-                    nc.sync.dma_start(words[:, stored : row + 1, COLS * q : COLS * (q + 1)],
-                                      codes[QUAD * q : QUAD * (q + 1), stored : row + 1, :].bitcast(I32))
-                stored = row + 1
-        for q in range(QUADS):
+            quantise_y(codes[:, COLS * c : COLS * (c + 1)], early_sc[QUADS * c : P, :], c)
+        nc.sync.dma_start(out_1[0].rearrange("p t b -> p (t b)").bitcast(I32), codes[:].bitcast(I32))
+        for q in (0, 2, 1, 3):
+            rows_q = out_2[0, QUADS * q : QUADS * (q + 1), :].rearrange("r (c t) -> c r t", c=QUADS)
+            nc.sync.dma_start(rows_q.bitcast(I32), early_sc[QUAD * q : QUAD * q + QUADS * QUADS, :].bitcast(I32))
+        store_tiles(3, 1)
+        for q in (0, 2, 1, 3):
             nc.sync.dma_start(out_2[1, :, COLS * q : COLS * (q + 1)].bitcast(I32),
-                              y_sc[QUAD * q : QUAD * q + QUADS * PACK, T : T + COLS].bitcast(I32))
+                              late_sc[QUAD * q : QUAD * q + QUADS * PACK, :].bitcast(I32))

@@ -30,6 +30,7 @@ LAST = TILES - 1
 LINE = 16
 BANK = 2048
 PAGES = 3
+SPLIT = 256
 FIRST_SHARED = 3
 
 
@@ -220,7 +221,9 @@ def tile_list_tgn_mguP_kernel(
                 late = psum.tile([P, 2, COLS], F32, name="late", tag="late%d" % (k % 2), bufs=1,
                                  offset=(6 - k % 2) * BANK)
                 hn, xn = [bank(5 + 2 * (k % 2)), late[:, 0, :]], [bank(4), late[:, 1, :]]
+                factors = ring.tile([P, 2, J - SPLIT], F32, name="factors", tag="factors", bufs=2, align_bytes=64)
                 passes(hn[0], "un", k, 0, True, True)
+                nc.scalar.activation(factors[:, 1, 0 : COLS - SPLIT], hn[0][:, SPLIT:COLS], ACT.Copy, scale=-1.0)
             else:
                 hn = [bank(n) for n in ((5, 6), (7, 5), (6, 7))[k]]
                 xn = [bank(n) for n in ((4, 3), (1, 4), (3, 1))[k]]
@@ -232,37 +235,39 @@ def tile_list_tgn_mguP_kernel(
                     passes(hn[half], "un", k, half, True, True)
                 nc.scalar.activation(stay[:, COLS * half : COLS * (half + 1)], sz, ACT.Sigmoid,
                                      bias=bz_neg[:, k : k + 1], scale=-1.0)
+                if shared:
+                    first = max(SPLIT, COLS * half)
+                    nc.scalar.activation(factors[:, 0, first - SPLIT : COLS * (half + 1) - SPLIT],
+                                         sz[:, first - COLS * half : COLS], ACT.Sigmoid, bias=bz_sb[:, k : k + 1])
             if not shared:
                 for half in range(HALVES):
                     passes(xn[half], "wn", k, half, True, True)
                 return stay, hn, xn
-            factors = ring.tile([P, 2, COLS], F32, name="factors", tag="factors", bufs=2, align_bytes=64)
             emptied = keep.tile([P, J], F32, name="xn_sb", tag="cand%d" % (3 * (k % 2)), align_bytes=64)
-            nc.scalar.activation(factors[:, 0, :], sz, ACT.Sigmoid, bias=bz_sb[:, k : k + 1])
             passes(xn[0], "wn", k, 0, True, True)
             nc.scalar.copy(emptied[:, 0:COLS], xn[0])
             passes(hn[1], "un", k, 1, True, True)
             passes(xn[1], "wn", k, 1, True, True)
-            nc.scalar.copy(factors[:, 1, :], hn[1])
+            nc.scalar.activation(factors[:, 1, COLS - SPLIT : J - SPLIT], hn[1], ACT.Copy, scale=-1.0)
             nc.scalar.copy(emptied[:, COLS:J], xn[1])
             return stay, [hn[0], factors], emptied
 
         def candidate(k, stay, hn, xn):
-            width = J + COLS if FIRST_SHARED <= k + 1 <= LAST else J
+            width = 2 * J if FIRST_SHARED <= k + 1 <= LAST else J
             both = keep.tile([P, width], F32, name="cand", tag="cand%d" % (2 - k % 2 if k else 0), align_bytes=64)
             cand = both[:, 0:J]
             if width > J:
                 spare[k + 1] = both[:, J:width]
             gated = spare[k]
-            for half in range(1 if k >= FIRST_SHARED else HALVES):
+            if k >= FIRST_SHARED:
+                nc.vector.scalar_tensor_tensor(gated[:, 0:SPLIT], stay[:, 0:SPLIT], 1.0, hn[0][:, 0:SPLIT],
+                                               ALU.subtract, ALU.mult)
+                nc.gpsimd.tensor_tensor(gated[:, SPLIT:J], hn[1][:, 0, :], hn[1][:, 1, :], ALU.mult)
+                nc.gpsimd.tensor_tensor(rows[k - 2], xn[:], gated, ALU.subtract)
+                return cand
+            for half in range(HALVES):
                 cols = slice(COLS * half, COLS * (half + 1))
                 nc.vector.scalar_tensor_tensor(gated[:, cols], stay[:, cols], 1.0, hn[half], ALU.subtract, ALU.mult)
-            if k >= FIRST_SHARED:
-                total = rows[k - 2]
-                nc.gpsimd.tensor_tensor(total[:, COLS:J], hn[1][:, 0, :], hn[1][:, 1, :], ALU.mult)
-                nc.gpsimd.tensor_tensor(total[:, COLS:J], total[:, COLS:J], xn[:, COLS:J], ALU.add)
-                nc.gpsimd.tensor_tensor(total[:, 0:COLS], xn[:, 0:COLS], gated[:, 0:COLS], ALU.subtract)
-                return cand
             for half in range(HALVES):
                 cols = slice(COLS * half, COLS * (half + 1))
                 nc.vector.scalar_tensor_tensor(cand[:, cols], gated[:, cols], -1.0, xn[half], ALU.mult, ALU.add)
@@ -342,8 +347,11 @@ def tile_list_tgn_mguP_kernel(
         woven = {}
 
         def read_back(c):
-            again[c] = keep.tile([P, PACK, COLS], F32, name="again", align_bytes=64,
-                                 tag=("state0", "third_x", "second_tile", "again")[c])
+            if c == QUADS - 1:
+                again[c] = big([P, PACK, COLS], F32, "again")
+            else:
+                again[c] = keep.tile([P, PACK, COLS], F32, name="again", align_bytes=64,
+                                     tag=("state0", "third_x", "second_tile")[c])
             rows = out_0[0:PASS, COLS * c : COLS * (c + 1)]
             nc.sync.dma_start(again[c][:], rows.rearrange("(p i) c -> p i c", i=PACK))
 

@@ -30,7 +30,7 @@ LAST = TILES - 1
 LINE = 16
 BANK = 2048
 PAGES = 3
-SPLIT = 256
+SPLIT = 128
 FIRST_SHARED = 3
 
 

@@ -209,21 +209,25 @@ def tile_list_tgn_mguP_kernel(
         first_tile = keep.tile([P, 2 * J], F32, name="first_tile", tag="third_x", align_bytes=64)
 
         def handed_on(k):
-            return ("un%d", "uz%d")[k % 2] % (k + 2)
+            return ("un%d", "uz%d")[k % 2] % (k + 2) if k else "wz2"
+
+        def vector_columns(k):
+            return COLS if k == FIRST_SHARED else SPLIT
 
         def gate(k):
             if k == 0:
                 stay = first_tile[:, 0:J]
             else:
                 stay = ring.tile([P, J], F32, name="stay", tag="stay", bufs=4, align_bytes=64)[:]
-            shared = k >= FIRST_SHARED
+            shared, split = k >= FIRST_SHARED, vector_columns(k)
             if shared:
                 late = psum.tile([P, 2, COLS], F32, name="late", tag="late%d" % (k % 2), bufs=1,
                                  offset=(6 - k % 2) * BANK)
                 hn, xn = [bank(5 + 2 * (k % 2)), late[:, 0, :]], [bank(4), late[:, 1, :]]
-                factors = ring.tile([P, 2, J - SPLIT], F32, name="factors", tag="factors", bufs=2, align_bytes=64)
+                factors = ring.tile([P, 2, J - split], F32, name="factors", tag="factors", bufs=2, align_bytes=64)
                 passes(hn[0], "un", k, 0, True, True)
-                nc.scalar.activation(factors[:, 1, 0 : COLS - SPLIT], hn[0][:, SPLIT:COLS], ACT.Copy, scale=-1.0)
+                if split < COLS:
+                    nc.scalar.activation(factors[:, 1, 0 : COLS - split], hn[0][:, split:COLS], ACT.Copy, scale=-1.0)
             else:
                 hn = [bank(n) for n in ((5, 6), (7, 5), (6, 7))[k]]
                 xn = [bank(n) for n in ((4, 3), (1, 4), (3, 1))[k]]
@@ -233,22 +237,28 @@ def tile_list_tgn_mguP_kernel(
                 passes(sz, "wz", k, half, False, True)
                 if not shared:
                     passes(hn[half], "un", k, half, True, True)
+                if k == 0:
+                    passes(xn[half], "wn", k, half, True, True)
                 nc.scalar.activation(stay[:, COLS * half : COLS * (half + 1)], sz, ACT.Sigmoid,
                                      bias=bz_neg[:, k : k + 1], scale=-1.0)
-                if shared:
-                    first = max(SPLIT, COLS * half)
-                    nc.scalar.activation(factors[:, 0, first - SPLIT : COLS * (half + 1) - SPLIT],
+                if shared and split < COLS * (half + 1):
+                    first = max(split, COLS * half)
+                    nc.scalar.activation(factors[:, 0, first - split : COLS * (half + 1) - split],
                                          sz[:, first - COLS * half : COLS], ACT.Sigmoid, bias=bz_sb[:, k : k + 1])
             if not shared:
-                for half in range(HALVES):
+                for half in range(HALVES if k else 0):
                     passes(xn[half], "wn", k, half, True, True)
                 return stay, hn, xn
+            return stay, hn, xn, factors
+
+        def finish_gate(k, stay, hn, xn, factors):
+            split = vector_columns(k)
             emptied = keep.tile([P, J], F32, name="xn_sb", tag="cand%d" % (3 * (k % 2)), align_bytes=64)
             passes(xn[0], "wn", k, 0, True, True)
             nc.scalar.copy(emptied[:, 0:COLS], xn[0])
             passes(hn[1], "un", k, 1, True, True)
             passes(xn[1], "wn", k, 1, True, True)
-            nc.scalar.activation(factors[:, 1, COLS - SPLIT : J - SPLIT], hn[1], ACT.Copy, scale=-1.0)
+            nc.scalar.activation(factors[:, 1, COLS - split : J - split], hn[1], ACT.Copy, scale=-1.0)
             nc.scalar.copy(emptied[:, COLS:J], xn[1])
             return stay, [hn[0], factors], emptied
 
@@ -258,18 +268,21 @@ def tile_list_tgn_mguP_kernel(
             cand = both[:, 0:J]
             if width > J:
                 spare[k + 1] = both[:, J:width]
-            gated = spare[k]
+            gated, split = spare[k], vector_columns(k)
             if k >= FIRST_SHARED:
-                nc.vector.scalar_tensor_tensor(gated[:, 0:SPLIT], stay[:, 0:SPLIT], 1.0, hn[0][:, 0:SPLIT],
+                nc.vector.scalar_tensor_tensor(gated[:, 0:split], stay[:, 0:split], 1.0, hn[0][:, 0:split],
                                                ALU.subtract, ALU.mult)
-                nc.gpsimd.tensor_tensor(gated[:, SPLIT:J], hn[1][:, 0, :], hn[1][:, 1, :], ALU.mult)
+                nc.gpsimd.tensor_tensor(gated[:, split:J], hn[1][:, 0, :], hn[1][:, 1, :], ALU.mult)
                 nc.gpsimd.tensor_tensor(rows[k - 2], xn[:], gated, ALU.subtract)
                 return cand
-            for half in range(HALVES):
+            for half in range(HALVES if k else 0):
                 cols = slice(COLS * half, COLS * (half + 1))
                 nc.vector.scalar_tensor_tensor(gated[:, cols], stay[:, cols], 1.0, hn[half], ALU.subtract, ALU.mult)
             for half in range(HALVES):
                 cols = slice(COLS * half, COLS * (half + 1))
+                if k == 0:
+                    nc.vector.scalar_tensor_tensor(gated[:, cols], stay[:, cols], 1.0, hn[half],
+                                                   ALU.subtract, ALU.mult)
                 nc.vector.scalar_tensor_tensor(cand[:, cols], gated[:, cols], -1.0, xn[half], ALU.mult, ALU.add)
                 nc.scalar.activation(cand[:, cols], cand[:, cols], ACT.Tanh, bias=bn_sb[:, k : k + 1])
             return cand
@@ -277,9 +290,13 @@ def tile_list_tgn_mguP_kernel(
         def gather(k, cand):
             if k == 0:
                 rows = first_tile[:, J : 2 * J]
-            else:
-                tag = "second_tile" if k == 1 else handed_on(k - 2)
-                rows = keep.tile([P, J], F32, name="rows", tag=tag, align_bytes=64)[:]
+                for half in range(HALVES):
+                    cols = slice(COLS * half, COLS * (half + 1))
+                    entries = offsets[:, COLS // 16 * half : COLS // 16 * (half + 1)]
+                    nc.vector.tensor_tensor(rows[:, cols], state[0][:].indirect(entries), cand[:, cols], ALU.subtract)
+                return rows
+            tag = "second_tile" if k == 1 else handed_on(k - 2)
+            rows = keep.tile([P, J], F32, name="rows", tag=tag, align_bytes=64)[:]
             nc.vector.tensor_tensor(rows, state[k][:].indirect(offsets[:]), cand, ALU.subtract)
             return rows
 
@@ -290,9 +307,13 @@ def tile_list_tgn_mguP_kernel(
                     cols = slice(COLS * half, COLS * (half + 1))
                     nc.gpsimd.tensor_tensor(mid[:, cols], rows[:, cols], stay[:, cols], ALU.mult)
                 return mid
-            nc.gpsimd.tensor_tensor(mid[:], rows, stay, ALU.mult)
             if k == 0:
-                nc.gpsimd.tensor_tensor(mid[:], mid[:], cand, ALU.add)
+                for half in range(HALVES):
+                    cols = slice(COLS * half, COLS * (half + 1))
+                    nc.gpsimd.tensor_tensor(mid[:, cols], rows[:, cols], stay[:, cols], ALU.mult)
+                    nc.gpsimd.tensor_tensor(mid[:, cols], mid[:, cols], cand[:, cols], ALU.add)
+                return mid
+            nc.gpsimd.tensor_tensor(mid[:], rows, stay, ALU.mult)
             return mid
 
         def weigh(k, rows, mid):
@@ -418,6 +439,7 @@ def tile_list_tgn_mguP_kernel(
         for k in (1, 2):
             cands[k] = candidate(k, *gates[k])
             gates[k + 1] = gate(k + 1)
+        gates[FIRST_SHARED] = finish_gate(FIRST_SHARED, *gates[FIRST_SHARED])
         for i in range(1, TILES + 1):
             if i <= LAST:
                 rows[i] = gather(i, cands[i])
@@ -433,8 +455,12 @@ def tile_list_tgn_mguP_kernel(
             scatter(i - 1, blended[i - 1])
             if i + 3 <= LAST:
                 gates[i + 3] = gate(i + 3)
+                if i > 1:
+                    gates[i + 3] = finish_gate(i + 3, *gates[i + 3])
             if i <= LAST:
                 blended[i] = weigh(i, rows[i], mid)
+            if i == 1:
+                gates[i + 3] = finish_gate(i + 3, *gates[i + 3])
             hand_out(i - 1)
             if i == PACK:
                 for c in range(QUADS):

from contextlib import ExitStack

import concourse.mybir as mybir
from concourse.masks import make_identity

K, M, N, T, J = 1024, 1024, 1024, 2048, 1024
FLOPS = 2 * (2 * K + 2 * M) * N * J

F32 = mybir.dt.float32
BF16 = mybir.dt.bfloat16
I32 = mybir.dt.int32
U32 = mybir.dt.uint32
U16 = mybir.dt.uint16
U8 = mybir.dt.uint8
FP8X4 = mybir.dt.float8_e4m3fn_x4
FP4X4 = mybir.dt.float4_e2m1fn_x4
ALU = mybir.AluOpType
ACT = mybir.ActivationFunctionType

P = 128
PACK = 4
PASS = P * PACK
COLS = 512
QUADS = 4
QUAD = 32
PASSES = K // PASS
HALVES = J // COLS
TILES = N // P
LAST = TILES - 1
LINE = 16
BANK = 2048
PAGES = 3
SPLIT = 128
FIRST_SHARED = 3


def tile_list_tgn_mguP_kernel(
    tc, x, tab_words, tab_scales, wz_words, wz_scales, uz_words, uz_scales, wn_words, wn_scales,
    un_words, un_scales, bz, bn, hT, wgo, offs, out_0, out_1, out_2,
):
    nc = tc.nc
    with ExitStack() as ctx:
        keep = ctx.enter_context(tc.tile_pool(name="keep", bufs=1))
        ring = ctx.enter_context(tc.tile_pool(name="ring", bufs=2))
        psum = ctx.enter_context(tc.psum_pool(name="psum", bufs=2))

        def big(shape, dtype, name):
            return ring.tile(shape, dtype, name=name, tag="big", bufs=4, align_bytes=64)

        def bank(n, first=None, last=None):
            first, last = n if first is None else first, n if last is None else last
            tile = psum.tile([P, last - first + 1, COLS], F32, name="bank", tag="bank%d_%d" % (first, last), bufs=1,
                             offset=first * BANK)
            return tile[:, n - first, :]

        def woven_tile(name):
            return ring.tile([P, COLS, PACK], BF16, name=name, tag="woven", bufs=3, align_bytes=64)

        offsets = keep.tile([P, J // 16], U16, name="offsets")
        nc.sync.dma_start(offsets[:], offs)

        tab_sc = keep.tile([P, PASSES, T], U8, name="tab_sc", tag="tab_sc", align_bytes=64)
        planes = [keep.tile([P, PASSES, N], U8, name="planes%d" % n, align_bytes=64) for n in range(4)]
        for tile in [tab_sc] + planes:
            nc.vector.memset(tile[:].rearrange("p a t -> p (a t)").bitcast(I32), 0)
        bias_rows = keep.tile([P, P], F32, name="bias_rows")
        nc.gpsimd.memset(bias_rows[:], 0.0)
        identity = keep.tile([P, P], F32, name="identity")
        make_identity(nc, identity[:])
        warm = keep.tile([P, 1], F32, name="warm")
        nc.scalar.activation(warm[:], identity[:, 0:1], ACT.Sigmoid)

        def load_x(a, half):
            if half:
                raw = keep.tile([P, PACK, COLS], F32, name="x_raw", tag=("third_x", "last_x")[a], align_bytes=64)
            else:
                raw = big([P, PACK, COLS], F32, "x_raw")
            rows = x[PASS * a : PASS * (a + 1), COLS * half : COLS * (half + 1)]
            nc.sync.dma_start(raw[:], rows.rearrange("(p i) c -> p i c", i=PACK))
            return raw

        def load_planes(dst, scales, first):
            for r in range(QUADS):
                nc.sync.dma_start(dst[first + r : P : QUAD, :, :].bitcast(I32),
                                  scales[:, r : QUADS * QUADS : QUADS, :].rearrange("a q t -> q a t").bitcast(I32))

        words_of = {"uz": uz_words, "un": un_words, "wz": wz_words, "wn": wn_words}
        weights = {}

        def load_words(name, first, count):
            lo, hi = P * first, P * (first + count)
            tile = keep.tile([P, PASSES, hi - lo], I32, name="words", tag="%s%d" % (name, lo // P), align_bytes=64)
            columns = words_of[name].rearrange("a p n i -> p a (n i)")[:, :, PACK * lo : PACK * hi]
            nc.sync.dma_start(tile[:], columns.bitcast(I32))
            for k in range(lo // P, hi // P):
                weights[name, k] = tile[:, :, P * k - lo : P * (k + 1) - lo]

        def load_state(k):
            if k == 0:
                rows = keep.tile([P, T], F32, name="state0", tag="state0", align_bytes=64)
            else:
                rows = big([P, T], F32, "state")
            nc.sync.dma_start(rows[:], hT[P * k : P * (k + 1), :])
            return rows

        tab_w = big([P, T], I32, "tab_w")
        tab_rows = tab_words[0].rearrange("p t b -> p (t b)").bitcast(I32)
        for c in range(2):
            nc.sync.dma_start(tab_w[:, J * c : J * (c + 1)], tab_rows[:, J * c : J * (c + 1)])
        x_raw, state = {}, {}
        x_raw[0, 0] = load_x(0, 0)
        load_planes(tab_sc, tab_scales, 0)
        x_raw[1, 0] = load_x(1, 0)
        load_planes(planes[0], uz_scales, 0)
        x_raw[0, 1] = load_x(0, 1)
        nc.sync.dma_start(bias_rows[0:TILES, :], bz.rearrange("(k p) -> k p", p=P))
        nc.sync.dma_start(bias_rows[TILES : 2 * TILES, :], bn.rearrange("(k p) -> k p", p=P))
        nc.sync.dma_start(bias_rows[2 * TILES : 3 * TILES, :], wgo[0].rearrange("(b p) -> b p", p=P))
        load_words("uz", 0, 2)
        load_words("un", 0, 2)
        load_planes(planes[1], un_scales, 0)
        x_raw[1, 1] = load_x(1, 1)
        load_planes(planes[2], wz_scales, QUADS)
        load_words("wz", 0, 2)
        load_words("wn", 0, 2)
        load_planes(planes[3], wn_scales, QUADS)
        state[0] = load_state(0)
        load_words("uz", 2, 1)
        for name in ("un", "wz", "wn"):
            load_words(name, 2, 2)
        load_words("uz", 3, 2)
        state[1] = load_state(1)
        wgo_sb = keep.tile([P, J], F32, name="wgo_sb", tag="wgo", align_bytes=64)
        nc.sync.dma_start(wgo_sb[:], wgo)
        state[2] = load_state(2)
        load_words("un", 4, 2)
        load_words("wz", 4, 4)
        load_words("wn", 4, 4)
        load_words("uz", 5, 2)
        load_words("un", 6, 2)
        load_words("uz", 7, 1)
        for k in range(3, TILES):
            state[k] = load_state(k)

        turned_bias = bank(1)
        nc.tensor.transpose(turned_bias[:, 0:P], bias_rows[:], identity[:])
        bn_sb = keep.tile([P, TILES], F32, name="bias")
        bz_neg = keep.tile([P, TILES], F32, name="bz_neg")
        nc.scalar.copy(bn_sb[:], turned_bias[:, TILES : 2 * TILES])
        nc.scalar.activation(bz_neg[:], turned_bias[:, 0:TILES], ACT.Copy, scale=-1.0)
        bz_sb = keep.tile([P, TILES], F32, name="bz_sb")
        nc.scalar.copy(bz_sb[:], turned_bias[:, 0:TILES])
        wgo_turned = keep.tile([P, TILES], F32, name="wgo_turned")
        nc.scalar.copy(wgo_turned[:], turned_bias[:, 2 * TILES : 3 * TILES])

        v_codes, v_sc, x_codes, x_sc = {}, {}, {}, {}

        def pick_table(half):
            entries = offsets[:, COLS // 16 * half : COLS // 16 * (half + 1)]
            picked = keep.tile([P, COLS], U32, name="picked", tag="picked", align_bytes=64)
            v_codes[half] = keep.tile([P, PASSES, 2 * COLS], U8, name="v_codes%d" % half, align_bytes=64)
            v_sc[half] = keep.tile([P, PASSES, COLS], U8, name="v_sc%d" % half, align_bytes=64)
            nc.vector.tensor_copy(picked[:], tab_w[:].bitcast(U32).indirect(entries))
            for a in range(PASSES):
                nc.vector.tensor_copy(v_sc[half][:, a, :], tab_sc[:, a, :].indirect(entries))
            nc.vector.tensor_copy(v_codes[half][:].bitcast(U16).rearrange("p a (c i) -> p c a i", i=LINE // 2),
                                  picked[:].bitcast(U16).rearrange("p (c i a) -> p c a i", i=LINE // 2, a=PASSES))

        def quantise_x(half):
            x_codes[half] = keep.tile([P, PASSES, COLS], U32, name="x_codes%d" % half, align_bytes=64)
            x_sc[half] = keep.tile([P, PASSES, COLS], U8, name="x_sc%d" % half, align_bytes=64)
            for a in range(PASSES):
                last = a == PASSES - 1 and half == HALVES - 1
                width = COLS // 2 if last else COLS
                copy = nc.vector.tensor_copy if last else nc.scalar.copy
                for n in range(COLS // width):
                    cols = slice(width * n, width * (n + 1))
                    if last:
                        rounded = keep.tile([P, width, PACK], BF16, name="x_last", tag="page%d" % n, align_bytes=64)
                    else:
                        rounded = woven_tile("x_rounded")
                    copy(rounded[:].rearrange("p (c n) i -> p c i n", n=LINE // 4),
                         x_raw[a, half][:, :, cols].rearrange("p i (c n) -> p c i n", n=LINE // 4))
                    nc.vector.quantize_mx(out=x_codes[half][:, a, cols].bitcast(FP8X4), scales=x_sc[half][:, a, cols],
                                          in_=rounded[:].rearrange("p c i -> p (c i)"))

        for half in range(HALVES):
            pick_table(half)
            quantise_x(half)
        pages = [keep.tile([P, T], F32, name="page", tag="page%d" % n, align_bytes=64) for n in range(PAGES - 1)]
        for page in pages:
            nc.gpsimd.memset(page[:], 0.0)

        def passes(acc, name, k, half, opens, closes):
            n, cols = list(words_of).index(name), slice(P * k, P * (k + 1))
            for a in range(PASSES):
                if n < 2:
                    plane, moving_sc = planes[n][:, a, cols], v_sc[half]
                    moving = v_codes[half][:, a, :].bitcast(FP4X4)
                else:
                    plane, moving_sc = planes[n][QUADS:P, a, cols], x_sc[half]
                    moving = x_codes[half][:, a, :].bitcast(FP8X4)
                nc.tensor.matmul_mx(out=acc, lhsT=weights[name, k][:, a, :].bitcast(FP8X4), lhsT_scale=plane,
                                    rhs=moving, rhs_scale=moving_sc[:, a, :],
                                    start=opens and a == 0, stop=closes and a == PASSES - 1)

        spare = {}
        cands = {}
        first_tile = keep.tile([P, 2 * J], F32, name="first_tile", tag="third_x", align_bytes=64)

        def handed_on(k):
            return ("un%d", "uz%d")[k % 2] % (k + 2) if k else "wz2"

        def vector_columns(k):
            return COLS if k == FIRST_SHARED else SPLIT

        def gate(k):
            if k == 0:
                stay = first_tile[:, 0:J]
            else:
                stay = ring.tile([P, J], F32, name="stay", tag="stay", bufs=4, align_bytes=64)[:]
            shared, split = k >= FIRST_SHARED, vector_columns(k)
            if shared:
                late = psum.tile([P, 2, COLS], F32, name="late", tag="late%d" % (k % 2), bufs=1,
                                 offset=(6 - k % 2) * BANK)
                hn, xn = [bank(5 + 2 * (k % 2)), late[:, 0, :]], [bank(4), late[:, 1, :]]
                factors = ring.tile([P, 2, J - split], F32, name="factors", tag="factors", bufs=2, align_bytes=64)
                passes(hn[0], "un", k, 0, True, True)
                if split < COLS:
                    nc.scalar.activation(factors[:, 1, 0 : COLS - split], hn[0][:, split:COLS], ACT.Copy, scale=-1.0)
            else:
                hn = [bank(n) for n in ((5, 6), (7, 5), (6, 7))[k]]
                xn = [bank(n) for n in ((4, 3), (1, 4), (3, 1))[k]]
            for half in range(HALVES):
                sz = bank(2 * half)
                passes(sz, "uz", k, half, True, False)
                passes(sz, "wz", k, half, False, True)
                if not shared:
                    passes(hn[half], "un", k, half, True, True)
                if k == 0:
                    passes(xn[half], "wn", k, half, True, True)
                nc.scalar.activation(stay[:, COLS * half : COLS * (half + 1)], sz, ACT.Sigmoid,
                                     bias=bz_neg[:, k : k + 1], scale=-1.0)
                if shared and split < COLS * (half + 1):
                    first = max(split, COLS * half)
                    nc.scalar.activation(factors[:, 0, first - split : COLS * (half + 1) - split],
                                         sz[:, first - COLS * half : COLS], ACT.Sigmoid, bias=bz_sb[:, k : k + 1])
            if not shared:
                for half in range(HALVES if k else 0):
                    passes(xn[half], "wn", k, half, True, True)
                return stay, hn, xn
            return stay, hn, xn, factors

        def finish_gate(k, stay, hn, xn, factors):
            split = vector_columns(k)
            emptied = keep.tile([P, J], F32, name="xn_sb", tag="cand%d" % (3 * (k % 2)), align_bytes=64)
            passes(xn[0], "wn", k, 0, True, True)
            nc.scalar.copy(emptied[:, 0:COLS], xn[0])
            passes(hn[1], "un", k, 1, True, True)
            passes(xn[1], "wn", k, 1, True, True)
            nc.scalar.activation(factors[:, 1, COLS - split : J - split], hn[1], ACT.Copy, scale=-1.0)
            nc.scalar.copy(emptied[:, COLS:J], xn[1])
            return stay, [hn[0], factors], emptied

        def candidate(k, stay, hn, xn):
            width = 2 * J if FIRST_SHARED <= k + 1 <= LAST else J
            both = keep.tile([P, width], F32, name="cand", tag="cand%d" % (2 - k % 2 if k else 0), align_bytes=64)
            cand = both[:, 0:J]
            if width > J:
                spare[k + 1] = both[:, J:width]
            gated, split = spare[k], vector_columns(k)
            if k >= FIRST_SHARED:
                nc.vector.scalar_tensor_tensor(gated[:, 0:split], stay[:, 0:split], 1.0, hn[0][:, 0:split],
                                               ALU.subtract, ALU.mult)
                nc.gpsimd.tensor_tensor(gated[:, split:J], hn[1][:, 0, :], hn[1][:, 1, :], ALU.mult)
                nc.gpsimd.tensor_tensor(rows[k - 2], xn[:], gated, ALU.subtract)
                return cand
            for half in range(HALVES if k else 0):
                cols = slice(COLS * half, COLS * (half + 1))
                nc.vector.scalar_tensor_tensor(gated[:, cols], stay[:, cols], 1.0, hn[half], ALU.subtract, ALU.mult)
            for half in range(HALVES):
                cols = slice(COLS * half, COLS * (half + 1))
                if k == 0:
                    nc.vector.scalar_tensor_tensor(gated[:, cols], stay[:, cols], 1.0, hn[half],
                                                   ALU.subtract, ALU.mult)
                nc.vector.scalar_tensor_tensor(cand[:, cols], gated[:, cols], -1.0, xn[half], ALU.mult, ALU.add)
                nc.scalar.activation(cand[:, cols], cand[:, cols], ACT.Tanh, bias=bn_sb[:, k : k + 1])
            return cand

        def gather(k, cand):
            if k == 0:
                rows = first_tile[:, J : 2 * J]
                for half in range(HALVES):
                    cols = slice(COLS * half, COLS * (half + 1))
                    entries = offsets[:, COLS // 16 * half : COLS // 16 * (half + 1)]
                    nc.vector.tensor_tensor(rows[:, cols], state[0][:].indirect(entries), cand[:, cols], ALU.subtract)
                return rows
            tag = "second_tile" if k == 1 else handed_on(k - 2)
            rows = keep.tile([P, J], F32, name="rows", tag=tag, align_bytes=64)[:]
            nc.vector.tensor_tensor(rows, state[k][:].indirect(offsets[:]), cand, ALU.subtract)
            return rows

        def blend(k, rows, stay, cand):
            mid = ring.tile([P, J], F32, name="mid", tag="mid", bufs=1)
            if k >= LAST - 1:
                for half in (1, 0):
                    cols = slice(COLS * half, COLS * (half + 1))
                    nc.gpsimd.tensor_tensor(mid[:, cols], rows[:, cols], stay[:, cols], ALU.mult)
                return mid
            if k == 0:
                for half in range(HALVES):
                    cols = slice(COLS * half, COLS * (half + 1))
                    nc.gpsimd.tensor_tensor(mid[:, cols], rows[:, cols], stay[:, cols], ALU.mult)
                    nc.gpsimd.tensor_tensor(mid[:, cols], mid[:, cols], cand[:, cols], ALU.add)
                return mid
            nc.gpsimd.tensor_tensor(mid[:], rows, stay, ALU.mult)
            return mid

        def weigh(k, rows, mid):
            into = rows
            if k + 2 <= LAST:
                into = keep.tile([P, J], F32, name="weighed", tag=handed_on(k), align_bytes=64)[:]
            if k == 0:
                nc.vector.tensor_tensor(into, mid[:], wgo_sb[:], ALU.mult)
                return into
            halves = range(HALVES)
            weighed = cands[k]
            if k >= LAST - 1:
                halves = (1,)
                nc.gpsimd.tensor_tensor(mid[:, 0:COLS], mid[:, 0:COLS], cands[k][:, 0:COLS], ALU.add)
                nc.gpsimd.tensor_tensor(into[:, 0:COLS], mid[:, 0:COLS], wgo_sb[:, 0:COLS], ALU.mult)
            for half in halves:
                if k >= LAST - 1:
                    turned = bank(5 if k == LAST else 6)
                else:
                    turned = bank(3, 3, 4) if half else bank(1, 0, 2)
                for n, term in enumerate((cands[k], mid)):
                    for b in range(QUADS):
                        first = COLS * half + P * b
                        nc.tensor.matmul(turned[:, P * b : P * (b + 1)], lhsT=term[:, first : first + P],
                                         rhs=identity[:], is_transpose=True,
                                         start=n == 0 and b == 0, stop=n == 1 and b == QUADS - 1)
                for b in range(QUADS):
                    block = QUADS * half + b
                    nc.scalar.activation(weighed[:, P * block : P * (block + 1)], turned[:, P * b : P * (b + 1)],
                                         ACT.Copy, scale=wgo_turned[:, block : block + 1])
            for half in halves:
                if k == LAST - 1:
                    back = bank(5, 0, 5)
                elif k == LAST:
                    back = bank(4, 0, 7)
                elif half:
                    back = bank(3, 3, 6) if k == PACK + 1 else bank(3)
                else:
                    back = bank(1, 0, 2) if k == PACK + 1 else bank(1)
                for b in range(QUADS):
                    first = COLS * half + P * b
                    nc.tensor.transpose(back[:, P * b : P * (b + 1)], weighed[:, first : first + P], identity[:])
                nc.scalar.copy(into[:, COLS * half : COLS * (half + 1)], back)
            if k + 2 <= LAST:
                nc.scalar.activation(cands[k + 2], rows, ACT.Tanh, bias=bn_sb[:, k + 2 : k + 3])
            return into

        def scatter(k, rows):
            nc.vector.tensor_copy(pages[k % PAGES][:].indirect(offsets[:]), rows)

        again = {}
        woven = {}

        def read_back(c):
            if c == QUADS - 1:
                again[c] = big([P, PACK, COLS], F32, "again")
            else:
                again[c] = keep.tile([P, PACK, COLS], F32, name="again", align_bytes=64,
                                     tag=("state0", "third_x", "second_tile")[c])
            rows = out_0[0:PASS, COLS * c : COLS * (c + 1)]
            nc.sync.dma_start(again[c][:], rows.rearrange("(p i) c -> p i c", i=PACK))

        def round_back(c):
            woven[c] = keep.tile([P, COLS, PACK], BF16, name="y_rounded", align_bytes=64,
                                 tag=(handed_on(PACK - 1), "cand2", "cand1", "tab_sc")[c])
            nc.scalar.copy(woven[c][:].rearrange("p (c n) i -> p c i n", n=LINE // 4),
                           again[c][:].rearrange("p i (c n) -> p c i n", n=LINE // 4))

        def turn_twice(k, page):
            if k < LAST - 1:
                woven[k] = woven_tile("y_rounded")
            else:
                woven[k] = keep.tile([P, COLS, PACK], BF16, name="y_turned", tag=("wz4", "wn4")[k - LAST + 1],
                                     align_bytes=64)
            words = woven[k][:].rearrange("p c i -> p (c i)").bitcast(F32)
            rounded = keep.tile([P, QUADS, COLS], BF16, name="rounded", align_bytes=64,
                                tag="rounded" if k % 2 else "tab_sc")
            base = 0 if k < LAST - 1 else QUADS
            for c in range(QUADS):
                turned = bank(base + 2 * (c % 2) + c // 2)
                for q in range(QUADS):
                    first = COLS * q + P * c
                    nc.tensor.transpose(turned[:, P * q : P * (q + 1)], page[:, first : first + P], identity[:])
                nc.scalar.copy(rounded[:, c, :].rearrange("t (u m e) -> t u m e", u=2, e=2),
                               turned.rearrange("t (m u e) -> t u m e", u=2, e=2))
            for pair in range(2):
                back = bank(base + 2 * pair, base + 2 * pair, base + 2 * pair + 1)
                for c in range(2):
                    for u in range(2):
                        first = P * (2 * c + u)
                        pairs = rounded[:, 2 * pair + c, :].bitcast(F32)
                        nc.tensor.transpose(back[:, first : first + P], pairs[:, P * u : P * (u + 1)], identity[:])
                nc.scalar.copy(words[:, COLS * pair : COLS * (pair + 1)].rearrange("m (c t u) -> m c t u", c=2, u=2),
                               back.rearrange("m (c u t) -> m c t u", c=2, u=2))

        def quantise_y(codes, scales, n):
            nc.vector.quantize_mx(out=codes.bitcast(FP8X4), scales=scales, in_=woven[n][:].rearrange("p c i -> p (c i)"))

        def store_tiles(first, count):
            codes = big([P, count, COLS], U32, "y_codes")
            words = out_1[1].rearrange("(k p) t b -> p k (t b)", p=QUAD).bitcast(I32)
            for row in range(count):
                quantise_y(codes[:, row, :], late_sc[QUADS * (first + row) : P, :], PACK + first + row)
            for q in (0, 2, 1, 3):
                nc.sync.dma_start(words[:, first : first + count, COLS * q : COLS * (q + 1)],
                                  codes[QUAD * q : QUAD * (q + 1), :, :].bitcast(I32))

        def hand_out(k):
            page = pages[k % PAGES]
            nc.sync.dma_start(out_0[P * k : P * (k + 1), :], page[:])

        first_gated = keep.tile([P, J], F32, name="first_gated", tag="last_x", align_bytes=64)
        spare[0] = first_gated[:]
        gates, blended = {0: gate(0)}, {}
        cands[0] = candidate(0, *gates[0])
        pages.append(keep.tile([P, T], F32, name="page", tag="last_x", align_bytes=64))
        nc.gpsimd.memset(pages[PAGES - 1][:], 0.0)
        gates[1] = gate(1)
        rows = {0: gather(0, cands[0])}
        mid = blend(0, rows[0], gates[0][0], cands[0])
        early = keep.tile([P, 2 * J], F32, name="early", tag="state0", align_bytes=64)
        spare[1], spare[2] = early[:, 0:J], early[:, J : 2 * J]
        for k in (1, 2):
            cands[k] = candidate(k, *gates[k])
            gates[k + 1] = gate(k + 1)
        gates[FIRST_SHARED] = finish_gate(FIRST_SHARED, *gates[FIRST_SHARED])
        for i in range(1, TILES + 1):
            if i <= LAST:
                rows[i] = gather(i, cands[i])
            if i == 1:
                blended[0] = weigh(0, rows[0], mid)
            if i <= LAST:
                mid = blend(i, rows[i], gates[i][0], cands[i])
            if i + 2 <= LAST:
                cands[i + 2] = candidate(i + 2, *gates[i + 2])
            if i == TILES:
                late_sc = keep.tile([P, COLS], U8, name="late_sc", tag=handed_on(LAST - 3), align_bytes=64)
                store_tiles(0, 2)
            scatter(i - 1, blended[i - 1])
            if i + 3 <= LAST:
                gates[i + 3] = gate(i + 3)
                if i > 1:
                    gates[i + 3] = finish_gate(i + 3, *gates[i + 3])
            if i <= LAST:
                blended[i] = weigh(i, rows[i], mid)
            if i == 1:
                gates[i + 3] = finish_gate(i + 3, *gates[i + 3])
            hand_out(i - 1)
            if i == PACK:
                for c in range(QUADS):
                    read_back(c)
            if i > PACK:
                turn_twice(i - 1, pages[(i - 1) % PAGES])
            if PACK < i < LAST:
                round_back(i - PACK - 1)
            if i == LAST:
                round_back(2)
                round_back(3)

        store_tiles(2, 1)
        early_sc = keep.tile([P, COLS], U8, name="early_sc", tag=handed_on(LAST - 2), align_bytes=64)
        codes = big([P, T], U32, "y_codes")
        for c in range(QUADS):
            quantise_y(codes[:, COLS * c : COLS * (c + 1)], early_sc[QUADS * c : P, :], c)
        nc.sync.dma_start(out_1[0].rearrange("p t b -> p (t b)").bitcast(I32), codes[:].bitcast(I32))
        for q in (0, 2, 1, 3):
            rows_q = out_2[0, QUADS * q : QUADS * (q + 1), :].rearrange("r (c t) -> c r t", c=QUADS)
            nc.sync.dma_start(rows_q.bitcast(I32), early_sc[QUAD * q : QUAD * q + QUADS * QUADS, :].bitcast(I32))
        store_tiles(3, 1)
        for q in (0, 2, 1, 3):
            nc.sync.dma_start(out_2[1, :, COLS * q : COLS * (q + 1)].bitcast(I32),
                              late_sc[QUAD * q : QUAD * q + QUADS * PACK, :].bitcast(I32))
